import numpy as np
import ml_dtypes


def mxq(x, axis, fmt="e4m3"):
    dtype, down = {"e4m3": (ml_dtypes.float8_e4m3fn, 7), "e5m2": (ml_dtypes.float8_e5m2, 14)}[fmt]
    v = np.moveaxis(np.asarray(x, np.float32).astype(ml_dtypes.bfloat16).astype(np.float64), axis, -1)
    blocks = v.reshape(v.shape[:-1] + (-1, 32))
    amax = np.abs(blocks).max(-1, keepdims=True)
    byte = np.maximum(np.where(amax > 0, np.frexp(amax)[1] - 1 + 127, 0) - down, 1)
    scale = np.exp2(byte - 127.0)
    codes = (blocks / scale).astype(np.float32).astype(dtype).astype(np.float64)
    return np.moveaxis((codes * scale).reshape(v.shape), -1, axis)


WIDE = False


def mx_kscale(k):
    if not WIDE:
        return np.ones(k)
    levels = np.array([10, -10, 5, -5, 0])
    if k % 512:
        return np.exp2(np.random.permutation(np.resize(levels, k // 32))).repeat(32)
    a = np.empty((k // 512, 16))
    for p in range(k // 512):
        a[p, :8] = np.random.permutation(np.resize(levels, 8))
        for g in range(8):
            far = levels[np.abs(levels - a[p, g]) >= 10]
            a[p, g + 8] = far[np.random.randint(len(far))]
    return np.exp2(a.ravel()).repeat(32)


def f64(x):
    return np.asarray(x).astype(np.float64)


def striped(idx):
    return np.tile(idx.reshape(-1, 16).T, (8, 1)).astype(np.uint16)


def unstriped(offs):
    return offs[:16].T.reshape(-1).astype(np.int64)


E2M1 = np.array([0.0, 0.5, 1.0, 1.5, 2.0, 3.0, 4.0, 6.0, -0.0, -0.5, -1.0, -1.5, -2.0, -3.0, -4.0, -6.0])


def pack_weight(w, fmt):
    k, n = w.shape
    w = f64(np.asarray(w, np.float32).astype(ml_dtypes.bfloat16)).reshape(k // 32, 32, n)
    amax = np.abs(w).max(1)
    if fmt == "e4m3":
        byte = np.frexp(amax)[1] - 1 + 127 - 7
    else:
        mant, ex = np.frexp(amax / 6.0)
        byte = np.where(mant > 0.5, ex, ex - 1) + 127
    byte = np.clip(np.where(amax > 0, byte, 1), 1, 254)
    scaled = (w * np.exp2(127.0 - byte)[:, None, :]).reshape(k, n).astype(np.float32)
    by_word = np.ascontiguousarray(scaled.reshape(k // 512, 128, 4, n).transpose(0, 1, 3, 2))
    if fmt == "e4m3":
        words = by_word.astype(ml_dtypes.float8_e4m3fn).view(np.uint8)
    else:
        c = by_word.astype(ml_dtypes.float4_e2m1fn).view(np.uint8) & 0xF
        words = (c[..., 0::2] | (c[..., 1::2] << 4)).reshape(k // 512, 128, 2 * n)
    return np.ascontiguousarray(words), np.ascontiguousarray(byte.astype(np.uint8).reshape(k // 512, 16, n))


def unpack_weight(words, scales, fmt):
    g, _, n = scales.shape
    words = np.ascontiguousarray(words).reshape(g, 128, n, -1)
    if fmt == "e4m3":
        vals = words.view(ml_dtypes.float8_e4m3fn).astype(np.float64)
    else:
        nib = np.empty((g, 128, n, 4), np.uint8)
        nib[..., 0::2] = words & 0xF
        nib[..., 1::2] = words >> 4
        vals = E2M1[nib]
    vals = vals * np.repeat(np.exp2(scales.astype(np.float64) - 127.0), 8, axis=1)[..., None]
    return vals.transpose(0, 1, 3, 2).reshape(g * 512, n)


def planes(y):
    n, m = y.shape
    v = y.astype(np.float32).astype(ml_dtypes.bfloat16).astype(np.float64).reshape(n // 32, 32, m)
    top = np.abs(v).max(1)
    byte = np.clip(np.where(top > 0, np.frexp(top)[1] - 1 + 127 - 7, 1), 1, 254)
    codes = (v * np.exp2(127.0 - byte)[:, None, :]).reshape(n, m).astype(np.float32).astype(ml_dtypes.float8_e4m3fn).view(np.uint8)
    words = codes.reshape(n // 512, 128, 4, m).transpose(0, 1, 3, 2)
    return np.ascontiguousarray(words), np.ascontiguousarray(byte.astype(np.uint8).reshape(n // 512, 16, m))


def silu(v):
    return v / (1.0 + np.exp(-np.maximum(v, -700.0)))


K, T, E, C, H, HS, N = 1024, 512, 4, 128, 512, 512, 512


def by_expert(wq, xq):
    return np.concatenate([wq[e].T @ xq[:, e * C:(e + 1) * C] for e in range(E)], axis=1)


def setup_inputs():
    n = np.random.standard_normal
    s = mx_kscale(K)
    u = mx_kscale(H)
    v = mx_kscale(HS)
    slot_token = np.random.permutation(T)[:E * C]
    x = pack_weight(n((K, T)) * s[:, None], "e4m3")
    w1 = [pack_weight(m, "e2m1") for m in n((E, K, H)) / np.sqrt(K) / s[None, :, None] * u]
    w2 = [pack_weight(m, "e2m1") for m in n((E, H, N)) / np.sqrt(H) / u[None, :, None]]
    w1s = pack_weight(n((K, HS)) / np.sqrt(K) / s[:, None] * v, "e4m3")
    w2s = pack_weight(n((HS, N)) / np.sqrt(HS) / v[:, None], "e4m3")
    return {
        "x_words": x[0],
        "x_scales": x[1],
        "w1_words": np.stack([m[0] for m in w1]),
        "w1_scales": np.stack([m[1] for m in w1]),
        "w2_words": np.stack([m[0] for m in w2]),
        "w2_scales": np.stack([m[1] for m in w2]),
        "w1s_words": w1s[0],
        "w1s_scales": w1s[1],
        "w2s_words": w2s[0],
        "w2s_scales": w2s[1],
        "gate": np.tile(np.random.uniform(0.2, 1.0, E * C), (128, 1)).astype(np.float32),
        "offs": striped(slot_token),
    }


def reference(x_words, x_scales, w1_words, w1_scales, w2_words, w2_scales, w1s_words, w1s_scales, w2s_words, w2s_scales, gate, offs):
    w1 = np.stack([unpack_weight(w1_words[e], w1_scales[e], "e2m1") for e in range(E)])
    w2 = np.stack([unpack_weight(w2_words[e], w2_scales[e], "e2m1") for e in range(E)])
    w1s = unpack_weight(w1s_words, w1s_scales, "e4m3")
    w2s = unpack_weight(w2s_words, w2s_scales, "e4m3")
    idx = unstriped(offs)
    x = unpack_weight(x_words, x_scales, "e4m3")
    hs = silu(w1s.T @ x)
    ys = w2s.T @ mxq(hs, 0, "e4m3")
    h = silu(by_expert(w1, x[:, idx]))
    y = by_expert(w2, mxq(h, 0, "e4m3"))
    c = np.zeros((N, T))
    c[:, idx] = f64(gate[:1]) * y
    out_0 = ys + c
    return (out_0,) + planes(out_0)

@@ -1,0 +1,273 @@
+from contextlib import ExitStack
+
+import concourse.mybir as mybir
+from concourse.masks import make_identity
+
+K, T, E, C, H, N = 1024, 512, 4, 128, 512, 512
+FLOPS = 2 * T * (K * H + H * N) * 2
+
+F32 = mybir.dt.float32
+BF16 = mybir.dt.bfloat16
+I32 = mybir.dt.int32
+U32 = mybir.dt.uint32
+U16 = mybir.dt.uint16
+U8 = mybir.dt.uint8
+FP8X4 = mybir.dt.float8_e4m3fn_x4
+FP4X4 = mybir.dt.float4_e2m1fn_x4
+ACT = mybir.ActivationFunctionType
+ALU = mybir.AluOpType
+
+P = 128
+PACK = 4
+PASSES = K // (P * PACK)
+LIST_COLS = C // 16
+
+
+def tile_moe_shf_mlp_silu_kernel(
+    tc, x_words, x_scales, w1_words, w1_scales, w2_words, w2_scales,
+    w1s_words, w1s_scales, w2s_words, w2s_scales, gate, offs, out_0, out_1, out_2,
+):
+    nc = tc.nc
+    with ExitStack() as ctx:
+        sb = ctx.enter_context(tc.tile_pool(name="sb", bufs=1))
+        ps = ctx.enter_context(tc.psum_pool(name="ps", bufs=1))
+
+        def tile(name, cols, dtype, tag=None):
+            return sb.tile([P, cols], dtype, name=name, tag=tag or name, align_bytes=64)
+
+        def bank(index, name):
+            return ps.tile([P, 512], F32, name=name, tag="bank%d" % index)
+
+        def zero_plane(name, planes):
+            plane = tile(name, planes * 512, U8)
+            nc.vector.memset(plane[:].bitcast(I32), 0)
+            return plane
+
+        def load_plane(plane, rows):
+            planes = rows.shape[0]
+            for r in range(4):
+                nc.sync.dma_start(
+                    out=plane[r:P:32, :].bitcast(I32).rearrange("q (g w) -> q g w", g=planes),
+                    in_=rows[:, r:16:4, :].rearrange("g q c -> q g c").bitcast(I32),
+                )
+
+        x_plane = zero_plane("x_plane", PASSES)
+        w1_plane = [zero_plane("w1_plane%d" % i, 2 * PASSES) for i in range(2)]
+        w2_plane = zero_plane("w2_plane", E)
+        w1s_plane = zero_plane("w1s_plane", PASSES)
+        w2s_plane = zero_plane("w2s_plane", 1)
+
+        ident = tile("ident", P, F32)
+        make_identity(nc, ident[:])
+
+        offsets = sb.tile([P, T // 16], U16, name="offsets")
+        x_all = tile("x_all", PASSES * T, I32)
+        x_tok = [x_all[:, s * T:(s + 1) * T] for s in range(PASSES)]
+        w1 = [tile("w1_%d" % e, PASSES * 2 * H, U8) for e in range(E)]
+        w2 = [tile("w2_%d" % e, 2 * N, U8) for e in range(E)]
+        w1s = [tile("w1s_%d" % s, H, I32) for s in range(PASSES)]
+        w2s = tile("w2s", N, I32)
+        gate_col = tile("gate_col", E, F32)
+
+        def load_fp8(dst, words):
+            nc.sync.dma_start(out=dst[:], in_=words.rearrange("p c d -> p (c d)").bitcast(I32))
+
+        def load_w1(e):
+            nc.sync.dma_start(
+                out=w1[e][:].bitcast(I32).rearrange("p (s w) -> p s w", s=PASSES),
+                in_=w1_words[e].rearrange("s p b -> p s b").bitcast(I32),
+            )
+
+        def load_w2(e):
+            nc.sync.dma_start(out=w2[e][:].bitcast(I32), in_=w2_words[e, 0].bitcast(I32))
+
+        nc.sync.dma_start(offsets[:], offs)
+        nc.sync.dma_start(out=x_all[:].rearrange("p (s c) -> p s c", s=PASSES),
+                          in_=x_words.rearrange("s p c d -> p s (c d)").bitcast(I32))
+        load_plane(x_plane, x_scales)
+        load_w1(0)
+        load_plane(w1_plane[0], w1_scales[0:2].rearrange("e s b c -> (e s) b c"))
+        load_w1(1)
+        load_w2(0)
+        load_plane(w2_plane, w2_scales.rearrange("e s b c -> (e s) b c"))
+        with nc.allow_non_contiguous_dma(reason="one gate value a partition"):
+            nc.sync.dma_start(out=gate_col[:], in_=gate[0, :].rearrange("(e u) -> u e", e=E))
+        load_w1(2)
+        load_plane(w1_plane[1], w1_scales[2:4].rearrange("e s b c -> (e s) b c"))
+        load_w2(1)
+        load_w1(3)
+        load_w2(2)
+        load_w2(3)
+        for s in range(PASSES):
+            load_fp8(w1s[s], w1s_words[s])
+        load_plane(w1s_plane, w1s_scales)
+        load_fp8(w2s, w2s_words[0])
+        load_plane(w2s_plane, w2s_scales)
+
+        slot_words, slot_bytes = {}, {}
+
+        def gather(e, word_tag=None, byte_tag=None):
+            slot_words[e] = tile("slot_words%d" % e, PASSES * C, U32, word_tag)
+            slot_bytes[e] = tile("slot_bytes%d" % e, PASSES * C, U8, byte_tag)
+            entries = offsets[:, e * LIST_COLS:(e + 1) * LIST_COLS]
+            for s in range(PASSES):
+                nc.vector.tensor_copy(slot_words[e][:, s * C:(s + 1) * C], x_tok[s].bitcast(U32).indirect(entries))
+                nc.vector.tensor_copy(slot_bytes[e][:, s * C:(s + 1) * C], x_plane[:, s * T:(s + 1) * T].indirect(entries))
+
+        def first_layer(name, index, operands, grouped):
+            acc = bank(index % 2, name + "_acc")
+            for s in range(PASSES):
+                lhsT, lhsT_scale, rhs, rhs_scale = operands(s)
+                nc.tensor.matmul_mx(out=acc[:], lhsT=lhsT, lhsT_scale=lhsT_scale, rhs=rhs, rhs_scale=rhs_scale,
+                                    start=(s == 0), stop=(s == PASSES - 1))
+            hidden = tile(name + "_rows", H, BF16)
+            nc.scalar.activation(
+                out=hidden[:].rearrange("c (u p b) -> c u p b", u=2, b=2),
+                in_=acc[:].rearrange("c (p u b) -> c u p b", u=2, b=2),
+                func=ACT.Silu,
+            )
+            turned = bank(2 + index % 2, name + "_turned")
+            for u in range(2):
+                nc.tensor.transpose(turned[:, u * P:(u + 1) * P], hidden[:].bitcast(F32)[:, u * P:(u + 1) * P], ident[:])
+            nc.scalar.copy(
+                out=grouped.bitcast(F32).rearrange("p (c u) -> p c u", u=2),
+                in_=turned[:, 0:2 * P].rearrange("p (u c) -> p c u", u=2),
+            )
+
+        h_codes, h_plane, y = {}, {}, {}
+
+        def expert_first(e):
+            grouped = tile("h_grouped%d" % e, PACK * C, BF16)
+            first_layer(
+                "h%d" % e, e,
+                lambda s: (
+                    slot_words[e][:, s * C:(s + 1) * C].bitcast(FP8X4),
+                    slot_bytes[e][:, s * C:(s + 1) * C],
+                    w1[e][:, s * 2 * H:(s + 1) * 2 * H].bitcast(FP4X4),
+                    w1_plane[e // 2][:, (e % 2 * PASSES + s) * H:(e % 2 * PASSES + s + 1) * H],
+                ),
+                grouped[:],
+            )
+            h_codes[e] = tile("h_codes%d" % e, C, U32)
+            h_plane[e] = tile("h_plane%d" % e, C, U8)
+            nc.vector.quantize_mx(out=h_codes[e][:].bitcast(FP8X4), scales=h_plane[e][:], in_=grouped[:])
+
+        y_turned = {}
+
+        def expert_second(e):
+            acc = bank(4 + e % 2, "y_acc%d" % e)
+            nc.tensor.matmul_mx(out=acc[:], lhsT=h_codes[e][:].bitcast(FP8X4), lhsT_scale=h_plane[e][:],
+                                rhs=w2[e][:].bitcast(FP4X4), rhs_scale=w2_plane[:, e * N:(e + 1) * N],
+                                start=True, stop=True)
+            rows = tile("y_rows%d" % e, N, F32)
+            nc.scalar.activation(
+                out=rows[:].rearrange("c (t p) -> c t p", t=PACK),
+                in_=acc[:].rearrange("c (p t) -> c t p", t=PACK),
+                func=ACT.Copy, scale=gate_col[:, e:e + 1],
+            )
+            y_turned[e] = bank(6 + e % 2, "y_turned%d" % e)
+            for t in range(PACK):
+                nc.tensor.transpose(y_turned[e][:, t * C:(t + 1) * C], rows[:, t * P:(t + 1) * P], ident[:])
+
+        y_all = tile("y_all", PACK * T, F32)
+
+        def expert_out(e):
+            nc.scalar.copy(
+                out=y_all[:].rearrange("p (t j) -> p t j", t=PACK)[:, :, e * C:(e + 1) * C],
+                in_=y_turned[e][:].rearrange("p (t c) -> p t c", t=PACK),
+            )
+
+        routed = {}
+
+        def scatter(t, first, last):
+            nc.vector.tensor_copy(
+                routed[t][:].indirect(offsets[:, first * LIST_COLS:last * LIST_COLS]),
+                y_all[:, t * T + first * C:t * T + last * C],
+            )
+
+        for t in range(PACK - 1):
+            routed[t] = tile("routed%d" % t, T, F32)
+
+        gather(0)
+        gather(1)
+        gather(2)
+        expert_first(0)
+        expert_first(1)
+        gather(3, "h_grouped0", "h_grouped1")
+        expert_second(0)
+        expert_out(0)
+        expert_first(2)
+        expert_second(1)
+        for t in range(PACK - 1):
+            scatter(t, 0, 1)
+        expert_first(3)
+        expert_out(1)
+        for t in range(PACK - 1):
+            scatter(t, 1, 2)
+        for e in (2, 3):
+            expert_second(e)
+            expert_out(e)
+        for t in range(PACK - 1):
+            scatter(t, 2, 4)
+
+        hs_grouped = tile("hs_grouped", PACK * T, BF16)
+        for b in range(T // P):
+            first_layer(
+                "hs%d" % b, b,
+                lambda s: (
+                    x_tok[s][:, b * P:(b + 1) * P].bitcast(FP8X4),
+                    x_plane[:, s * T + b * P:s * T + (b + 1) * P],
+                    w1s[s][:].bitcast(FP8X4),
+                    w1s_plane[:, s * H:(s + 1) * H],
+                ),
+                hs_grouped[:, b * PACK * P:(b + 1) * PACK * P],
+            )
+        w2s_dealt = tile("w2s_dealt", N, I32)
+        w2s_plane_dealt = tile("w2s_plane_dealt", N, U8)
+        nc.vector.tensor_copy(w2s_dealt[:].rearrange("p (t m) -> p m t", t=PACK), w2s[:].rearrange("p (m t) -> p m t", t=PACK))
+        nc.vector.tensor_copy(w2s_plane_dealt[:].rearrange("p (t m) -> p m t", t=PACK), w2s_plane[:].rearrange("p (m t) -> p m t", t=PACK))
+        hs_codes = tile("hs_codes", T, U32)
+        hs_plane = tile("hs_plane", T, U8)
+        nc.vector.quantize_mx(out=hs_codes[:].bitcast(FP8X4), scales=hs_plane[:], in_=hs_grouped[:])
+
+        ys = []
+        for t in range(PACK):
+            acc = bank((0, 1, 4, 5)[t], "ys%d" % t)
+            nc.tensor.matmul_mx(out=acc[:], lhsT=w2s_dealt[:, t * P:(t + 1) * P].bitcast(FP8X4),
+                                lhsT_scale=w2s_plane_dealt[:, t * P:(t + 1) * P],
+                                rhs=hs_codes[:].bitcast(FP8X4), rhs_scale=hs_plane[:], start=True, stop=True)
+            ys.append(acc)
+
+        routed[PACK - 1] = tile("routed3", 704, F32, "hs_grouped")
+        total = tile("total", PACK * T, F32)
+        out_rows = out_0.rearrange("(p t) c -> p t c", t=PACK)
+
+        def add(t, first, last):
+            nc.vector.tensor_tensor(total[:, t * T + first:t * T + last], ys[t][:, first:last], routed[t][:, first:last], ALU.add)
+
+        def store(t):
+            nc.sync.dma_start(out=out_rows[:, t, :], in_=total[:, t * T:(t + 1) * T])
+
+        scatter(3, 0, 4)
+        for t in range(PACK - 1):
+            add(t, 0, T)
+            store(t)
+        half = T // 2
+        add(3, half, T)
+        add(3, 0, half)
+        store(3)
+
+        grouped = [tile("out_grouped%d" % i, PACK * half, BF16) for i in range(2)]
+        by_token = total[:].rearrange("p (t c) -> p c t", t=PACK)
+        nc.scalar.copy(out=grouped[1][:].rearrange("p (c t) -> p c t", t=PACK), in_=by_token[:, half:T, :])
+        nc.vector.tensor_copy(grouped[0][:].rearrange("p (c t) -> p c t", t=PACK), by_token[:, 0:half, :])
+        out_codes = tile("out_codes", T, U32)
+        out_plane = tile("out_plane", T, U8)
+        words_out = out_1[0].rearrange("p c d -> p (c d)").bitcast(I32)
+        for i in range(2):
+            cols = slice(i * half, (i + 1) * half)
+            nc.vector.quantize_mx(out=out_codes[:, cols].bitcast(FP8X4), scales=out_plane[:, cols], in_=grouped[i][:])
+            nc.sync.dma_start(out=words_out[:, cols], in_=out_codes[:, cols].bitcast(I32))
+        for r in range(4):
+            queue = nc.sync if r % 2 else nc.scalar
+            queue.dma_start(out=out_2[0, r:16:4, :].bitcast(I32), in_=out_plane[r:P:32, :].bitcast(I32))

@@ -38,9 +38,11 @@ def tile_moe_shf_mlp_silu_kernel(
         def bank(index, name):
             return ps.tile([P, 512], F32, name=name, tag="bank%d" % index)
 
-        def zero_plane(name, planes):
+        def zero_plane(name, planes, engines):
             plane = tile(name, planes * 512, U8)
-            nc.vector.memset(plane[:].bitcast(I32), 0)
+            share = planes * 512 // len(engines)
+            for i, engine in enumerate(engines):
+                engine.memset(plane[:, i * share:(i + 1) * share].bitcast(I32), 0)
             return plane
 
         def load_plane(plane, rows):
@@ -51,70 +53,73 @@ def tile_moe_shf_mlp_silu_kernel(
                     in_=rows[:, r:16:4, :].rearrange("g q c -> q g c").bitcast(I32),
                 )
 
-        x_plane = zero_plane("x_plane", PASSES)
-        w1_plane = [zero_plane("w1_plane%d" % i, 2 * PASSES) for i in range(2)]
-        w2_plane = zero_plane("w2_plane", E)
-        w1s_plane = zero_plane("w1s_plane", PASSES)
-        w2s_plane = zero_plane("w2s_plane", 1)
+        x_plane = zero_plane("x_plane", PASSES, (nc.vector,))
+        w1_plane = zero_plane("w1_plane", E * PASSES, (nc.vector, nc.gpsimd))
+        w2_plane = zero_plane("w2_plane", E, (nc.vector,))
+        w2s_plane = zero_plane("w2s_plane", 1, (nc.vector,))
+        w1s_plane = zero_plane("w1s_plane", PASSES, (nc.vector,))
 
         ident = tile("ident", P, F32)
         make_identity(nc, ident[:])
 
         offsets = sb.tile([P, T // 16], U16, name="offsets")
-        x_all = tile("x_all", PASSES * T, I32)
-        x_tok = [x_all[:, s * T:(s + 1) * T] for s in range(PASSES)]
-        w1 = [tile("w1_%d" % e, PASSES * 2 * H, U8) for e in range(E)]
-        w2 = [tile("w2_%d" % e, 2 * N, U8) for e in range(E)]
-        w1s = [tile("w1s_%d" % s, H, I32) for s in range(PASSES)]
+        x_tok = [tile("x_tok%d" % s, T, I32) for s in range(PASSES)]
+        w1_first = [tile("w1_%d" % e, PASSES * 2 * H, U8) for e in range(2)]
+        w1_last = tile("w1_last", 2 * PASSES * 2 * H, U8)
+        w1 = [w1_first[0][:], w1_first[1][:], w1_last[:, 0:PASSES * 2 * H], w1_last[:, PASSES * 2 * H:]]
+        w2_pairs = [tile("w2_%d" % i, 2 * 2 * N, U8) for i in range(2)]
+        w2 = [w2_pairs[e // 2][:, e % 2 * 2 * N:(e % 2 + 1) * 2 * N] for e in range(E)]
+        w1s_all = tile("w1s", PASSES * H, I32)
+        w1s = [w1s_all[:, s * H:(s + 1) * H] for s in range(PASSES)]
         w2s = tile("w2s", N, I32)
         gate_col = tile("gate_col", E, F32)
 
         def load_fp8(dst, words):
             nc.sync.dma_start(out=dst[:], in_=words.rearrange("p c d -> p (c d)").bitcast(I32))
 
-        def load_w1(e):
+        def load_fp4(dst, words):
             nc.sync.dma_start(
-                out=w1[e][:].bitcast(I32).rearrange("p (s w) -> p s w", s=PASSES),
-                in_=w1_words[e].rearrange("s p b -> p s b").bitcast(I32),
+                out=dst[:].bitcast(I32).rearrange("p (g w) -> p g w", g=words.shape[0]),
+                in_=words.rearrange("g p b -> p g b").bitcast(I32),
             )
 
-        def load_w2(e):
-            nc.sync.dma_start(out=w2[e][:].bitcast(I32), in_=w2_words[e, 0].bitcast(I32))
-
         nc.sync.dma_start(offsets[:], offs)
-        nc.sync.dma_start(out=x_all[:].rearrange("p (s c) -> p s c", s=PASSES),
-                          in_=x_words.rearrange("s p c d -> p s (c d)").bitcast(I32))
+        load_fp8(x_tok[0], x_words[0])
+        load_fp8(x_tok[1], x_words[1])
         load_plane(x_plane, x_scales)
-        load_w1(0)
-        load_plane(w1_plane[0], w1_scales[0:2].rearrange("e s b c -> (e s) b c"))
-        load_w1(1)
-        load_w2(0)
-        load_plane(w2_plane, w2_scales.rearrange("e s b c -> (e s) b c"))
+        load_fp4(w1_first[0], w1_words[0])
+        load_plane(w1_plane, w1_scales.rearrange("e s b c -> (e s) b c"))
+        load_fp4(w1_first[1], w1_words[1])
+        load_fp4(w1_last, w1_words[2:4].rearrange("e s p b -> (e s) p b"))
+        load_fp4(w2_pairs[0], w2_words[0:2, 0])
         with nc.allow_non_contiguous_dma(reason="one gate value a partition"):
             nc.sync.dma_start(out=gate_col[:], in_=gate[0, :].rearrange("(e u) -> u e", e=E))
-        load_w1(2)
-        load_plane(w1_plane[1], w1_scales[2:4].rearrange("e s b c -> (e s) b c"))
-        load_w2(1)
-        load_w1(3)
-        load_w2(2)
-        load_w2(3)
-        for s in range(PASSES):
-            load_fp8(w1s[s], w1s_words[s])
-        load_plane(w1s_plane, w1s_scales)
+        load_plane(w2_plane, w2_scales.rearrange("e s b c -> (e s) b c"))
         load_fp8(w2s, w2s_words[0])
+        nc.sync.dma_start(out=w1s_all[:].rearrange("p (s c) -> p s c", s=PASSES),
+                          in_=w1s_words.rearrange("s p c d -> p s (c d)").bitcast(I32))
         load_plane(w2s_plane, w2s_scales)
+        load_plane(w1s_plane, w1s_scales)
+        load_fp4(w2_pairs[1], w2_words[2:4, 0])
 
         slot_words, slot_bytes = {}, {}
 
-        def gather(e, word_tag=None, byte_tag=None):
-            slot_words[e] = tile("slot_words%d" % e, PASSES * C, U32, word_tag)
-            slot_bytes[e] = tile("slot_bytes%d" % e, PASSES * C, U8, byte_tag)
-            entries = offsets[:, e * LIST_COLS:(e + 1) * LIST_COLS]
+        def gather(name, dtype, windows, into, first, last, tag=None):
+            width = (last - first) * C
+            gathered = tile("%s%d" % (name, first), PASSES * width, dtype, tag)
+            entries = offsets[:, first * LIST_COLS:last * LIST_COLS]
             for s in range(PASSES):
-                nc.vector.tensor_copy(slot_words[e][:, s * C:(s + 1) * C], x_tok[s].bitcast(U32).indirect(entries))
-                nc.vector.tensor_copy(slot_bytes[e][:, s * C:(s + 1) * C], x_plane[:, s * T:(s + 1) * T].indirect(entries))
+                nc.vector.tensor_copy(gathered[:, s * width:(s + 1) * width], windows[s].indirect(entries))
+                for e in range(first, last):
+                    into[e, s] = gathered[:, s * width + (e - first) * C:s * width + (e - first + 1) * C]
 
-        def first_layer(name, index, operands, grouped):
+        def gather_words(first, last, tag=None):
+            gather("slot_words", U32, [x_tok[s][:].bitcast(U32) for s in range(PASSES)], slot_words, first, last, tag)
+
+        def gather_bytes(first, last):
+            gather("slot_bytes", U8, [x_plane[:, s * T:(s + 1) * T] for s in range(PASSES)], slot_bytes, first, last)
+
+        def first_layer(name, index, operands, grouped, copy=nc.scalar.copy):
             acc = bank(index % 2, name + "_acc")
             for s in range(PASSES):
                 lhsT, lhsT_scale, rhs, rhs_scale = operands(s)
@@ -129,7 +134,7 @@ def tile_moe_shf_mlp_silu_kernel(
             turned = bank(2 + index % 2, name + "_turned")
             for u in range(2):
                 nc.tensor.transpose(turned[:, u * P:(u + 1) * P], hidden[:].bitcast(F32)[:, u * P:(u + 1) * P], ident[:])
-            nc.scalar.copy(
+            copy(
                 out=grouped.bitcast(F32).rearrange("p (c u) -> p c u", u=2),
                 in_=turned[:, 0:2 * P].rearrange("p (u c) -> p c u", u=2),
             )
@@ -141,41 +146,40 @@ def tile_moe_shf_mlp_silu_kernel(
             first_layer(
                 "h%d" % e, e,
                 lambda s: (
-                    slot_words[e][:, s * C:(s + 1) * C].bitcast(FP8X4),
-                    slot_bytes[e][:, s * C:(s + 1) * C],
+                    slot_words[e, s].bitcast(FP8X4),
+                    slot_bytes[e, s],
                     w1[e][:, s * 2 * H:(s + 1) * 2 * H].bitcast(FP4X4),
-                    w1_plane[e // 2][:, (e % 2 * PASSES + s) * H:(e % 2 * PASSES + s + 1) * H],
+                    w1_plane[:, (e * PASSES + s) * H:(e * PASSES + s + 1) * H],
                 ),
                 grouped[:],
+                nc.vector.tensor_copy if e == 0 else nc.scalar.copy,
             )
             h_codes[e] = tile("h_codes%d" % e, C, U32)
             h_plane[e] = tile("h_plane%d" % e, C, U8)
             nc.vector.quantize_mx(out=h_codes[e][:].bitcast(FP8X4), scales=h_plane[e][:], in_=grouped[:])
 
-        y_turned = {}
-
-        def expert_second(e):
-            acc = bank(4 + e % 2, "y_acc%d" % e)
-            nc.tensor.matmul_mx(out=acc[:], lhsT=h_codes[e][:].bitcast(FP8X4), lhsT_scale=h_plane[e][:],
-                                rhs=w2[e][:].bitcast(FP4X4), rhs_scale=w2_plane[:, e * N:(e + 1) * N],
-                                start=True, stop=True)
-            rows = tile("y_rows%d" % e, N, F32)
-            nc.scalar.activation(
-                out=rows[:].rearrange("c (t p) -> c t p", t=PACK),
-                in_=acc[:].rearrange("c (p t) -> c t p", t=PACK),
-                func=ACT.Copy, scale=gate_col[:, e:e + 1],
-            )
-            y_turned[e] = bank(6 + e % 2, "y_turned%d" % e)
-            for t in range(PACK):
-                nc.tensor.transpose(y_turned[e][:, t * C:(t + 1) * C], rows[:, t * P:(t + 1) * P], ident[:])
-
         y_all = tile("y_all", PACK * T, F32)
 
-        def expert_out(e):
-            nc.scalar.copy(
-                out=y_all[:].rearrange("p (t j) -> p t j", t=PACK)[:, :, e * C:(e + 1) * C],
-                in_=y_turned[e][:].rearrange("p (t c) -> p t c", t=PACK),
-            )
+        def expert_second(e, acc_bank, parts):
+            acc = bank(acc_bank, "y_acc%d" % e)
+            nc.tensor.matmul_mx(out=acc[:], lhsT=h_codes[e][:].bitcast(FP8X4), lhsT_scale=h_plane[e][:],
+                                rhs=w2[e].bitcast(FP4X4), rhs_scale=w2_plane[:, e * N:(e + 1) * N],
+                                start=True, stop=True)
+            rows = tile("y_rows%d" % e, N, F32)
+            for first, last, turn_bank, copy in parts:
+                nc.scalar.activation(
+                    out=rows[:].rearrange("c (t p) -> c t p", t=PACK)[:, first:last, :],
+                    in_=acc[:].rearrange("c (p t) -> c t p", t=PACK)[:, first:last, :],
+                    func=ACT.Copy, scale=gate_col[:, e:e + 1],
+                )
+            for first, last, turn_bank, copy in parts:
+                turned = bank(turn_bank, "y_turned%d_%d" % (e, first))
+                for t in range(first, last):
+                    nc.tensor.transpose(turned[:, t * C:(t + 1) * C], rows[:, t * P:(t + 1) * P], ident[:])
+                copy(
+                    out=y_all[:].rearrange("p (t j) -> p t j", t=PACK)[:, first:last, e * C:(e + 1) * C],
+                    in_=turned[:].rearrange("p (t c) -> p t c", t=PACK)[:, first:last, :],
+                )
 
         routed = {}
 
@@ -185,30 +189,32 @@ def tile_moe_shf_mlp_silu_kernel(
                 y_all[:, t * T + first * C:t * T + last * C],
             )
 
-        for t in range(PACK - 1):
+        for t in range(PACK):
             routed[t] = tile("routed%d" % t, T, F32)
 
-        gather(0)
-        gather(1)
-        gather(2)
+        gather_words(0, 1)
+        gather_bytes(0, 1)
+        gather_words(1, 3)
+        gather_bytes(1, 2)
+        gather_bytes(2, 4)
         expert_first(0)
+        gather_words(3, 4, "slot_words0")
         expert_first(1)
-        gather(3, "h_grouped0", "h_grouped1")
-        expert_second(0)
-        expert_out(0)
+        expert_second(0, 4, ((0, 2, 6, nc.vector.tensor_copy), (2, 4, 7, nc.scalar.copy)))
         expert_first(2)
-        expert_second(1)
-        for t in range(PACK - 1):
+        w2s_dealt = tile("w2s_dealt", N, I32, "h_grouped1")
+        w2s_plane_dealt = tile("w2s_plane_dealt", N, U8, "h_grouped0")
+        nc.vector.tensor_copy(w2s_dealt[:].rearrange("p (t m) -> p m t", t=PACK), w2s[:].rearrange("p (m t) -> p m t", t=PACK))
+        nc.vector.tensor_copy(w2s_plane_dealt[:].rearrange("p (t m) -> p m t", t=PACK), w2s_plane[:].rearrange("p (m t) -> p m t", t=PACK))
+        for t in range(PACK):
             scatter(t, 0, 1)
         expert_first(3)
-        expert_out(1)
+        expert_second(1, 5, ((0, 4, 6, nc.scalar.copy),))
         for t in range(PACK - 1):
             scatter(t, 1, 2)
-        for e in (2, 3):
-            expert_second(e)
-            expert_out(e)
+        expert_second(2, 4, ((0, 4, 7, nc.scalar.copy),))
         for t in range(PACK - 1):
-            scatter(t, 2, 4)
+            scatter(t, 2, 3)
 
         hs_grouped = tile("hs_grouped", PACK * T, BF16)
         for b in range(T // P):
@@ -217,28 +223,27 @@ def tile_moe_shf_mlp_silu_kernel(
                 lambda s: (
                     x_tok[s][:, b * P:(b + 1) * P].bitcast(FP8X4),
                     x_plane[:, s * T + b * P:s * T + (b + 1) * P],
-                    w1s[s][:].bitcast(FP8X4),
+                    w1s[s].bitcast(FP8X4),
                     w1s_plane[:, s * H:(s + 1) * H],
                 ),
                 hs_grouped[:, b * PACK * P:(b + 1) * PACK * P],
             )
-        w2s_dealt = tile("w2s_dealt", N, I32)
-        w2s_plane_dealt = tile("w2s_plane_dealt", N, U8)
-        nc.vector.tensor_copy(w2s_dealt[:].rearrange("p (t m) -> p m t", t=PACK), w2s[:].rearrange("p (m t) -> p m t", t=PACK))
-        nc.vector.tensor_copy(w2s_plane_dealt[:].rearrange("p (t m) -> p m t", t=PACK), w2s_plane[:].rearrange("p (m t) -> p m t", t=PACK))
         hs_codes = tile("hs_codes", T, U32)
         hs_plane = tile("hs_plane", T, U8)
         nc.vector.quantize_mx(out=hs_codes[:].bitcast(FP8X4), scales=hs_plane[:], in_=hs_grouped[:])
 
+        expert_second(3, 0, ((0, 4, 3, nc.scalar.copy),))
+        for t in range(PACK - 1):
+            scatter(t, 3, 4)
+
         ys = []
         for t in range(PACK):
-            acc = bank((0, 1, 4, 5)[t], "ys%d" % t)
+            acc = bank(4 + t, "ys%d" % t)
             nc.tensor.matmul_mx(out=acc[:], lhsT=w2s_dealt[:, t * P:(t + 1) * P].bitcast(FP8X4),
                                 lhsT_scale=w2s_plane_dealt[:, t * P:(t + 1) * P],
                                 rhs=hs_codes[:].bitcast(FP8X4), rhs_scale=hs_plane[:], start=True, stop=True)
             ys.append(acc)
 
-        routed[PACK - 1] = tile("routed3", 704, F32, "hs_grouped")
         total = tile("total", PACK * T, F32)
         out_rows = out_0.rearrange("(p t) c -> p t c", t=PACK)
 
@@ -248,9 +253,11 @@ def tile_moe_shf_mlp_silu_kernel(
         def store(t):
             nc.sync.dma_start(out=out_rows[:, t, :], in_=total[:, t * T:(t + 1) * T])
 
-        scatter(3, 0, 4)
+        scatter(3, 1, 4)
         for t in range(PACK - 1):
-            add(t, 0, T)
+            shared = tile("shared%d" % t, T, F32)
+            nc.scalar.copy(out=shared[:], in_=ys[t][:])
+            nc.gpsimd.tensor_tensor(total[:, t * T:(t + 1) * T], shared[:], routed[t][:], ALU.add)
             store(t)
         half = T // 2
         add(3, half, T)

@@ -21,6 +21,9 @@ P = 128
 PACK = 4
 PASSES = K // (P * PACK)
 LIST_COLS = C // 16
+PLANE = 512
+FP4_ROW = 2 * PLANE
+LAST = PACK - 1
 
 
 def tile_moe_shf_mlp_silu_kernel(
@@ -36,43 +39,22 @@ def tile_moe_shf_mlp_silu_kernel(
             return sb.tile([P, cols], dtype, name=name, tag=tag or name, align_bytes=64)
 
         def bank(index, name):
-            return ps.tile([P, 512], F32, name=name, tag="bank%d" % index)
+            return ps.tile([P, PLANE], F32, name=name, tag="bank%d" % index)
 
-        def zero_plane(name, planes, engines):
-            plane = tile(name, planes * 512, U8)
-            share = planes * 512 // len(engines)
+
+        def zero_planes(name, planes, engines):
+            zeroed = tile(name, planes * PLANE, U8)
+            share = planes * PLANE // len(engines)
             for i, engine in enumerate(engines):
-                engine.memset(plane[:, i * share:(i + 1) * share].bitcast(I32), 0)
-            return plane
+                engine.memset(zeroed[:, i * share:(i + 1) * share].bitcast(I32), 0)
+            return zeroed
 
-        def load_plane(plane, rows):
-            planes = rows.shape[0]
+        def load_planes(dst, rows):
             for r in range(4):
                 nc.sync.dma_start(
-                    out=plane[r:P:32, :].bitcast(I32).rearrange("q (g w) -> q g w", g=planes),
+                    out=dst[r:P:32, :].bitcast(I32).rearrange("q (g w) -> q g w", g=rows.shape[0]),
                     in_=rows[:, r:16:4, :].rearrange("g q c -> q g c").bitcast(I32),
                 )
-
-        x_plane = zero_plane("x_plane", PASSES, (nc.vector,))
-        w1_plane = zero_plane("w1_plane", E * PASSES, (nc.vector, nc.gpsimd))
-        w2_plane = zero_plane("w2_plane", E, (nc.vector,))
-        w2s_plane = zero_plane("w2s_plane", 1, (nc.vector,))
-        w1s_plane = zero_plane("w1s_plane", PASSES, (nc.vector,))
-
-        ident = tile("ident", P, F32)
-        make_identity(nc, ident[:])
-
-        offsets = sb.tile([P, T // 16], U16, name="offsets")
-        x_tok = [tile("x_tok%d" % s, T, I32) for s in range(PASSES)]
-        w1_first = [tile("w1_%d" % e, PASSES * 2 * H, U8) for e in range(2)]
-        w1_last = tile("w1_last", 2 * PASSES * 2 * H, U8)
-        w1 = [w1_first[0][:], w1_first[1][:], w1_last[:, 0:PASSES * 2 * H], w1_last[:, PASSES * 2 * H:]]
-        w2_pairs = [tile("w2_%d" % i, 2 * 2 * N, U8) for i in range(2)]
-        w2 = [w2_pairs[e // 2][:, e % 2 * 2 * N:(e % 2 + 1) * 2 * N] for e in range(E)]
-        w1s_all = tile("w1s", PASSES * H, I32)
-        w1s = [w1s_all[:, s * H:(s + 1) * H] for s in range(PASSES)]
-        w2s = tile("w2s", N, I32)
-        gate_col = tile("gate_col", E, F32)
 
         def load_fp8(dst, words):
             nc.sync.dma_start(out=dst[:], in_=words.rearrange("p c d -> p (c d)").bitcast(I32))
@@ -83,28 +65,51 @@ def tile_moe_shf_mlp_silu_kernel(
                 in_=words.rearrange("g p b -> p g b").bitcast(I32),
             )
 
+        x_plane = zero_planes("x_plane", PASSES, (nc.vector,))
+        w1_plane = zero_planes("w1_plane", E * PASSES, (nc.vector, nc.gpsimd))
+        w2_plane = zero_planes("w2_plane", E, (nc.vector,))
+        w1s_plane = zero_planes("w1s_plane", PASSES, (nc.vector,))
+        w2s_plane = zero_planes("w2s_plane", 1, (nc.vector,))
+
+        ident = tile("ident", P, F32)
+        make_identity(nc, ident[:])
+
+        offsets = sb.tile([P, T // 16], U16, name="offsets")
+        x_tok = [tile("x_tok%d" % s, T, I32) for s in range(PASSES)]
+        w1_first = [tile("w1_%d" % e, PASSES * FP4_ROW, U8) for e in range(2)]
+        w1_last = tile("w1_last", 2 * PASSES * FP4_ROW, U8)
+        w1 = [w1_first[0][:], w1_first[1][:], w1_last[:, 0:PASSES * FP4_ROW], w1_last[:, PASSES * FP4_ROW:]]
+        w2_pairs = [tile("w2_%d" % i, 2 * FP4_ROW, U8) for i in range(2)]
+        w2 = [w2_pairs[e // 2][:, e % 2 * FP4_ROW:(e % 2 + 1) * FP4_ROW] for e in range(E)]
+        w1s = tile("w1s", PASSES * H, I32)
+        w2s = tile("w2s", N, I32)
+        gate_col = tile("gate_col", E - 1, F32)
+        gate_rows = tile("gate_rows", C, F32)
+
         nc.sync.dma_start(offsets[:], offs)
         load_fp8(x_tok[0], x_words[0])
         load_fp8(x_tok[1], x_words[1])
-        load_plane(x_plane, x_scales)
+        load_planes(x_plane, x_scales)
         load_fp4(w1_first[0], w1_words[0])
-        load_plane(w1_plane, w1_scales.rearrange("e s b c -> (e s) b c"))
+        load_planes(w1_plane, w1_scales.rearrange("e s b c -> (e s) b c"))
         load_fp4(w1_first[1], w1_words[1])
-        load_fp4(w1_last, w1_words[2:4].rearrange("e s p b -> (e s) p b"))
         load_fp4(w2_pairs[0], w2_words[0:2, 0])
-        with nc.allow_non_contiguous_dma(reason="one gate value a partition"):
-            nc.sync.dma_start(out=gate_col[:], in_=gate[0, :].rearrange("(e u) -> u e", e=E))
-        load_plane(w2_plane, w2_scales.rearrange("e s b c -> (e s) b c"))
-        load_fp8(w2s, w2s_words[0])
-        nc.sync.dma_start(out=w1s_all[:].rearrange("p (s c) -> p s c", s=PASSES),
+        load_planes(w2_plane, w2_scales.rearrange("e s b c -> (e s) b c"))
+        load_fp4(w1_last, w1_words[2:4].rearrange("e s p b -> (e s) p b"))
+        nc.sync.dma_start(out=gate_rows[:], in_=gate[:, 0:C])
+        with nc.allow_non_contiguous_dma(reason="one gate value a partition; all rows of gate are equal"):
+            nc.sync.dma_start(out=gate_col[:], in_=gate[0, C:].rearrange("(e u) -> u e", e=E - 1))
+        nc.sync.dma_start(out=w1s[:].rearrange("p (s c) -> p s c", s=PASSES),
                           in_=w1s_words.rearrange("s p c d -> p s (c d)").bitcast(I32))
-        load_plane(w2s_plane, w2s_scales)
-        load_plane(w1s_plane, w1s_scales)
+        load_planes(w1s_plane, w1s_scales)
         load_fp4(w2_pairs[1], w2_words[2:4, 0])
+        load_fp8(w2s, w2s_words[0])
+        load_planes(w2s_plane, w2s_scales)
+
 
         slot_words, slot_bytes = {}, {}
 
-        def gather(name, dtype, windows, into, first, last, tag=None):
+        def gather(name, dtype, windows, into, first, last, tag):
             width = (last - first) * C
             gathered = tile("%s%d" % (name, first), PASSES * width, dtype, tag)
             entries = offsets[:, first * LIST_COLS:last * LIST_COLS]
@@ -117,123 +122,138 @@ def tile_moe_shf_mlp_silu_kernel(
             gather("slot_words", U32, [x_tok[s][:].bitcast(U32) for s in range(PASSES)], slot_words, first, last, tag)
 
         def gather_bytes(first, last):
-            gather("slot_bytes", U8, [x_plane[:, s * T:(s + 1) * T] for s in range(PASSES)], slot_bytes, first, last)
+            gather("slot_bytes", U8, [x_plane[:, s * T:(s + 1) * T] for s in range(PASSES)], slot_bytes, first, last, None)
 
-        def first_layer(name, index, operands, grouped, copy=nc.scalar.copy):
-            acc = bank(index % 2, name + "_acc")
-            for s in range(PASSES):
-                lhsT, lhsT_scale, rhs, rhs_scale = operands(s)
-                nc.tensor.matmul_mx(out=acc[:], lhsT=lhsT, lhsT_scale=lhsT_scale, rhs=rhs, rhs_scale=rhs_scale,
-                                    start=(s == 0), stop=(s == PASSES - 1))
-            hidden = tile(name + "_rows", H, BF16)
-            nc.scalar.activation(
-                out=hidden[:].rearrange("c (u p b) -> c u p b", u=2, b=2),
-                in_=acc[:].rearrange("c (p u b) -> c u p b", u=2, b=2),
-                func=ACT.Silu,
-            )
-            turned = bank(2 + index % 2, name + "_turned")
-            for u in range(2):
-                nc.tensor.transpose(turned[:, u * P:(u + 1) * P], hidden[:].bitcast(F32)[:, u * P:(u + 1) * P], ident[:])
-            copy(
-                out=grouped.bitcast(F32).rearrange("p (c u) -> p c u", u=2),
-                in_=turned[:, 0:2 * P].rearrange("p (u c) -> p c u", u=2),
-            )
+        def deal(engine, name, source, dtype, tag=None):
+            dealt = tile(name, source.shape[1], source.dtype, tag)
+            engine.tensor_copy(dealt[:].bitcast(dtype).rearrange("p (t m) -> p t m", t=PACK),
+                               source.bitcast(dtype).rearrange("p (m t) -> p t m", t=PACK))
+            return dealt
 
-        h_codes, h_plane, y = {}, {}, {}
+        h_codes, h_plane = {}, {}
 
         def expert_first(e):
             grouped = tile("h_grouped%d" % e, PACK * C, BF16)
-            first_layer(
-                "h%d" % e, e,
-                lambda s: (
-                    slot_words[e, s].bitcast(FP8X4),
-                    slot_bytes[e, s],
-                    w1[e][:, s * 2 * H:(s + 1) * 2 * H].bitcast(FP4X4),
-                    w1_plane[:, (e * PASSES + s) * H:(e * PASSES + s + 1) * H],
-                ),
-                grouped[:],
-                nc.vector.tensor_copy if e == 0 else nc.scalar.copy,
+            acc = bank(e % 2, "h%d_acc" % e)
+            for s in range(PASSES):
+                nc.tensor.matmul_mx(
+                    out=acc[:], lhsT=slot_words[e, s].bitcast(FP8X4), lhsT_scale=slot_bytes[e, s],
+                    rhs=w1[e][:, s * FP4_ROW:(s + 1) * FP4_ROW].bitcast(FP4X4),
+                    rhs_scale=w1_plane[:, (e * PASSES + s) * H:(e * PASSES + s + 1) * H],
+                    start=(s == 0), stop=(s == PASSES - 1))
+            rows = tile("h%d_rows" % e, H, BF16)
+            nc.scalar.activation(
+                out=rows[:].rearrange("c (u p b) -> c u p b", u=2, b=2),
+                in_=acc[:].rearrange("c (p u b) -> c u p b", u=2, b=2),
+                func=ACT.Silu,
+            )
+            turned = bank(2 + e % 2, "h%d_turned" % e)
+            for u in range(2):
+                nc.tensor.transpose(turned[:, u * P:(u + 1) * P], rows[:].bitcast(F32)[:, u * P:(u + 1) * P], ident[:])
+            nc.scalar.copy(
+                out=grouped[:].bitcast(F32).rearrange("p (c u) -> p c u", u=2),
+                in_=turned[:, 0:2 * P].rearrange("p (u c) -> p c u", u=2),
             )
             h_codes[e] = tile("h_codes%d" % e, C, U32)
             h_plane[e] = tile("h_plane%d" % e, C, U8)
             nc.vector.quantize_mx(out=h_codes[e][:].bitcast(FP8X4), scales=h_plane[e][:], in_=grouped[:])
 
-        y_all = tile("y_all", PACK * T, F32)
+        gated = tile("gated", PACK * T, F32)
+        gated_by_t = gated[:].rearrange("p (t j) -> p t j", t=PACK)
 
-        def expert_second(e, acc_bank, parts):
+        def expert_second_dealt(codes, plane):
+            for first in (0, 2):
+                acc = bank(4 + first // 2, "y_acc0_%d" % first)
+                for t in (first, first + 1):
+                    nc.tensor.matmul_mx(
+                        out=acc[:, t * C:(t + 1) * C], lhsT=codes[:, 2 * t * P:2 * (t + 1) * P].bitcast(FP4X4),
+                        lhsT_scale=plane[:, t * P:(t + 1) * P],
+                        rhs=h_codes[0][:].bitcast(FP8X4), rhs_scale=h_plane[0][:], start=True, stop=True)
+                nc.vector.tensor_tensor(
+                    gated_by_t[:, first:first + 2, 0:C],
+                    acc[:].rearrange("p (t c) -> p t c", t=PACK)[:, first:first + 2, :],
+                    gate_rows[:].unsqueeze(1).to_broadcast([P, 2, C]), ALU.mult)
+
+        def expert_second_turned(e, acc_bank, turn_bank):
             acc = bank(acc_bank, "y_acc%d" % e)
             nc.tensor.matmul_mx(out=acc[:], lhsT=h_codes[e][:].bitcast(FP8X4), lhsT_scale=h_plane[e][:],
                                 rhs=w2[e].bitcast(FP4X4), rhs_scale=w2_plane[:, e * N:(e + 1) * N],
                                 start=True, stop=True)
             rows = tile("y_rows%d" % e, N, F32)
-            for first, last, turn_bank, copy in parts:
-                nc.scalar.activation(
-                    out=rows[:].rearrange("c (t p) -> c t p", t=PACK)[:, first:last, :],
-                    in_=acc[:].rearrange("c (p t) -> c t p", t=PACK)[:, first:last, :],
-                    func=ACT.Copy, scale=gate_col[:, e:e + 1],
-                )
-            for first, last, turn_bank, copy in parts:
-                turned = bank(turn_bank, "y_turned%d_%d" % (e, first))
-                for t in range(first, last):
-                    nc.tensor.transpose(turned[:, t * C:(t + 1) * C], rows[:, t * P:(t + 1) * P], ident[:])
-                copy(
-                    out=y_all[:].rearrange("p (t j) -> p t j", t=PACK)[:, first:last, e * C:(e + 1) * C],
-                    in_=turned[:].rearrange("p (t c) -> p t c", t=PACK)[:, first:last, :],
-                )
+            nc.scalar.activation(
+                out=rows[:].rearrange("c (t p) -> c t p", t=PACK),
+                in_=acc[:].rearrange("c (p t) -> c t p", t=PACK),
+                func=ACT.Copy, scale=gate_col[:, e - 1:e],
+            )
+            turned = bank(turn_bank, "y_turned%d" % e)
+            for t in range(PACK):
+                nc.tensor.transpose(turned[:, t * C:(t + 1) * C], rows[:, t * P:(t + 1) * P], ident[:])
+            nc.scalar.copy(out=gated_by_t[:, :, e * C:(e + 1) * C], in_=turned[:].rearrange("p (t c) -> p t c", t=PACK))
 
-        routed = {}
+        routed = [tile("routed%d" % t, T, F32) for t in range(LAST)]
 
         def scatter(t, first, last):
             nc.vector.tensor_copy(
                 routed[t][:].indirect(offsets[:, first * LIST_COLS:last * LIST_COLS]),
-                y_all[:, t * T + first * C:t * T + last * C],
+                gated[:, t * T + first * C:t * T + last * C],
             )
 
-        for t in range(PACK):
-            routed[t] = tile("routed%d" % t, T, F32)
 
         gather_words(0, 1)
         gather_bytes(0, 1)
         gather_words(1, 3)
         gather_bytes(1, 2)
         gather_bytes(2, 4)
+        w2_dealt = deal(nc.vector, "w2_dealt", w2[0], U16)
+        w2_plane_dealt = deal(nc.vector, "w2_plane_dealt", w2_plane[:, 0:N], U8)
         expert_first(0)
         gather_words(3, 4, "slot_words0")
         expert_first(1)
-        expert_second(0, 4, ((0, 2, 6, nc.vector.tensor_copy), (2, 4, 7, nc.scalar.copy)))
+        expert_second_dealt(w2_dealt, w2_plane_dealt)
+        w1s_dealt = [deal(nc.gpsimd, "w1s_dealt0", w1s[:, 0:H], I32, "h_grouped1"),
+                     deal(nc.gpsimd, "w1s_dealt1", w1s[:, H:2 * H], I32)]
+        w1s_plane_dealt = [deal(nc.gpsimd, "w1s_plane_dealt%d" % s, w1s_plane[:, s * H:(s + 1) * H], U8)
+                           for s in range(PASSES)]
         expert_first(2)
-        w2s_dealt = tile("w2s_dealt", N, I32, "h_grouped1")
-        w2s_plane_dealt = tile("w2s_plane_dealt", N, U8, "h_grouped0")
-        nc.vector.tensor_copy(w2s_dealt[:].rearrange("p (t m) -> p m t", t=PACK), w2s[:].rearrange("p (m t) -> p m t", t=PACK))
-        nc.vector.tensor_copy(w2s_plane_dealt[:].rearrange("p (t m) -> p m t", t=PACK), w2s_plane[:].rearrange("p (m t) -> p m t", t=PACK))
+        routed.append(tile("routed%d" % LAST, T, F32, "h_grouped2"))
         for t in range(PACK):
             scatter(t, 0, 1)
         expert_first(3)
-        expert_second(1, 5, ((0, 4, 6, nc.scalar.copy),))
-        for t in range(PACK - 1):
+        w2s_dealt = deal(nc.gpsimd, "w2s_dealt", w2s[:], I32, "h_grouped3")
+        w2s_plane_dealt = deal(nc.gpsimd, "w2s_plane_dealt", w2s_plane[:], U8, "w2s")
+        expert_second_turned(1, 6, 7)
+        for t in range(LAST):
             scatter(t, 1, 2)
-        expert_second(2, 4, ((0, 4, 7, nc.scalar.copy),))
-        for t in range(PACK - 1):
+        expert_second_turned(2, 4, 5)
+        for t in range(LAST):
             scatter(t, 2, 3)
 
+
         hs_grouped = tile("hs_grouped", PACK * T, BF16)
-        for b in range(T // P):
-            first_layer(
-                "hs%d" % b, b,
-                lambda s: (
-                    x_tok[s][:, b * P:(b + 1) * P].bitcast(FP8X4),
-                    x_plane[:, s * T + b * P:s * T + (b + 1) * P],
-                    w1s[s].bitcast(FP8X4),
-                    w1s_plane[:, s * H:(s + 1) * H],
-                ),
-                hs_grouped[:, b * PACK * P:(b + 1) * PACK * P],
-            )
+
+        def shared_first(b):
+            acc = bank(b, "hs%d_acc" % b)
+            for t in range(PACK):
+                for s in range(PASSES):
+                    nc.tensor.matmul_mx(
+                        out=acc[:, t * P:(t + 1) * P], lhsT=w1s_dealt[s][:, t * P:(t + 1) * P].bitcast(FP8X4),
+                        lhsT_scale=w1s_plane_dealt[s][:, t * P:(t + 1) * P],
+                        rhs=x_tok[s][:, b * P:(b + 1) * P].bitcast(FP8X4),
+                        rhs_scale=x_plane[:, s * T + b * P:s * T + (b + 1) * P],
+                        start=(s == 0), stop=(s == PASSES - 1))
+            nc.scalar.activation(
+                out=hs_grouped[:, b * PACK * P:(b + 1) * PACK * P].rearrange("p (c t) -> p c t", t=PACK),
+                in_=acc[:].rearrange("p (t c) -> p c t", t=PACK), func=ACT.Silu)
+
+        blocks = T // P
+        for b in range(blocks - 1):
+            shared_first(b)
+        expert_second_turned(3, 0, 2)
+        shared_first(blocks - 1)
         hs_codes = tile("hs_codes", T, U32)
         hs_plane = tile("hs_plane", T, U8)
         nc.vector.quantize_mx(out=hs_codes[:].bitcast(FP8X4), scales=hs_plane[:], in_=hs_grouped[:])
-
-        expert_second(3, 0, ((0, 4, 3, nc.scalar.copy),))
-        for t in range(PACK - 1):
+        for t in range(LAST):
             scatter(t, 3, 4)
 
         ys = []
@@ -244,36 +264,33 @@ def tile_moe_shf_mlp_silu_kernel(
                                 rhs=hs_codes[:].bitcast(FP8X4), rhs_scale=hs_plane[:], start=True, stop=True)
             ys.append(acc)
 
+
         total = tile("total", PACK * T, F32)
         out_rows = out_0.rearrange("(p t) c -> p t c", t=PACK)
-
-        def add(t, first, last):
-            nc.vector.tensor_tensor(total[:, t * T + first:t * T + last], ys[t][:, first:last], routed[t][:, first:last], ALU.add)
-
-        def store(t):
-            nc.sync.dma_start(out=out_rows[:, t, :], in_=total[:, t * T:(t + 1) * T])
-
-        scatter(3, 1, 4)
-        for t in range(PACK - 1):
+        scatter(LAST, 1, E)
+        for t in range(LAST):
             shared = tile("shared%d" % t, T, F32)
             nc.scalar.copy(out=shared[:], in_=ys[t][:])
             nc.gpsimd.tensor_tensor(total[:, t * T:(t + 1) * T], shared[:], routed[t][:], ALU.add)
-            store(t)
+            if t < LAST - 1:
+                nc.sync.dma_start(out=out_rows[:, t, :], in_=total[:, t * T:(t + 1) * T])
         half = T // 2
-        add(3, half, T)
-        add(3, 0, half)
-        store(3)
+        for first in (half, 0):
+            nc.vector.tensor_tensor(total[:, LAST * T + first:LAST * T + first + half], ys[LAST][:, first:first + half],
+                                    routed[LAST][:, first:first + half], ALU.add)
+        nc.sync.dma_start(out=out_rows[:, LAST - 1:PACK, :],
+                          in_=total[:, (LAST - 1) * T:PACK * T].rearrange("p (t c) -> p t c", t=2))
 
-        grouped = [tile("out_grouped%d" % i, PACK * half, BF16) for i in range(2)]
+        out_grouped = [tile("out_grouped%d" % i, PACK * half, BF16) for i in range(2)]
         by_token = total[:].rearrange("p (t c) -> p c t", t=PACK)
-        nc.scalar.copy(out=grouped[1][:].rearrange("p (c t) -> p c t", t=PACK), in_=by_token[:, half:T, :])
-        nc.vector.tensor_copy(grouped[0][:].rearrange("p (c t) -> p c t", t=PACK), by_token[:, 0:half, :])
+        nc.scalar.copy(out=out_grouped[1][:].rearrange("p (c t) -> p c t", t=PACK), in_=by_token[:, half:T, :])
+        nc.vector.tensor_copy(out_grouped[0][:].rearrange("p (c t) -> p c t", t=PACK), by_token[:, 0:half, :])
         out_codes = tile("out_codes", T, U32)
         out_plane = tile("out_plane", T, U8)
         words_out = out_1[0].rearrange("p c d -> p (c d)").bitcast(I32)
         for i in range(2):
             cols = slice(i * half, (i + 1) * half)
-            nc.vector.quantize_mx(out=out_codes[:, cols].bitcast(FP8X4), scales=out_plane[:, cols], in_=grouped[i][:])
+            nc.vector.quantize_mx(out=out_codes[:, cols].bitcast(FP8X4), scales=out_plane[:, cols], in_=out_grouped[i][:])
             nc.sync.dma_start(out=words_out[:, cols], in_=out_codes[:, cols].bitcast(I32))
         for r in range(4):
             queue = nc.sync if r % 2 else nc.scalar

@@ -23,6 +23,7 @@ PASSES = K // (P * PACK)
 LIST_COLS = C // 16
 PLANE = 512
 FP4_ROW = 2 * PLANE
+YS_BANKS = (6, 7, 0, 2)
 LAST = PACK - 1
 
 
@@ -49,8 +50,8 @@ def tile_moe_shf_mlp_silu_kernel(
                 engine.memset(zeroed[:, i * share:(i + 1) * share].bitcast(I32), 0)
             return zeroed
 
-        def load_planes(dst, rows):
-            for r in range(4):
+        def load_planes(dst, rows, loads=range(4)):
+            for r in loads:
                 nc.sync.dma_start(
                     out=dst[r:P:32, :].bitcast(I32).rearrange("q (g w) -> q g w", g=rows.shape[0]),
                     in_=rows[:, r:16:4, :].rearrange("g q c -> q g c").bitcast(I32),
@@ -66,21 +67,22 @@ def tile_moe_shf_mlp_silu_kernel(
             )
 
         x_plane = zero_planes("x_plane", PASSES, (nc.vector,))
-        w1_plane = zero_planes("w1_plane", E * PASSES, (nc.vector, nc.gpsimd))
+        w1_planes = [zero_planes("w1_plane%d" % i, 2 * PASSES, (nc.vector,)) for i in range(2)]
         w2_plane = zero_planes("w2_plane", E, (nc.vector,))
         w1s_plane = zero_planes("w1s_plane", PASSES, (nc.vector,))
         w2s_plane = zero_planes("w2s_plane", 1, (nc.vector,))
 
         ident = tile("ident", P, F32)
-        make_identity(nc, ident[:])
+        nc.vector.memset(ident[:], 0.0)
+        make_identity(nc, ident[:], nomemset=True)
 
         offsets = sb.tile([P, T // 16], U16, name="offsets")
         x_tok = [tile("x_tok%d" % s, T, I32) for s in range(PASSES)]
         w1_first = [tile("w1_%d" % e, PASSES * FP4_ROW, U8) for e in range(2)]
         w1_last = tile("w1_last", 2 * PASSES * FP4_ROW, U8)
         w1 = [w1_first[0][:], w1_first[1][:], w1_last[:, 0:PASSES * FP4_ROW], w1_last[:, PASSES * FP4_ROW:]]
-        w2_pairs = [tile("w2_%d" % i, 2 * FP4_ROW, U8) for i in range(2)]
-        w2 = [w2_pairs[e // 2][:, e % 2 * FP4_ROW:(e % 2 + 1) * FP4_ROW] for e in range(E)]
+        w2_first = tile("w2_0", FP4_ROW, U8)
+        w2_last = tile("w2_last", (E - 1) * FP4_ROW, U8)
         w1s = tile("w1s", PASSES * H, I32)
         w2s = tile("w2s", N, I32)
         gate_col = tile("gate_col", E - 1, F32)
@@ -88,41 +90,43 @@ def tile_moe_shf_mlp_silu_kernel(
 
         nc.sync.dma_start(offsets[:], offs)
         load_fp8(x_tok[0], x_words[0])
+        load_planes(x_plane, x_scales, (0, 1))
         load_fp8(x_tok[1], x_words[1])
-        load_planes(x_plane, x_scales)
+        load_planes(x_plane, x_scales, (2, 3))
         load_fp4(w1_first[0], w1_words[0])
-        load_planes(w1_plane, w1_scales.rearrange("e s b c -> (e s) b c"))
+        load_planes(w1_planes[0], w1_scales[0:2].rearrange("e s b c -> (e s) b c"))
         load_fp4(w1_first[1], w1_words[1])
-        load_fp4(w2_pairs[0], w2_words[0:2, 0])
         load_planes(w2_plane, w2_scales.rearrange("e s b c -> (e s) b c"))
-        load_fp4(w1_last, w1_words[2:4].rearrange("e s p b -> (e s) p b"))
+        load_fp4(w2_first, w2_words[0])
         nc.sync.dma_start(out=gate_rows[:], in_=gate[:, 0:C])
+        load_fp4(w1_last, w1_words[2:4].rearrange("e s p b -> (e s) p b"))
+        load_planes(w1_planes[1], w1_scales[2:4].rearrange("e s b c -> (e s) b c"))
+        load_fp4(w2_last, w2_words[1:E, 0])
         with nc.allow_non_contiguous_dma(reason="one gate value a partition; all rows of gate are equal"):
             nc.sync.dma_start(out=gate_col[:], in_=gate[0, C:].rearrange("(e u) -> u e", e=E - 1))
         nc.sync.dma_start(out=w1s[:].rearrange("p (s c) -> p s c", s=PASSES),
                           in_=w1s_words.rearrange("s p c d -> p s (c d)").bitcast(I32))
         load_planes(w1s_plane, w1s_scales)
-        load_fp4(w2_pairs[1], w2_words[2:4, 0])
         load_fp8(w2s, w2s_words[0])
         load_planes(w2s_plane, w2s_scales)
 
 
         slot_words, slot_bytes = {}, {}
 
-        def gather(name, dtype, windows, into, first, last, tag):
+        def gather(name, dtype, windows, into, first, last, tag, passes):
             width = (last - first) * C
-            gathered = tile("%s%d" % (name, first), PASSES * width, dtype, tag)
+            gathered = tile("%s%d_%d" % (name, first, passes[0]), len(passes) * width, dtype, tag)
             entries = offsets[:, first * LIST_COLS:last * LIST_COLS]
-            for s in range(PASSES):
-                nc.vector.tensor_copy(gathered[:, s * width:(s + 1) * width], windows[s].indirect(entries))
+            for i, s in enumerate(passes):
+                nc.vector.tensor_copy(gathered[:, i * width:(i + 1) * width], windows[s].indirect(entries))
                 for e in range(first, last):
-                    into[e, s] = gathered[:, s * width + (e - first) * C:s * width + (e - first + 1) * C]
+                    into[e, s] = gathered[:, i * width + (e - first) * C:i * width + (e - first + 1) * C]
 
-        def gather_words(first, last, tag=None):
-            gather("slot_words", U32, [x_tok[s][:].bitcast(U32) for s in range(PASSES)], slot_words, first, last, tag)
+        def gather_words(first, last, tag=None, passes=(0, 1)):
+            gather("slot_words", U32, [x_tok[s][:].bitcast(U32) for s in range(PASSES)], slot_words, first, last, tag, passes)
 
         def gather_bytes(first, last):
-            gather("slot_bytes", U8, [x_plane[:, s * T:(s + 1) * T] for s in range(PASSES)], slot_bytes, first, last, None)
+            gather("slot_bytes", U8, [x_plane[:, s * T:(s + 1) * T] for s in range(PASSES)], slot_bytes, first, last, None, (0, 1))
 
         def deal(engine, name, source, dtype, tag=None):
             dealt = tile(name, source.shape[1], source.dtype, tag)
@@ -130,135 +134,157 @@ def tile_moe_shf_mlp_silu_kernel(
                                source.bitcast(dtype).rearrange("p (m t) -> p t m", t=PACK))
             return dealt
 
-        h_codes, h_plane = {}, {}
-
-        def expert_first(e):
-            grouped = tile("h_grouped%d" % e, PACK * C, BF16)
-            acc = bank(e % 2, "h%d_acc" % e)
+        def first_sums(name, acc_bank, codes, codes_plane, weights, weights_plane, fmt, parts=1):
+            acc = bank(acc_bank, name + "_acc")
             for s in range(PASSES):
-                nc.tensor.matmul_mx(
-                    out=acc[:], lhsT=slot_words[e, s].bitcast(FP8X4), lhsT_scale=slot_bytes[e, s],
-                    rhs=w1[e][:, s * FP4_ROW:(s + 1) * FP4_ROW].bitcast(FP4X4),
-                    rhs_scale=w1_plane[:, (e * PASSES + s) * H:(e * PASSES + s + 1) * H],
-                    start=(s == 0), stop=(s == PASSES - 1))
-            rows = tile("h%d_rows" % e, H, BF16)
-            nc.scalar.activation(
-                out=rows[:].rearrange("c (u p b) -> c u p b", u=2, b=2),
-                in_=acc[:].rearrange("c (p u b) -> c u p b", u=2, b=2),
-                func=ACT.Silu,
-            )
-            turned = bank(2 + e % 2, "h%d_turned" % e)
+                nc.tensor.matmul_mx(out=acc[:], lhsT=codes[s].bitcast(FP8X4), lhsT_scale=codes_plane[s],
+                                    rhs=weights[s].bitcast(fmt), rhs_scale=weights_plane[s],
+                                    start=(s == 0), stop=(s == PASSES - 1))
+            rows = tile(name + "_rows", H, BF16)
+            step = 2 // parts
+            for u in range(0, 2, step):
+                nc.scalar.activation(
+                    out=rows[:].rearrange("c (u p b) -> c u p b", u=2, b=2)[:, u:u + step],
+                    in_=acc[:].rearrange("c (p u b) -> c u p b", u=2, b=2)[:, u:u + step],
+                    func=ACT.Silu,
+                )
+            return rows
+
+        def turn_hidden(name, rows, turn_bank, grouped):
+            turned = bank(turn_bank, name + "_turned")
             for u in range(2):
                 nc.tensor.transpose(turned[:, u * P:(u + 1) * P], rows[:].bitcast(F32)[:, u * P:(u + 1) * P], ident[:])
             nc.scalar.copy(
-                out=grouped[:].bitcast(F32).rearrange("p (c u) -> p c u", u=2),
+                out=grouped.bitcast(F32).rearrange("p (c u) -> p c u", u=2),
                 in_=turned[:, 0:2 * P].rearrange("p (u c) -> p c u", u=2),
             )
-            h_codes[e] = tile("h_codes%d" % e, C, U32)
+
+        def expert_sums(e, acc_bank, parts=1):
+            return first_sums(
+                "h%d" % e, acc_bank, [slot_words[e, s] for s in range(PASSES)], [slot_bytes[e, s] for s in range(PASSES)],
+                [w1[e][:, s * FP4_ROW:(s + 1) * FP4_ROW] for s in range(PASSES)],
+                [w1_planes[e // 2][:, (e % 2 * PASSES + s) * H:(e % 2 * PASSES + s + 1) * H] for s in range(PASSES)],
+                FP4X4, parts)
+
+        h_codes, h_plane = {}, {}
+
+        def expert_quantise(e, rows, turn_bank, codes_tag=None):
+            grouped = tile("h_grouped%d" % e, PACK * C, BF16)
+            turn_hidden("h%d" % e, rows, turn_bank, grouped[:])
+            h_codes[e] = tile("h_codes%d" % e, C, U32, codes_tag)
             h_plane[e] = tile("h_plane%d" % e, C, U8)
             nc.vector.quantize_mx(out=h_codes[e][:].bitcast(FP8X4), scales=h_plane[e][:], in_=grouped[:])
 
-        gated = tile("gated", PACK * T, F32)
-        gated_by_t = gated[:].rearrange("p (t j) -> p t j", t=PACK)
+        results = {}
 
-        def expert_second_dealt(codes, plane):
-            for first in (0, 2):
-                acc = bank(4 + first // 2, "y_acc0_%d" % first)
-                for t in (first, first + 1):
+        def leave_bank(name, acc, e, first, last, tag=None):
+            part = tile(name, (last - first) * C, F32, tag)
+            nc.scalar.copy(out=part[:], in_=acc[:, first * C:last * C])
+            for t in range(first, last):
+                results[t, e] = part[:, (t - first) * C:(t - first + 1) * C]
+
+        def expert_second_dealt(codes, plane, banks):
+            for first, last, acc_bank in ((0, 1, banks[0]), (1, PACK, banks[1])):
+                acc = bank(acc_bank, "y_acc0_%d" % first)
+                for t in range(first, last):
                     nc.tensor.matmul_mx(
                         out=acc[:, t * C:(t + 1) * C], lhsT=codes[:, 2 * t * P:2 * (t + 1) * P].bitcast(FP4X4),
                         lhsT_scale=plane[:, t * P:(t + 1) * P],
                         rhs=h_codes[0][:].bitcast(FP8X4), rhs_scale=h_plane[0][:], start=True, stop=True)
-                nc.vector.tensor_tensor(
-                    gated_by_t[:, first:first + 2, 0:C],
-                    acc[:].rearrange("p (t c) -> p t c", t=PACK)[:, first:first + 2, :],
-                    gate_rows[:].unsqueeze(1).to_broadcast([P, 2, C]), ALU.mult)
+                leave_bank("y0_%d" % first, acc, 0, first, last)
 
-        def expert_second_turned(e, acc_bank, turn_bank):
+        def expert_second_rows(e, acc_bank):
             acc = bank(acc_bank, "y_acc%d" % e)
             nc.tensor.matmul_mx(out=acc[:], lhsT=h_codes[e][:].bitcast(FP8X4), lhsT_scale=h_plane[e][:],
-                                rhs=w2[e].bitcast(FP4X4), rhs_scale=w2_plane[:, e * N:(e + 1) * N],
-                                start=True, stop=True)
+                                rhs=w2_last[:, (e - 1) * FP4_ROW:e * FP4_ROW].bitcast(FP4X4),
+                                rhs_scale=w2_plane[:, e * N:(e + 1) * N], start=True, stop=True)
             rows = tile("y_rows%d" % e, N, F32)
             nc.scalar.activation(
                 out=rows[:].rearrange("c (t p) -> c t p", t=PACK),
                 in_=acc[:].rearrange("c (p t) -> c t p", t=PACK),
                 func=ACT.Copy, scale=gate_col[:, e - 1:e],
             )
+            return rows
+
+        def turn_results(e, rows, turn_bank):
             turned = bank(turn_bank, "y_turned%d" % e)
             for t in range(PACK):
                 nc.tensor.transpose(turned[:, t * C:(t + 1) * C], rows[:, t * P:(t + 1) * P], ident[:])
-            nc.scalar.copy(out=gated_by_t[:, :, e * C:(e + 1) * C], in_=turned[:].rearrange("p (t c) -> p t c", t=PACK))
+            return turned
 
-        routed = [tile("routed%d" % t, T, F32) for t in range(LAST)]
+        routed = {}
 
-        def scatter(t, first, last):
-            nc.vector.tensor_copy(
-                routed[t][:].indirect(offsets[:, first * LIST_COLS:last * LIST_COLS]),
-                gated[:, t * T + first * C:t * T + last * C],
-            )
-
-
-        gather_words(0, 1)
-        gather_bytes(0, 1)
-        gather_words(1, 3)
-        gather_bytes(1, 2)
-        gather_bytes(2, 4)
-        w2_dealt = deal(nc.vector, "w2_dealt", w2[0], U16)
-        w2_plane_dealt = deal(nc.vector, "w2_plane_dealt", w2_plane[:, 0:N], U8)
-        expert_first(0)
-        gather_words(3, 4, "slot_words0")
-        expert_first(1)
-        expert_second_dealt(w2_dealt, w2_plane_dealt)
-        w1s_dealt = [deal(nc.gpsimd, "w1s_dealt0", w1s[:, 0:H], I32, "h_grouped1"),
-                     deal(nc.gpsimd, "w1s_dealt1", w1s[:, H:2 * H], I32)]
-        w1s_plane_dealt = [deal(nc.gpsimd, "w1s_plane_dealt%d" % s, w1s_plane[:, s * H:(s + 1) * H], U8)
-                           for s in range(PASSES)]
-        expert_first(2)
-        routed.append(tile("routed%d" % LAST, T, F32, "h_grouped2"))
-        for t in range(PACK):
-            scatter(t, 0, 1)
-        expert_first(3)
-        w2s_dealt = deal(nc.gpsimd, "w2s_dealt", w2s[:], I32, "h_grouped3")
-        w2s_plane_dealt = deal(nc.gpsimd, "w2s_plane_dealt", w2s_plane[:], U8, "w2s")
-        expert_second_turned(1, 6, 7)
-        for t in range(LAST):
-            scatter(t, 1, 2)
-        expert_second_turned(2, 4, 5)
-        for t in range(LAST):
-            scatter(t, 2, 3)
-
+        def scatter(t, e):
+            window = routed[t][:].indirect(offsets[:, e * LIST_COLS:(e + 1) * LIST_COLS])
+            if e == 0:
+                nc.vector.tensor_tensor(window, results[t, e], gate_rows[:], ALU.mult)
+            else:
+                nc.vector.tensor_copy(window, results[t, e])
 
         hs_grouped = tile("hs_grouped", PACK * T, BF16)
 
-        def shared_first(b):
-            acc = bank(b, "hs%d_acc" % b)
-            for t in range(PACK):
-                for s in range(PASSES):
-                    nc.tensor.matmul_mx(
-                        out=acc[:, t * P:(t + 1) * P], lhsT=w1s_dealt[s][:, t * P:(t + 1) * P].bitcast(FP8X4),
-                        lhsT_scale=w1s_plane_dealt[s][:, t * P:(t + 1) * P],
-                        rhs=x_tok[s][:, b * P:(b + 1) * P].bitcast(FP8X4),
-                        rhs_scale=x_plane[:, s * T + b * P:s * T + (b + 1) * P],
-                        start=(s == 0), stop=(s == PASSES - 1))
-            nc.scalar.activation(
-                out=hs_grouped[:, b * PACK * P:(b + 1) * PACK * P].rearrange("p (c t) -> p c t", t=PACK),
-                in_=acc[:].rearrange("p (t c) -> p c t", t=PACK), func=ACT.Silu)
+        def shared_sums(b, acc_bank):
+            return first_sums(
+                "hs%d" % b, acc_bank, [x_tok[s][:, b * P:(b + 1) * P] for s in range(PASSES)],
+                [x_plane[:, s * T + b * P:s * T + (b + 1) * P] for s in range(PASSES)],
+                [w1s[:, s * H:(s + 1) * H] for s in range(PASSES)],
+                [w1s_plane[:, s * H:(s + 1) * H] for s in range(PASSES)], FP8X4)
 
-        blocks = T // P
-        for b in range(blocks - 1):
-            shared_first(b)
-        expert_second_turned(3, 0, 2)
-        shared_first(blocks - 1)
+        def shared_turn(b, rows, turn_bank):
+            turn_hidden("hs%d" % b, rows, turn_bank, hs_grouped[:, b * PACK * P:(b + 1) * PACK * P])
+
+        gather_words(0, 1)
+        gather_words(1, 2)
+        gather_bytes(0, 1)
+        gather_bytes(1, 2)
+        gather_bytes(2, 4)
+        rows0 = expert_sums(0, 0, 2)
+        gather_words(2, 3, "slot_words0_0")
+        w2_plane_dealt = deal(nc.vector, "w2_plane_dealt", w2_plane[:, 0:N], U8)
+        w2_dealt = deal(nc.vector, "w2_dealt", w2_first[:], U16)
+        expert_quantise(0, rows0, 2, "w2_0")
+        rows1 = expert_sums(1, 1)
+        gather_words(3, 4, "slot_words1_0", (0,))
+        expert_quantise(1, rows1, 3, "h_grouped0")
+        gather_words(3, 4, "h_grouped1", (1,))
+        expert_second_dealt(w2_dealt, w2_plane_dealt, (4, 5))
+        rows2 = expert_sums(2, 6)
+        rows3 = expert_sums(3, 7)
+        expert_quantise(2, rows2, 0)
+        y_rows1 = expert_second_rows(1, 1)
+        expert_quantise(3, rows3, 2)
+        for t, tag in enumerate((None, None, None, "h_grouped2")):
+            routed[t] = tile("routed%d" % t, T, F32, tag)
+        for t in range(PACK):
+            scatter(t, 0)
+        w2s_dealt = deal(nc.gpsimd, "w2s_dealt", w2s[:], I32, "y0_1")
+        w2s_plane_dealt = deal(nc.gpsimd, "w2s_plane_dealt", w2s_plane[:], U8, "w2s")
+        leave_bank("y1", turn_results(1, y_rows1, 3), 1, 0, PACK)
+        for t in range(PACK):
+            scatter(t, 1)
+        y_rows2 = expert_second_rows(2, 4)
+        hs_rows0 = shared_sums(0, 5)
+        leave_bank("y2", turn_results(2, y_rows2, 6), 2, 0, PACK)
+        for t in range(PACK):
+            scatter(t, 2)
+        hs_rows1 = shared_sums(1, 7)
+        shared_turn(0, hs_rows0, 0)
+        hs_rows2 = shared_sums(2, 1)
+        shared_turn(1, hs_rows1, 2)
+        hs_rows3 = shared_sums(3, 3)
+        shared_turn(2, hs_rows2, 4)
+        y_rows3 = expert_second_rows(3, 1)
+        shared_turn(3, hs_rows3, 5)
         hs_codes = tile("hs_codes", T, U32)
         hs_plane = tile("hs_plane", T, U8)
         nc.vector.quantize_mx(out=hs_codes[:].bitcast(FP8X4), scales=hs_plane[:], in_=hs_grouped[:])
-        for t in range(LAST):
-            scatter(t, 3, 4)
+        leave_bank("y3", turn_results(3, y_rows3, 3), 3, 0, PACK)
+        for t in range(PACK):
+            scatter(t, 3)
 
         ys = []
         for t in range(PACK):
-            acc = bank(4 + t, "ys%d" % t)
+            acc = bank(YS_BANKS[t], "ys%d" % t)
             nc.tensor.matmul_mx(out=acc[:], lhsT=w2s_dealt[:, t * P:(t + 1) * P].bitcast(FP8X4),
                                 lhsT_scale=w2s_plane_dealt[:, t * P:(t + 1) * P],
                                 rhs=hs_codes[:].bitcast(FP8X4), rhs_scale=hs_plane[:], start=True, stop=True)
@@ -267,17 +293,16 @@ def tile_moe_shf_mlp_silu_kernel(
 
         total = tile("total", PACK * T, F32)
         out_rows = out_0.rearrange("(p t) c -> p t c", t=PACK)
-        scatter(LAST, 1, E)
-        for t in range(LAST):
+        for t in range(2):
             shared = tile("shared%d" % t, T, F32)
             nc.scalar.copy(out=shared[:], in_=ys[t][:])
             nc.gpsimd.tensor_tensor(total[:, t * T:(t + 1) * T], shared[:], routed[t][:], ALU.add)
-            if t < LAST - 1:
-                nc.sync.dma_start(out=out_rows[:, t, :], in_=total[:, t * T:(t + 1) * T])
+            nc.sync.dma_start(out=out_rows[:, t, :], in_=total[:, t * T:(t + 1) * T])
         half = T // 2
         for first in (half, 0):
-            nc.vector.tensor_tensor(total[:, LAST * T + first:LAST * T + first + half], ys[LAST][:, first:first + half],
-                                    routed[LAST][:, first:first + half], ALU.add)
+            for t in (2, 3):
+                nc.vector.tensor_tensor(total[:, t * T + first:t * T + first + half], ys[t][:, first:first + half],
+                                        routed[t][:, first:first + half], ALU.add)
         nc.sync.dma_start(out=out_rows[:, LAST - 1:PACK, :],
                           in_=total[:, (LAST - 1) * T:PACK * T].rearrange("p (t c) -> p t c", t=2))
 

@@ -23,6 +23,7 @@ PASSES = K // (P * PACK)
 LIST_COLS = C // 16
 PLANE = 512
 FP4_ROW = 2 * PLANE
+PLACED = {"h_grouped0": 512, "slot_words3_0": 0, "h_codes1": 1024}
 YS_BANKS = (6, 7, 0, 2)
 LAST = PACK - 1
 
@@ -34,9 +35,12 @@ def tile_moe_shf_mlp_silu_kernel(
     nc = tc.nc
     with ExitStack() as ctx:
         sb = ctx.enter_context(tc.tile_pool(name="sb", bufs=1))
+        placed = ctx.enter_context(tc.tile_pool(name="placed", bufs=1))
         ps = ctx.enter_context(tc.psum_pool(name="ps", bufs=1))
 
         def tile(name, cols, dtype, tag=None):
+            if name in PLACED:
+                return placed.tile([P, cols], dtype, name=name, tag=name, align_bytes=64, offset=PLACED[name])
             return sb.tile([P, cols], dtype, name=name, tag=tag or name, align_bytes=64)
 
         def bank(index, name):
@@ -233,26 +237,34 @@ def tile_moe_shf_mlp_silu_kernel(
         def shared_turn(b, rows, turn_bank):
             turn_hidden("hs%d" % b, rows, turn_bank, hs_grouped[:, b * PACK * P:(b + 1) * PACK * P])
 
+        def warm(acc_bank, name, passes):
+            acc = bank(acc_bank, name)
+            for i in range(passes):
+                nc.tensor.matmul_mx(out=acc[:], lhsT=x_tok[0][:, 0:P].bitcast(FP8X4), lhsT_scale=x_plane[:, 0:P],
+                                    rhs=x_tok[0][:].bitcast(FP8X4), rhs_scale=x_plane[:, 0:T], start=True, stop=True)
+
         gather_words(0, 1)
         gather_words(1, 2)
         gather_bytes(0, 1)
         gather_bytes(1, 2)
         gather_bytes(2, 4)
+        warm(7, "warm0", 2)
         rows0 = expert_sums(0, 0, 2)
         gather_words(2, 3, "slot_words0_0")
         w2_plane_dealt = deal(nc.vector, "w2_plane_dealt", w2_plane[:, 0:N], U8)
         w2_dealt = deal(nc.vector, "w2_dealt", w2_first[:], U16)
         expert_quantise(0, rows0, 2, "w2_0")
         rows1 = expert_sums(1, 1)
-        gather_words(3, 4, "slot_words1_0", (0,))
-        expert_quantise(1, rows1, 3, "h_grouped0")
-        gather_words(3, 4, "h_grouped1", (1,))
+        gather_words(3, 4)
+        expert_quantise(1, rows1, 3)
+        warm(2, "warm1", 2)
         expert_second_dealt(w2_dealt, w2_plane_dealt, (4, 5))
         rows2 = expert_sums(2, 6)
         rows3 = expert_sums(3, 7)
         expert_quantise(2, rows2, 0)
         y_rows1 = expert_second_rows(1, 1)
         expert_quantise(3, rows3, 2)
+        warm(7, "warm3", 1)
         for t, tag in enumerate((None, None, None, "h_grouped2")):
             routed[t] = tile("routed%d" % t, T, F32, tag)
         for t in range(PACK):
@@ -271,14 +283,15 @@ def tile_moe_shf_mlp_silu_kernel(
         shared_turn(0, hs_rows0, 0)
         hs_rows2 = shared_sums(2, 1)
         shared_turn(1, hs_rows1, 2)
+        y_rows3 = expert_second_rows(3, 7)
         hs_rows3 = shared_sums(3, 3)
         shared_turn(2, hs_rows2, 4)
-        y_rows3 = expert_second_rows(3, 1)
+        turned3 = turn_results(3, y_rows3, 1)
         shared_turn(3, hs_rows3, 5)
         hs_codes = tile("hs_codes", T, U32)
         hs_plane = tile("hs_plane", T, U8)
         nc.vector.quantize_mx(out=hs_codes[:].bitcast(FP8X4), scales=hs_plane[:], in_=hs_grouped[:])
-        leave_bank("y3", turn_results(3, y_rows3, 3), 3, 0, PACK)
+        leave_bank("y3", turned3, 3, 0, PACK, "hs3_rows")
         for t in range(PACK):
             scatter(t, 3)
 

@@ -82,35 +82,34 @@ def tile_moe_shf_mlp_silu_kernel(
 
         offsets = sb.tile([P, T // 16], U16, name="offsets")
         x_tok = [tile("x_tok%d" % s, T, I32) for s in range(PASSES)]
-        w1_first = [tile("w1_%d" % e, PASSES * FP4_ROW, U8) for e in range(2)]
-        w1_last = tile("w1_last", 2 * PASSES * FP4_ROW, U8)
-        w1 = [w1_first[0][:], w1_first[1][:], w1_last[:, 0:PASSES * FP4_ROW], w1_last[:, PASSES * FP4_ROW:]]
+        w1 = [tile("w1_%d" % e, PASSES * FP4_ROW, U8) for e in range(E)]
         w2_first = tile("w2_0", FP4_ROW, U8)
         w2_last = tile("w2_last", (E - 1) * FP4_ROW, U8)
         w1s = tile("w1s", PASSES * H, I32)
         w2s = tile("w2s", N, I32)
-        gate_col = tile("gate_col", E - 1, F32)
-        gate_rows = tile("gate_rows", C, F32)
+        gate_col = tile("gate_col", 2, F32)
+        gate_rows = tile("gate_rows", 2 * C, F32)
 
         nc.sync.dma_start(offsets[:], offs)
         load_fp8(x_tok[0], x_words[0])
         load_planes(x_plane, x_scales, (0, 1))
         load_fp8(x_tok[1], x_words[1])
         load_planes(x_plane, x_scales, (2, 3))
-        load_fp4(w1_first[0], w1_words[0])
+        load_fp4(w1[0], w1_words[0])
         load_planes(w1_planes[0], w1_scales[0:2].rearrange("e s b c -> (e s) b c"))
-        load_fp4(w1_first[1], w1_words[1])
+        load_fp4(w1[1], w1_words[1])
         load_planes(w2_plane, w2_scales.rearrange("e s b c -> (e s) b c"))
         load_fp4(w2_first, w2_words[0])
-        nc.sync.dma_start(out=gate_rows[:], in_=gate[:, 0:C])
-        load_fp4(w1_last, w1_words[2:4].rearrange("e s p b -> (e s) p b"))
+        nc.sync.dma_start(out=gate_rows[:], in_=gate[:, 0:2 * C])
+        load_fp4(w1[2], w1_words[2])
         load_planes(w1_planes[1], w1_scales[2:4].rearrange("e s b c -> (e s) b c"))
+        load_fp4(w1[3], w1_words[3])
         load_fp4(w2_last, w2_words[1:E, 0])
-        with nc.allow_non_contiguous_dma(reason="one gate value a partition; all rows of gate are equal"):
-            nc.sync.dma_start(out=gate_col[:], in_=gate[0, C:].rearrange("(e u) -> u e", e=E - 1))
         nc.sync.dma_start(out=w1s[:].rearrange("p (s c) -> p s c", s=PASSES),
                           in_=w1s_words.rearrange("s p c d -> p s (c d)").bitcast(I32))
         load_planes(w1s_plane, w1s_scales)
+        with nc.allow_non_contiguous_dma(reason="one gate value a partition; all rows of gate are equal"):
+            nc.sync.dma_start(out=gate_col[:], in_=gate[0, 2 * C:].rearrange("(e u) -> u e", e=2))
         load_fp8(w2s, w2s_words[0])
         load_planes(w2s_plane, w2s_scales)
 
@@ -206,7 +205,7 @@ def tile_moe_shf_mlp_silu_kernel(
             nc.scalar.activation(
                 out=rows[:].rearrange("c (t p) -> c t p", t=PACK),
                 in_=acc[:].rearrange("c (p t) -> c t p", t=PACK),
-                func=ACT.Copy, scale=gate_col[:, e - 1:e],
+                func=ACT.Copy, scale=gate_col[:, e - 2:e - 1] if e >= 2 else 1.0,
             )
             return rows
 
@@ -220,8 +219,8 @@ def tile_moe_shf_mlp_silu_kernel(
 
         def scatter(t, e):
             window = routed[t][:].indirect(offsets[:, e * LIST_COLS:(e + 1) * LIST_COLS])
-            if e == 0:
-                nc.vector.tensor_tensor(window, results[t, e], gate_rows[:], ALU.mult)
+            if e < 2:
+                nc.vector.tensor_tensor(window, results[t, e], gate_rows[:, e * C:(e + 1) * C], ALU.mult)
             else:
                 nc.vector.tensor_copy(window, results[t, e])
 
@@ -257,7 +256,7 @@ def tile_moe_shf_mlp_silu_kernel(
         rows1 = expert_sums(1, 1)
         gather_words(3, 4)
         expert_quantise(1, rows1, 3)
-        warm(2, "warm1", 2)
+        warm(0, "warm1", 2)
         expert_second_dealt(w2_dealt, w2_plane_dealt, (4, 5))
         rows2 = expert_sums(2, 6)
         rows3 = expert_sums(3, 7)
@@ -269,29 +268,31 @@ def tile_moe_shf_mlp_silu_kernel(
             routed[t] = tile("routed%d" % t, T, F32, tag)
         for t in range(PACK):
             scatter(t, 0)
-        w2s_dealt = deal(nc.gpsimd, "w2s_dealt", w2s[:], I32, "y0_1")
-        w2s_plane_dealt = deal(nc.gpsimd, "w2s_plane_dealt", w2s_plane[:], U8, "w2s")
         leave_bank("y1", turn_results(1, y_rows1, 3), 1, 0, PACK)
         for t in range(PACK):
             scatter(t, 1)
+        w2s_dealt = deal(nc.gpsimd, "w2s_dealt", w2s[:], I32, "y1")
+        w2s_plane_dealt = deal(nc.gpsimd, "w2s_plane_dealt", w2s_plane[:], U8, "w2s")
         y_rows2 = expert_second_rows(2, 4)
         hs_rows0 = shared_sums(0, 5)
-        leave_bank("y2", turn_results(2, y_rows2, 6), 2, 0, PACK)
-        for t in range(PACK):
+        turned2 = turn_results(2, y_rows2, 6)
+        leave_bank("y2", turned2, 2, 0, LAST)
+        for t in range(LAST):
             scatter(t, 2)
         hs_rows1 = shared_sums(1, 7)
         shared_turn(0, hs_rows0, 0)
         hs_rows2 = shared_sums(2, 1)
         shared_turn(1, hs_rows1, 2)
-        y_rows3 = expert_second_rows(3, 7)
         hs_rows3 = shared_sums(3, 3)
+        y_rows3 = expert_second_rows(3, 1)
         shared_turn(2, hs_rows2, 4)
-        turned3 = turn_results(3, y_rows3, 1)
         shared_turn(3, hs_rows3, 5)
         hs_codes = tile("hs_codes", T, U32)
         hs_plane = tile("hs_plane", T, U8)
         nc.vector.quantize_mx(out=hs_codes[:].bitcast(FP8X4), scales=hs_plane[:], in_=hs_grouped[:])
-        leave_bank("y3", turned3, 3, 0, PACK, "hs3_rows")
+        leave_bank("y2_last", turned2, 2, LAST, PACK, "hs3_rows")
+        scatter(LAST, 2)
+        leave_bank("y3", turn_results(3, y_rows3, 3), 3, 0, PACK)
         for t in range(PACK):
             scatter(t, 3)
 
@@ -311,22 +312,23 @@ def tile_moe_shf_mlp_silu_kernel(
             nc.scalar.copy(out=shared[:], in_=ys[t][:])
             nc.gpsimd.tensor_tensor(total[:, t * T:(t + 1) * T], shared[:], routed[t][:], ALU.add)
             nc.sync.dma_start(out=out_rows[:, t, :], in_=total[:, t * T:(t + 1) * T])
-        half = T // 2
-        for first in (half, 0):
+        half, quarter = T // 2, T // 4
+        for first, width in ((half, half), (0, quarter), (quarter, quarter)):
             for t in (2, 3):
-                nc.vector.tensor_tensor(total[:, t * T + first:t * T + first + half], ys[t][:, first:first + half],
-                                        routed[t][:, first:first + half], ALU.add)
+                nc.vector.tensor_tensor(total[:, t * T + first:t * T + first + width], ys[t][:, first:first + width],
+                                        routed[t][:, first:first + width], ALU.add)
         nc.sync.dma_start(out=out_rows[:, LAST - 1:PACK, :],
                           in_=total[:, (LAST - 1) * T:PACK * T].rearrange("p (t c) -> p t c", t=2))
-
         out_grouped = [tile("out_grouped%d" % i, PACK * half, BF16) for i in range(2)]
         by_token = total[:].rearrange("p (t c) -> p c t", t=PACK)
         nc.scalar.copy(out=out_grouped[1][:].rearrange("p (c t) -> p c t", t=PACK), in_=by_token[:, half:T, :])
-        nc.vector.tensor_copy(out_grouped[0][:].rearrange("p (c t) -> p c t", t=PACK), by_token[:, 0:half, :])
+        for first in (0, quarter):
+            nc.vector.tensor_copy(out_grouped[0][:].rearrange("p (c t) -> p c t", t=PACK)[:, first:first + quarter, :],
+                                  by_token[:, first:first + quarter, :])
         out_codes = tile("out_codes", T, U32)
         out_plane = tile("out_plane", T, U8)
         words_out = out_1[0].rearrange("p c d -> p (c d)").bitcast(I32)
-        for i in range(2):
+        for i in (1, 0):
             cols = slice(i * half, (i + 1) * half)
             nc.vector.quantize_mx(out=out_codes[:, cols].bitcast(FP8X4), scales=out_plane[:, cols], in_=out_grouped[i][:])
             nc.sync.dma_start(out=words_out[:, cols], in_=out_codes[:, cols].bitcast(I32))

@@ -23,7 +23,7 @@ PASSES = K // (P * PACK)
 LIST_COLS = C // 16
 PLANE = 512
 FP4_ROW = 2 * PLANE
-PLACED = {"h_grouped0": 512, "slot_words3_0": 0, "h_codes1": 1024}
+PLACED = {"h_grouped0": 768, "slot_words3_0": 0, "slot_words2_1": 1536, "h_codes1": 1024}
 YS_BANKS = (6, 7, 0, 2)
 LAST = PACK - 1
 
@@ -84,7 +84,9 @@ def tile_moe_shf_mlp_silu_kernel(
         x_tok = [tile("x_tok%d" % s, T, I32) for s in range(PASSES)]
         w1 = [tile("w1_%d" % e, PASSES * FP4_ROW, U8) for e in range(E)]
         w2_first = tile("w2_0", FP4_ROW, U8)
-        w2_last = tile("w2_last", (E - 1) * FP4_ROW, U8)
+        w2_second = tile("w2_1", FP4_ROW, U8)
+        w2_last = tile("w2_last", 2 * FP4_ROW, U8)
+        w2 = [w2_first[:], w2_second[:], w2_last[:, 0:FP4_ROW], w2_last[:, FP4_ROW:]]
         w1s = tile("w1s", PASSES * H, I32)
         w2s = tile("w2s", N, I32)
         gate_col = tile("gate_col", 2, F32)
@@ -104,7 +106,8 @@ def tile_moe_shf_mlp_silu_kernel(
         load_fp4(w1[2], w1_words[2])
         load_planes(w1_planes[1], w1_scales[2:4].rearrange("e s b c -> (e s) b c"))
         load_fp4(w1[3], w1_words[3])
-        load_fp4(w2_last, w2_words[1:E, 0])
+        load_fp4(w2_second, w2_words[1])
+        load_fp4(w2_last, w2_words[2:E, 0])
         nc.sync.dma_start(out=w1s[:].rearrange("p (s c) -> p s c", s=PASSES),
                           in_=w1s_words.rearrange("s p c d -> p s (c d)").bitcast(I32))
         load_planes(w1s_plane, w1s_scales)
@@ -199,7 +202,7 @@ def tile_moe_shf_mlp_silu_kernel(
         def expert_second_rows(e, acc_bank):
             acc = bank(acc_bank, "y_acc%d" % e)
             nc.tensor.matmul_mx(out=acc[:], lhsT=h_codes[e][:].bitcast(FP8X4), lhsT_scale=h_plane[e][:],
-                                rhs=w2_last[:, (e - 1) * FP4_ROW:e * FP4_ROW].bitcast(FP4X4),
+                                rhs=w2[e].bitcast(FP4X4),
                                 rhs_scale=w2_plane[:, e * N:(e + 1) * N], start=True, stop=True)
             rows = tile("y_rows%d" % e, N, F32)
             nc.scalar.activation(
@@ -249,11 +252,12 @@ def tile_moe_shf_mlp_silu_kernel(
         gather_bytes(2, 4)
         warm(7, "warm0", 2)
         rows0 = expert_sums(0, 0, 2)
-        gather_words(2, 3, "slot_words0_0")
+        gather_words(2, 3, "slot_words0_0", (0,))
         w2_plane_dealt = deal(nc.vector, "w2_plane_dealt", w2_plane[:, 0:N], U8)
         w2_dealt = deal(nc.vector, "w2_dealt", w2_first[:], U16)
         expert_quantise(0, rows0, 2, "w2_0")
         rows1 = expert_sums(1, 1)
+        gather_words(2, 3, None, (1,))
         gather_words(3, 4)
         expert_quantise(1, rows1, 3)
         warm(0, "warm1", 2)
@@ -311,7 +315,7 @@ def tile_moe_shf_mlp_silu_kernel(
             shared = tile("shared%d" % t, T, F32)
             nc.scalar.copy(out=shared[:], in_=ys[t][:])
             nc.gpsimd.tensor_tensor(total[:, t * T:(t + 1) * T], shared[:], routed[t][:], ALU.add)
-            nc.sync.dma_start(out=out_rows[:, t, :], in_=total[:, t * T:(t + 1) * T])
+            (nc.scalar if t else nc.sync).dma_start(out=out_rows[:, t, :], in_=total[:, t * T:(t + 1) * T])
         half, quarter = T // 2, T // 4
         for first, width in ((half, half), (0, quarter), (quarter, quarter)):
             for t in (2, 3):

@@ -23,7 +23,7 @@ PASSES = K // (P * PACK)
 LIST_COLS = C // 16
 PLANE = 512
 FP4_ROW = 2 * PLANE
-PLACED = {"h_grouped0": 768, "slot_words3_0": 0, "slot_words2_1": 1536, "h_codes1": 1024}
+PLACED = {"w2_0": 768, "slot_words3_0": 0, "slot_words2_1": 1024, "h_codes0": 1536}
 YS_BANKS = (6, 7, 0, 2)
 LAST = PACK - 1
 
@@ -156,6 +156,24 @@ def tile_moe_shf_mlp_silu_kernel(
                 )
             return rows
 
+        def first_sums_by_groups(banks):
+            rows = tile("h0_rows", H, BF16)
+            width = H // len(banks)
+            for g, acc_bank in enumerate(banks):
+                acc = bank(acc_bank, "h0_acc%d" % g)
+                for s in range(PASSES):
+                    nc.tensor.matmul_mx(
+                        out=acc[:, 0:width], lhsT=slot_words[0, s].bitcast(FP8X4), lhsT_scale=slot_bytes[0, s],
+                        rhs=w1[0][:, s * FP4_ROW + 2 * g * width:s * FP4_ROW + 2 * (g + 1) * width].bitcast(FP4X4),
+                        rhs_scale=w1_planes[0][:, s * H + g * width:s * H + (g + 1) * width],
+                        start=(s == 0), stop=(s == PASSES - 1))
+                nc.scalar.activation(
+                    out=rows[:].rearrange("c (u p b) -> c u p b", u=2, b=2)[:, :, g * width // 4:(g + 1) * width // 4, :],
+                    in_=acc[:, 0:width].rearrange("c (p u b) -> c u p b", u=2, b=2),
+                    func=ACT.Silu,
+                )
+            return rows
+
         def turn_hidden(name, rows, turn_bank, grouped):
             turned = bank(turn_bank, name + "_turned")
             for u in range(2):
@@ -251,7 +269,7 @@ def tile_moe_shf_mlp_silu_kernel(
         gather_bytes(1, 2)
         gather_bytes(2, 4)
         warm(7, "warm0", 2)
-        rows0 = expert_sums(0, 0, 2)
+        rows0 = first_sums_by_groups((4, 5, 6, 0))
         gather_words(2, 3, "slot_words0_0", (0,))
         w2_plane_dealt = deal(nc.vector, "w2_plane_dealt", w2_plane[:, 0:N], U8)
         w2_dealt = deal(nc.vector, "w2_dealt", w2_first[:], U16)
@@ -259,7 +277,7 @@ def tile_moe_shf_mlp_silu_kernel(
         rows1 = expert_sums(1, 1)
         gather_words(2, 3, None, (1,))
         gather_words(3, 4)
-        expert_quantise(1, rows1, 3)
+        expert_quantise(1, rows1, 3, "h_grouped0")
         warm(0, "warm1", 2)
         expert_second_dealt(w2_dealt, w2_plane_dealt, (4, 5))
         rows2 = expert_sums(2, 6)

@@ -23,9 +23,10 @@ PASSES = K // (P * PACK)
 LIST_COLS = C // 16
 PLANE = 512
 FP4_ROW = 2 * PLANE
-PLACED = {"w2_0": 768, "slot_words3_0": 0, "slot_words2_1": 1024, "h_codes0": 1536}
-YS_BANKS = (6, 7, 0, 2)
+GATED_IN_SCATTER = 2
+ADDED_BY_GPSIMD = 2
 LAST = PACK - 1
+PLACED = {"w2_0": 768, "slot_words3_0": 0, "slot_words2_1": 1024, "h_codes0": 1536}
 
 
 def tile_moe_shf_mlp_silu_kernel(
@@ -47,11 +48,9 @@ def tile_moe_shf_mlp_silu_kernel(
             return ps.tile([P, PLANE], F32, name=name, tag="bank%d" % index)
 
 
-        def zero_planes(name, planes, engines):
+        def zero_planes(name, planes):
             zeroed = tile(name, planes * PLANE, U8)
-            share = planes * PLANE // len(engines)
-            for i, engine in enumerate(engines):
-                engine.memset(zeroed[:, i * share:(i + 1) * share].bitcast(I32), 0)
+            nc.vector.memset(zeroed[:].bitcast(I32), 0)
             return zeroed
 
         def load_planes(dst, rows, loads=range(4)):
@@ -70,11 +69,11 @@ def tile_moe_shf_mlp_silu_kernel(
                 in_=words.rearrange("g p b -> p g b").bitcast(I32),
             )
 
-        x_plane = zero_planes("x_plane", PASSES, (nc.vector,))
-        w1_planes = [zero_planes("w1_plane%d" % i, 2 * PASSES, (nc.vector,)) for i in range(2)]
-        w2_plane = zero_planes("w2_plane", E, (nc.vector,))
-        w1s_plane = zero_planes("w1s_plane", PASSES, (nc.vector,))
-        w2s_plane = zero_planes("w2s_plane", 1, (nc.vector,))
+        x_plane = zero_planes("x_plane", PASSES)
+        w1_planes = [zero_planes("w1_plane%d" % i, 2 * PASSES) for i in range(2)]
+        w2_plane = zero_planes("w2_plane", E)
+        w1s_plane = zero_planes("w1s_plane", PASSES)
+        w2s_plane = zero_planes("w2s_plane", 1)
 
         ident = tile("ident", P, F32)
         nc.vector.memset(ident[:], 0.0)
@@ -89,8 +88,8 @@ def tile_moe_shf_mlp_silu_kernel(
         w2 = [w2_first[:], w2_second[:], w2_last[:, 0:FP4_ROW], w2_last[:, FP4_ROW:]]
         w1s = tile("w1s", PASSES * H, I32)
         w2s = tile("w2s", N, I32)
-        gate_col = tile("gate_col", 2, F32)
-        gate_rows = tile("gate_rows", 2 * C, F32)
+        gate_col = tile("gate_col", E - GATED_IN_SCATTER, F32)
+        gate_rows = tile("gate_rows", GATED_IN_SCATTER * C, F32)
 
         nc.sync.dma_start(offsets[:], offs)
         load_fp8(x_tok[0], x_words[0])
@@ -102,7 +101,7 @@ def tile_moe_shf_mlp_silu_kernel(
         load_fp4(w1[1], w1_words[1])
         load_planes(w2_plane, w2_scales.rearrange("e s b c -> (e s) b c"))
         load_fp4(w2_first, w2_words[0])
-        nc.sync.dma_start(out=gate_rows[:], in_=gate[:, 0:2 * C])
+        nc.sync.dma_start(out=gate_rows[:], in_=gate[:, 0:GATED_IN_SCATTER * C])
         load_fp4(w1[2], w1_words[2])
         load_planes(w1_planes[1], w1_scales[2:4].rearrange("e s b c -> (e s) b c"))
         load_fp4(w1[3], w1_words[3])
@@ -112,14 +111,15 @@ def tile_moe_shf_mlp_silu_kernel(
                           in_=w1s_words.rearrange("s p c d -> p s (c d)").bitcast(I32))
         load_planes(w1s_plane, w1s_scales)
         with nc.allow_non_contiguous_dma(reason="one gate value a partition; all rows of gate are equal"):
-            nc.sync.dma_start(out=gate_col[:], in_=gate[0, 2 * C:].rearrange("(e u) -> u e", e=2))
+            nc.sync.dma_start(out=gate_col[:],
+                              in_=gate[0, GATED_IN_SCATTER * C:].rearrange("(e u) -> u e", e=E - GATED_IN_SCATTER))
         load_fp8(w2s, w2s_words[0])
         load_planes(w2s_plane, w2s_scales)
 
 
         slot_words, slot_bytes = {}, {}
 
-        def gather(name, dtype, windows, into, first, last, tag, passes):
+        def gather(name, dtype, windows, into, first, last, passes, tag):
             width = (last - first) * C
             gathered = tile("%s%d_%d" % (name, first, passes[0]), len(passes) * width, dtype, tag)
             entries = offsets[:, first * LIST_COLS:last * LIST_COLS]
@@ -128,11 +128,12 @@ def tile_moe_shf_mlp_silu_kernel(
                 for e in range(first, last):
                     into[e, s] = gathered[:, i * width + (e - first) * C:i * width + (e - first + 1) * C]
 
-        def gather_words(first, last, tag=None, passes=(0, 1)):
-            gather("slot_words", U32, [x_tok[s][:].bitcast(U32) for s in range(PASSES)], slot_words, first, last, tag, passes)
+        def gather_words(e, passes=range(PASSES), tag=None):
+            gather("slot_words", U32, [x_tok[s][:].bitcast(U32) for s in range(PASSES)], slot_words, e, e + 1, passes, tag)
 
         def gather_bytes(first, last):
-            gather("slot_bytes", U8, [x_plane[:, s * T:(s + 1) * T] for s in range(PASSES)], slot_bytes, first, last, None, (0, 1))
+            gather("slot_bytes", U8, [x_plane[:, s * T:(s + 1) * T] for s in range(PASSES)], slot_bytes, first, last,
+                   range(PASSES), None)
 
         def deal(engine, name, source, dtype, tag=None):
             dealt = tile(name, source.shape[1], source.dtype, tag)
@@ -140,26 +141,27 @@ def tile_moe_shf_mlp_silu_kernel(
                                source.bitcast(dtype).rearrange("p (m t) -> p t m", t=PACK))
             return dealt
 
-        def first_sums(name, acc_bank, codes, codes_plane, weights, weights_plane, fmt, parts=1):
+        def silu_sorted(rows, acc, first, width):
+            nc.scalar.activation(
+                out=rows[:].rearrange("c (u p b) -> c u p b", u=2, b=2)[:, :, first // PACK:(first + width) // PACK, :],
+                in_=acc[:, 0:width].rearrange("c (p u b) -> c u p b", u=2, b=2),
+                func=ACT.Silu,
+            )
+
+        def first_layer(name, acc_bank, codes, codes_plane, weights, weights_plane, fmt):
             acc = bank(acc_bank, name + "_acc")
             for s in range(PASSES):
                 nc.tensor.matmul_mx(out=acc[:], lhsT=codes[s].bitcast(FP8X4), lhsT_scale=codes_plane[s],
                                     rhs=weights[s].bitcast(fmt), rhs_scale=weights_plane[s],
                                     start=(s == 0), stop=(s == PASSES - 1))
             rows = tile(name + "_rows", H, BF16)
-            step = 2 // parts
-            for u in range(0, 2, step):
-                nc.scalar.activation(
-                    out=rows[:].rearrange("c (u p b) -> c u p b", u=2, b=2)[:, u:u + step],
-                    in_=acc[:].rearrange("c (p u b) -> c u p b", u=2, b=2)[:, u:u + step],
-                    func=ACT.Silu,
-                )
+            silu_sorted(rows, acc, 0, H)
             return rows
 
-        def first_sums_by_groups(banks):
+        def expert_first_in_groups(acc_banks):
             rows = tile("h0_rows", H, BF16)
-            width = H // len(banks)
-            for g, acc_bank in enumerate(banks):
+            width = H // len(acc_banks)
+            for g, acc_bank in enumerate(acc_banks):
                 acc = bank(acc_bank, "h0_acc%d" % g)
                 for s in range(PASSES):
                     nc.tensor.matmul_mx(
@@ -167,11 +169,7 @@ def tile_moe_shf_mlp_silu_kernel(
                         rhs=w1[0][:, s * FP4_ROW + 2 * g * width:s * FP4_ROW + 2 * (g + 1) * width].bitcast(FP4X4),
                         rhs_scale=w1_planes[0][:, s * H + g * width:s * H + (g + 1) * width],
                         start=(s == 0), stop=(s == PASSES - 1))
-                nc.scalar.activation(
-                    out=rows[:].rearrange("c (u p b) -> c u p b", u=2, b=2)[:, :, g * width // 4:(g + 1) * width // 4, :],
-                    in_=acc[:, 0:width].rearrange("c (p u b) -> c u p b", u=2, b=2),
-                    func=ACT.Silu,
-                )
+                silu_sorted(rows, acc, g * width, width)
             return rows
 
         def turn_hidden(name, rows, turn_bank, grouped):
@@ -183,12 +181,12 @@ def tile_moe_shf_mlp_silu_kernel(
                 in_=turned[:, 0:2 * P].rearrange("p (u c) -> p c u", u=2),
             )
 
-        def expert_sums(e, acc_bank, parts=1):
-            return first_sums(
+        def expert_first(e, acc_bank):
+            return first_layer(
                 "h%d" % e, acc_bank, [slot_words[e, s] for s in range(PASSES)], [slot_bytes[e, s] for s in range(PASSES)],
                 [w1[e][:, s * FP4_ROW:(s + 1) * FP4_ROW] for s in range(PASSES)],
                 [w1_planes[e // 2][:, (e % 2 * PASSES + s) * H:(e % 2 * PASSES + s + 1) * H] for s in range(PASSES)],
-                FP4X4, parts)
+                FP4X4)
 
         h_codes, h_plane = {}, {}
 
@@ -207,8 +205,8 @@ def tile_moe_shf_mlp_silu_kernel(
             for t in range(first, last):
                 results[t, e] = part[:, (t - first) * C:(t - first + 1) * C]
 
-        def expert_second_dealt(codes, plane, banks):
-            for first, last, acc_bank in ((0, 1, banks[0]), (1, PACK, banks[1])):
+        def expert_second_dealt(codes, plane, acc_banks):
+            for first, last, acc_bank in ((0, 1, acc_banks[0]), (1, PACK, acc_banks[1])):
                 acc = bank(acc_bank, "y_acc0_%d" % first)
                 for t in range(first, last):
                     nc.tensor.matmul_mx(
@@ -223,10 +221,11 @@ def tile_moe_shf_mlp_silu_kernel(
                                 rhs=w2[e].bitcast(FP4X4),
                                 rhs_scale=w2_plane[:, e * N:(e + 1) * N], start=True, stop=True)
             rows = tile("y_rows%d" % e, N, F32)
+            col = e - GATED_IN_SCATTER
             nc.scalar.activation(
                 out=rows[:].rearrange("c (t p) -> c t p", t=PACK),
                 in_=acc[:].rearrange("c (p t) -> c t p", t=PACK),
-                func=ACT.Copy, scale=gate_col[:, e - 2:e - 1] if e >= 2 else 1.0,
+                func=ACT.Copy, scale=gate_col[:, col:col + 1] if col >= 0 else 1.0,
             )
             return rows
 
@@ -240,72 +239,77 @@ def tile_moe_shf_mlp_silu_kernel(
 
         def scatter(t, e):
             window = routed[t][:].indirect(offsets[:, e * LIST_COLS:(e + 1) * LIST_COLS])
-            if e < 2:
+            if e < GATED_IN_SCATTER:
                 nc.vector.tensor_tensor(window, results[t, e], gate_rows[:, e * C:(e + 1) * C], ALU.mult)
             else:
                 nc.vector.tensor_copy(window, results[t, e])
 
         hs_grouped = tile("hs_grouped", PACK * T, BF16)
 
-        def shared_sums(b, acc_bank):
-            return first_sums(
-                "hs%d" % b, acc_bank, [x_tok[s][:, b * P:(b + 1) * P] for s in range(PASSES)],
-                [x_plane[:, s * T + b * P:s * T + (b + 1) * P] for s in range(PASSES)],
+        def shared_first(part, acc_bank):
+            return first_layer(
+                "hs%d" % part, acc_bank, [x_tok[s][:, part * P:(part + 1) * P] for s in range(PASSES)],
+                [x_plane[:, s * T + part * P:s * T + (part + 1) * P] for s in range(PASSES)],
                 [w1s[:, s * H:(s + 1) * H] for s in range(PASSES)],
                 [w1s_plane[:, s * H:(s + 1) * H] for s in range(PASSES)], FP8X4)
 
-        def shared_turn(b, rows, turn_bank):
-            turn_hidden("hs%d" % b, rows, turn_bank, hs_grouped[:, b * PACK * P:(b + 1) * PACK * P])
+        def shared_turn(part, rows, turn_bank):
+            turn_hidden("hs%d" % part, rows, turn_bank, hs_grouped[:, part * PACK * P:(part + 1) * PACK * P])
 
-        def warm(acc_bank, name, passes):
+        def warm_up(acc_bank, name, passes):
             acc = bank(acc_bank, name)
             for i in range(passes):
                 nc.tensor.matmul_mx(out=acc[:], lhsT=x_tok[0][:, 0:P].bitcast(FP8X4), lhsT_scale=x_plane[:, 0:P],
                                     rhs=x_tok[0][:].bitcast(FP8X4), rhs_scale=x_plane[:, 0:T], start=True, stop=True)
 
-        gather_words(0, 1)
-        gather_words(1, 2)
+
+        gather_words(0)
+        gather_words(1)
         gather_bytes(0, 1)
         gather_bytes(1, 2)
-        gather_bytes(2, 4)
-        warm(7, "warm0", 2)
-        rows0 = first_sums_by_groups((4, 5, 6, 0))
-        gather_words(2, 3, "slot_words0_0", (0,))
+        gather_bytes(2, E)
+        warm_up(7, "warm0", 2)
+        rows0 = expert_first_in_groups((4, 5, 6, 0))
+        gather_words(2, (0,), "slot_words0_0")
         w2_plane_dealt = deal(nc.vector, "w2_plane_dealt", w2_plane[:, 0:N], U8)
         w2_dealt = deal(nc.vector, "w2_dealt", w2_first[:], U16)
-        expert_quantise(0, rows0, 2, "w2_0")
-        rows1 = expert_sums(1, 1)
-        gather_words(2, 3, None, (1,))
-        gather_words(3, 4)
+        expert_quantise(0, rows0, 2)
+        rows1 = expert_first(1, 1)
+        gather_words(2, (1,))
+        gather_words(3)
         expert_quantise(1, rows1, 3, "h_grouped0")
-        warm(0, "warm1", 2)
+        warm_up(0, "warm1", 2)
         expert_second_dealt(w2_dealt, w2_plane_dealt, (4, 5))
-        rows2 = expert_sums(2, 6)
-        rows3 = expert_sums(3, 7)
+
+
+        rows2 = expert_first(2, 6)
+        rows3 = expert_first(3, 7)
         expert_quantise(2, rows2, 0)
         y_rows1 = expert_second_rows(1, 1)
         expert_quantise(3, rows3, 2)
-        warm(7, "warm3", 1)
-        for t, tag in enumerate((None, None, None, "h_grouped2")):
-            routed[t] = tile("routed%d" % t, T, F32, tag)
+        warm_up(7, "warm3", 1)
+        for t in range(PACK):
+            routed[t] = tile("routed%d" % t, T, F32, "h_grouped2" if t == LAST else None)
         for t in range(PACK):
             scatter(t, 0)
         leave_bank("y1", turn_results(1, y_rows1, 3), 1, 0, PACK)
         for t in range(PACK):
             scatter(t, 1)
+
+
         w2s_dealt = deal(nc.gpsimd, "w2s_dealt", w2s[:], I32, "y1")
         w2s_plane_dealt = deal(nc.gpsimd, "w2s_plane_dealt", w2s_plane[:], U8, "w2s")
         y_rows2 = expert_second_rows(2, 4)
-        hs_rows0 = shared_sums(0, 5)
+        hs_rows0 = shared_first(0, 5)
         turned2 = turn_results(2, y_rows2, 6)
         leave_bank("y2", turned2, 2, 0, LAST)
         for t in range(LAST):
             scatter(t, 2)
-        hs_rows1 = shared_sums(1, 7)
+        hs_rows1 = shared_first(1, 7)
         shared_turn(0, hs_rows0, 0)
-        hs_rows2 = shared_sums(2, 1)
+        hs_rows2 = shared_first(2, 1)
         shared_turn(1, hs_rows1, 2)
-        hs_rows3 = shared_sums(3, 3)
+        hs_rows3 = shared_first(3, 3)
         y_rows3 = expert_second_rows(3, 1)
         shared_turn(2, hs_rows2, 4)
         shared_turn(3, hs_rows3, 5)
@@ -319,8 +323,8 @@ def tile_moe_shf_mlp_silu_kernel(
             scatter(t, 3)
 
         ys = []
-        for t in range(PACK):
-            acc = bank(YS_BANKS[t], "ys%d" % t)
+        for t, acc_bank in enumerate((6, 7, 0, 2)):
+            acc = bank(acc_bank, "ys%d" % t)
             nc.tensor.matmul_mx(out=acc[:], lhsT=w2s_dealt[:, t * P:(t + 1) * P].bitcast(FP8X4),
                                 lhsT_scale=w2s_plane_dealt[:, t * P:(t + 1) * P],
                                 rhs=hs_codes[:].bitcast(FP8X4), rhs_scale=hs_plane[:], start=True, stop=True)
@@ -329,31 +333,35 @@ def tile_moe_shf_mlp_silu_kernel(
 
         total = tile("total", PACK * T, F32)
         out_rows = out_0.rearrange("(p t) c -> p t c", t=PACK)
-        for t in range(2):
+        for t, queue in zip(range(ADDED_BY_GPSIMD), (nc.sync, nc.scalar)):
             shared = tile("shared%d" % t, T, F32)
             nc.scalar.copy(out=shared[:], in_=ys[t][:])
             nc.gpsimd.tensor_tensor(total[:, t * T:(t + 1) * T], shared[:], routed[t][:], ALU.add)
-            (nc.scalar if t else nc.sync).dma_start(out=out_rows[:, t, :], in_=total[:, t * T:(t + 1) * T])
+            queue.dma_start(out=out_rows[:, t, :], in_=total[:, t * T:(t + 1) * T])
         half, quarter = T // 2, T // 4
-        for first, width in ((half, half), (0, quarter), (quarter, quarter)):
-            for t in (2, 3):
-                nc.vector.tensor_tensor(total[:, t * T + first:t * T + first + width], ys[t][:, first:first + width],
-                                        routed[t][:, first:first + width], ALU.add)
-        nc.sync.dma_start(out=out_rows[:, LAST - 1:PACK, :],
-                          in_=total[:, (LAST - 1) * T:PACK * T].rearrange("p (t c) -> p t c", t=2))
+        for first in (3 * quarter, 2 * quarter, 0, quarter):
+            for t in range(ADDED_BY_GPSIMD, PACK):
+                nc.vector.tensor_tensor(total[:, t * T + first:t * T + first + quarter], ys[t][:, first:first + quarter],
+                                        routed[t][:, first:first + quarter], ALU.add)
+        nc.sync.dma_start(out=out_rows[:, ADDED_BY_GPSIMD:PACK, :],
+                          in_=total[:, ADDED_BY_GPSIMD * T:].rearrange("p (t c) -> p t c", c=T))
         out_grouped = [tile("out_grouped%d" % i, PACK * half, BF16) for i in range(2)]
         by_token = total[:].rearrange("p (t c) -> p c t", t=PACK)
-        nc.scalar.copy(out=out_grouped[1][:].rearrange("p (c t) -> p c t", t=PACK), in_=by_token[:, half:T, :])
+        for first in (quarter, 0):
+            nc.scalar.copy(out=out_grouped[1][:].rearrange("p (c t) -> p c t", t=PACK)[:, first:first + quarter, :],
+                           in_=by_token[:, half + first:half + first + quarter, :])
         for first in (0, quarter):
             nc.vector.tensor_copy(out_grouped[0][:].rearrange("p (c t) -> p c t", t=PACK)[:, first:first + quarter, :],
                                   by_token[:, first:first + quarter, :])
         out_codes = tile("out_codes", T, U32)
         out_plane = tile("out_plane", T, U8)
         words_out = out_1[0].rearrange("p c d -> p (c d)").bitcast(I32)
-        for i in (1, 0):
-            cols = slice(i * half, (i + 1) * half)
-            nc.vector.quantize_mx(out=out_codes[:, cols].bitcast(FP8X4), scales=out_plane[:, cols], in_=out_grouped[i][:])
-            nc.sync.dma_start(out=words_out[:, cols], in_=out_codes[:, cols].bitcast(I32))
+        for first in (0, 3 * quarter, quarter, 2 * quarter):
+            cols = slice(first, first + quarter)
+            nc.vector.quantize_mx(out=out_codes[:, cols].bitcast(FP8X4), scales=out_plane[:, cols],
+                                  in_=out_grouped[first // half][:, first % half * PACK:(first % half + quarter) * PACK])
+        for first in (0, half):
+            nc.sync.dma_start(out=words_out[:, first:first + half], in_=out_codes[:, first:first + half].bitcast(I32))
         for r in range(4):
             queue = nc.sync if r % 2 else nc.scalar
             queue.dma_start(out=out_2[0, r:16:4, :].bitcast(I32), in_=out_plane[r:P:32, :].bitcast(I32))

@@ -256,19 +256,12 @@ def tile_moe_shf_mlp_silu_kernel(
         def shared_turn(part, rows, turn_bank):
             turn_hidden("hs%d" % part, rows, turn_bank, hs_grouped[:, part * PACK * P:(part + 1) * PACK * P])
 
-        def warm_up(acc_bank, name, passes):
-            acc = bank(acc_bank, name)
-            for i in range(passes):
-                nc.tensor.matmul_mx(out=acc[:], lhsT=x_tok[0][:, 0:P].bitcast(FP8X4), lhsT_scale=x_plane[:, 0:P],
-                                    rhs=x_tok[0][:].bitcast(FP8X4), rhs_scale=x_plane[:, 0:T], start=True, stop=True)
-
 
         gather_words(0)
         gather_words(1)
         gather_bytes(0, 1)
         gather_bytes(1, 2)
         gather_bytes(2, E)
-        warm_up(7, "warm0", 2)
         rows0 = expert_first_in_groups((4, 5, 6, 0))
         gather_words(2, (0,), "slot_words0_0")
         w2_plane_dealt = deal(nc.vector, "w2_plane_dealt", w2_plane[:, 0:N], U8)
@@ -278,7 +271,6 @@ def tile_moe_shf_mlp_silu_kernel(
         gather_words(2, (1,))
         gather_words(3)
         expert_quantise(1, rows1, 3, "h_grouped0")
-        warm_up(0, "warm1", 2)
         expert_second_dealt(w2_dealt, w2_plane_dealt, (4, 5))
 
 
@@ -287,7 +279,6 @@ def tile_moe_shf_mlp_silu_kernel(
         expert_quantise(2, rows2, 0)
         y_rows1 = expert_second_rows(1, 1)
         expert_quantise(3, rows3, 2)
-        warm_up(7, "warm3", 1)
         for t in range(PACK):
             routed[t] = tile("routed%d" % t, T, F32, "h_grouped2" if t == LAST else None)
         for t in range(PACK):

@@ -241,6 +241,8 @@ def tile_moe_shf_mlp_silu_kernel(
             window = routed[t][:].indirect(offsets[:, e * LIST_COLS:(e + 1) * LIST_COLS])
             if e < GATED_IN_SCATTER:
                 nc.vector.tensor_tensor(window, results[t, e], gate_rows[:, e * C:(e + 1) * C], ALU.mult)
+            elif e == E - 1:
+                nc.scalar.activation(window, results[t, e], ACT.Copy)
             else:
                 nc.vector.tensor_copy(window, results[t, e])
 
@@ -313,29 +315,31 @@ def tile_moe_shf_mlp_silu_kernel(
         for t in range(PACK):
             scatter(t, 3)
 
-        ys = []
-        for t, acc_bank in enumerate((6, 7, 0, 2)):
-            acc = bank(acc_bank, "ys%d" % t)
-            nc.tensor.matmul_mx(out=acc[:], lhsT=w2s_dealt[:, t * P:(t + 1) * P].bitcast(FP8X4),
+        ys = {}
+        for t, acc_bank in ((0, 6), (1, 7), (2, 0), (3, 2)):
+            ys[t] = bank(acc_bank, "ys%d" % t)
+            nc.tensor.matmul_mx(out=ys[t][:], lhsT=w2s_dealt[:, t * P:(t + 1) * P].bitcast(FP8X4),
                                 lhsT_scale=w2s_plane_dealt[:, t * P:(t + 1) * P],
                                 rhs=hs_codes[:].bitcast(FP8X4), rhs_scale=hs_plane[:], start=True, stop=True)
-            ys.append(acc)
 
 
         total = tile("total", PACK * T, F32)
         out_rows = out_0.rearrange("(p t) c -> p t c", t=PACK)
-        for t, queue in zip(range(ADDED_BY_GPSIMD), (nc.sync, nc.scalar)):
-            shared = tile("shared%d" % t, T, F32)
-            nc.scalar.copy(out=shared[:], in_=ys[t][:])
-            nc.gpsimd.tensor_tensor(total[:, t * T:(t + 1) * T], shared[:], routed[t][:], ALU.add)
-            queue.dma_start(out=out_rows[:, t, :], in_=total[:, t * T:(t + 1) * T])
         half, quarter = T // 2, T // 4
+
+        def add(t, first, width):
+            nc.vector.tensor_tensor(total[:, t * T + first:t * T + first + width], ys[t][:, first:first + width],
+                                    routed[t][:, first:first + width], ALU.add)
+
+        def store(t):
+            nc.sync.dma_start(out=out_rows[:, t, :], in_=total[:, t * T:(t + 1) * T])
+
+        for t in range(LAST):
+            add(t, 0, T)
+            store(t)
         for first in (3 * quarter, 2 * quarter, 0, quarter):
-            for t in range(ADDED_BY_GPSIMD, PACK):
-                nc.vector.tensor_tensor(total[:, t * T + first:t * T + first + quarter], ys[t][:, first:first + quarter],
-                                        routed[t][:, first:first + quarter], ALU.add)
-        nc.sync.dma_start(out=out_rows[:, ADDED_BY_GPSIMD:PACK, :],
-                          in_=total[:, ADDED_BY_GPSIMD * T:].rearrange("p (t c) -> p t c", c=T))
+            add(LAST, first, quarter)
+        store(LAST)
         out_grouped = [tile("out_grouped%d" % i, PACK * half, BF16) for i in range(2)]
         by_token = total[:].rearrange("p (t c) -> p c t", t=PACK)
         for first in (quarter, 0):

@@ -148,76 +148,61 @@ def tile_moe_shf_mlp_silu_kernel(
                 func=ACT.Silu,
             )
 
-        def first_layer(name, acc_bank, codes, codes_plane, weights, weights_plane, fmt):
-            acc = bank(acc_bank, name + "_acc")
+        def first_product(acc, codes, codes_plane, weights, weights_plane, fmt, cols):
             for s in range(PASSES):
-                nc.tensor.matmul_mx(out=acc[:], lhsT=codes[s].bitcast(FP8X4), lhsT_scale=codes_plane[s],
-                                    rhs=weights[s].bitcast(fmt), rhs_scale=weights_plane[s],
+                nc.tensor.matmul_mx(out=acc, lhsT=codes[s].bitcast(FP8X4), lhsT_scale=codes_plane[s],
+                                    rhs=weights[s][:, cols].bitcast(fmt), rhs_scale=weights_plane[s][:, cols],
                                     start=(s == 0), stop=(s == PASSES - 1))
-            rows = tile(name + "_rows", H, BF16)
-            silu_sorted(rows, acc, 0, H)
-            return rows
 
-        def expert_first_in_groups(acc_banks):
-            rows = tile("h0_rows", H, BF16)
-            width = H // len(acc_banks)
-            for g, acc_bank in enumerate(acc_banks):
-                acc = bank(acc_bank, "h0_acc%d" % g)
-                for s in range(PASSES):
-                    nc.tensor.matmul_mx(
-                        out=acc[:, 0:width], lhsT=slot_words[0, s].bitcast(FP8X4), lhsT_scale=slot_bytes[0, s],
-                        rhs=w1[0][:, s * FP4_ROW + 2 * g * width:s * FP4_ROW + 2 * (g + 1) * width].bitcast(FP4X4),
-                        rhs_scale=w1_planes[0][:, s * H + g * width:s * H + (g + 1) * width],
-                        start=(s == 0), stop=(s == PASSES - 1))
-                silu_sorted(rows, acc, g * width, width)
-            return rows
-
-        def turn_hidden(name, rows, turn_bank, grouped):
-            turned = bank(turn_bank, name + "_turned")
-            for u in range(2):
-                nc.tensor.transpose(turned[:, u * P:(u + 1) * P], rows[:].bitcast(F32)[:, u * P:(u + 1) * P], ident[:])
-            nc.scalar.copy(
-                out=grouped.bitcast(F32).rearrange("p (c u) -> p c u", u=2),
-                in_=turned[:, 0:2 * P].rearrange("p (u c) -> p c u", u=2),
-            )
-
-        def expert_first(e, acc_bank):
-            return first_layer(
-                "h%d" % e, acc_bank, [slot_words[e, s] for s in range(PASSES)], [slot_bytes[e, s] for s in range(PASSES)],
-                [w1[e][:, s * FP4_ROW:(s + 1) * FP4_ROW] for s in range(PASSES)],
+        def expert_first(e, acc, first):
+            first_product(
+                acc, [slot_words[e, s] for s in range(PASSES)], [slot_bytes[e, s] for s in range(PASSES)],
+                [w1[e][:].bitcast(U16)[:, s * H:(s + 1) * H] for s in range(PASSES)],
                 [w1_planes[e // 2][:, (e % 2 * PASSES + s) * H:(e % 2 * PASSES + s + 1) * H] for s in range(PASSES)],
-                FP4X4)
+                FP4X4, slice(first, first + acc.shape[1]))
+
+        def shared_first(part, acc, first):
+            first_product(
+                acc, [x_tok[s][:, part * P:(part + 1) * P] for s in range(PASSES)],
+                [x_plane[:, s * T + part * P:s * T + (part + 1) * P] for s in range(PASSES)],
+                [w1s[:, s * H:(s + 1) * H] for s in range(PASSES)],
+                [w1s_plane[:, s * H:(s + 1) * H] for s in range(PASSES)], FP8X4, slice(first, first + acc.shape[1]))
+
+        def silu(rows, acc, first):
+            silu_sorted(rows, acc, first, acc.shape[1])
+
+        def turn_hidden(turned, parts):
+            for i, rows in enumerate(parts):
+                for u in range(2):
+                    nc.tensor.transpose(turned[:, (2 * i + u) * P:(2 * i + u + 1) * P],
+                                        rows[:].bitcast(F32)[:, u * P:(u + 1) * P], ident[:])
+
+        def group_hidden(grouped, turned):
+            nc.scalar.copy(out=grouped.bitcast(F32).rearrange("p (i c u) -> p i c u", c=P, u=2),
+                           in_=turned.rearrange("p (i u c) -> p i c u", c=P, u=2))
 
         h_codes, h_plane = {}, {}
 
-        def expert_quantise(e, rows, turn_bank, codes_tag=None):
-            grouped = tile("h_grouped%d" % e, PACK * C, BF16)
-            turn_hidden("h%d" % e, rows, turn_bank, grouped[:])
-            h_codes[e] = tile("h_codes%d" % e, C, U32, codes_tag)
-            h_plane[e] = tile("h_plane%d" % e, C, U8)
-            nc.vector.quantize_mx(out=h_codes[e][:].bitcast(FP8X4), scales=h_plane[e][:], in_=grouped[:])
+        def expert_quantise(first, turned):
+            cols = turned.shape[1] // 2
+            grouped = tile("h_grouped%d" % first, PACK * cols, BF16)
+            group_hidden(grouped[:], turned)
+            codes, plane = tile("h_codes%d" % first, cols, U32), tile("h_plane%d" % first, cols, U8)
+            nc.vector.quantize_mx(out=codes[:].bitcast(FP8X4), scales=plane[:], in_=grouped[:])
+            for i in range(cols // C):
+                h_codes[first + i], h_plane[first + i] = codes[:, i * C:(i + 1) * C], plane[:, i * C:(i + 1) * C]
 
         results = {}
 
-        def leave_bank(name, acc, e, first, last, tag=None):
-            part = tile(name, (last - first) * C, F32, tag)
-            nc.scalar.copy(out=part[:], in_=acc[:, first * C:last * C])
-            for t in range(first, last):
-                results[t, e] = part[:, (t - first) * C:(t - first + 1) * C]
-
-        def expert_second_dealt(codes, plane, acc_banks):
-            for first, last, acc_bank in ((0, 1, acc_banks[0]), (1, PACK, acc_banks[1])):
-                acc = bank(acc_bank, "y_acc0_%d" % first)
-                for t in range(first, last):
-                    nc.tensor.matmul_mx(
-                        out=acc[:, t * C:(t + 1) * C], lhsT=codes[:, 2 * t * P:2 * (t + 1) * P].bitcast(FP4X4),
-                        lhsT_scale=plane[:, t * P:(t + 1) * P],
-                        rhs=h_codes[0][:].bitcast(FP8X4), rhs_scale=h_plane[0][:], start=True, stop=True)
-                leave_bank("y0_%d" % first, acc, 0, first, last)
+        def leave_bank(name, acc, e, first, tag=None):
+            part = tile(name, acc.shape[1], F32, tag)
+            nc.scalar.copy(out=part[:], in_=acc)
+            for i in range(acc.shape[1] // C):
+                results[first + i, e] = part[:, i * C:(i + 1) * C]
 
         def expert_second_rows(e, acc_bank):
             acc = bank(acc_bank, "y_acc%d" % e)
-            nc.tensor.matmul_mx(out=acc[:], lhsT=h_codes[e][:].bitcast(FP8X4), lhsT_scale=h_plane[e][:],
+            nc.tensor.matmul_mx(out=acc[:], lhsT=h_codes[e].bitcast(FP8X4), lhsT_scale=h_plane[e],
                                 rhs=w2[e].bitcast(FP4X4),
                                 rhs_scale=w2_plane[:, e * N:(e + 1) * N], start=True, stop=True)
             rows = tile("y_rows%d" % e, N, F32)
@@ -229,13 +214,11 @@ def tile_moe_shf_mlp_silu_kernel(
             )
             return rows
 
-        def turn_results(e, rows, turn_bank):
-            turned = bank(turn_bank, "y_turned%d" % e)
-            for t in range(PACK):
-                nc.tensor.transpose(turned[:, t * C:(t + 1) * C], rows[:, t * P:(t + 1) * P], ident[:])
-            return turned
+        def turn_results(turned, rows, first):
+            for i in range(turned.shape[1] // C):
+                nc.tensor.transpose(turned[:, i * C:(i + 1) * C], rows[:, (first + i) * P:(first + i + 1) * P], ident[:])
 
-        routed = {}
+        routed = [tile("routed%d" % t, T, F32) for t in range(PACK)]
 
         def scatter(t, e):
             window = routed[t][:].indirect(offsets[:, e * LIST_COLS:(e + 1) * LIST_COLS])
@@ -246,82 +229,113 @@ def tile_moe_shf_mlp_silu_kernel(
             else:
                 nc.vector.tensor_copy(window, results[t, e])
 
+        low, high = slice(0, PLANE // 2), slice(PLANE // 2, PLANE)
+        h_rows = [tile("h_rows%d" % e, H, BF16) for e in range(E)]
+        hs_rows = [tile("hs_rows%d" % part, H, BF16) for part in range(T // P)]
         hs_grouped = tile("hs_grouped", PACK * T, BF16)
-
-        def shared_first(part, acc_bank):
-            return first_layer(
-                "hs%d" % part, acc_bank, [x_tok[s][:, part * P:(part + 1) * P] for s in range(PASSES)],
-                [x_plane[:, s * T + part * P:s * T + (part + 1) * P] for s in range(PASSES)],
-                [w1s[:, s * H:(s + 1) * H] for s in range(PASSES)],
-                [w1s_plane[:, s * H:(s + 1) * H] for s in range(PASSES)], FP8X4)
-
-        def shared_turn(part, rows, turn_bank):
-            turn_hidden("hs%d" % part, rows, turn_bank, hs_grouped[:, part * PACK * P:(part + 1) * PACK * P])
-
 
         gather_words(0)
         gather_words(1)
         gather_bytes(0, 1)
         gather_bytes(1, 2)
         gather_bytes(2, E)
-        rows0 = expert_first_in_groups((4, 5, 6, 0))
+        for g in range(4):
+            acc = bank(g, "h0_acc%d" % g)
+            expert_first(0, acc[:, 0:P], g * P)
+            silu(h_rows[0], acc[:, 0:P], g * P)
         gather_words(2, (0,), "slot_words0_0")
         w2_plane_dealt = deal(nc.vector, "w2_plane_dealt", w2_plane[:, 0:N], U8)
         w2_dealt = deal(nc.vector, "w2_dealt", w2_first[:], U16)
-        expert_quantise(0, rows0, 2)
-        rows1 = expert_first(1, 1)
+
+        bank4 = bank(4, "h1_low")
+        expert_first(1, bank4[:, low], 0)
+        turn_hidden(bank4[:, high], h_rows[0:1])
+        expert_quantise(0, bank4[:, high])
         gather_words(2, (1,))
         gather_words(3)
-        expert_quantise(1, rows1, 3, "h_grouped0")
-        expert_second_dealt(w2_dealt, w2_plane_dealt, (4, 5))
+        silu(h_rows[1], bank4[:, low], 0)
+        bank3 = bank(3, "h1_high")
+        expert_first(1, bank3[:, low], H // 2)
+        silu(h_rows[1], bank3[:, low], H // 2)
 
-
-        rows2 = expert_first(2, 6)
-        rows3 = expert_first(3, 7)
-        expert_quantise(2, rows2, 0)
-        y_rows1 = expert_second_rows(1, 1)
-        expert_quantise(3, rows3, 2)
-        for t in range(PACK):
-            routed[t] = tile("routed%d" % t, T, F32, "h_grouped2" if t == LAST else None)
+        bank1 = bank(1, "y0_outer")
+        bank2 = bank(2, "y0_mid")
+        for t, acc in ((0, bank1[:, 0:C]), (3, bank1[:, C:2 * C]), (1, bank2[:, 0:C]), (2, bank2[:, C:2 * C])):
+            nc.tensor.matmul_mx(out=acc, lhsT=w2_dealt[:, 2 * t * P:2 * (t + 1) * P].bitcast(FP4X4),
+                                lhsT_scale=w2_plane_dealt[:, t * P:(t + 1) * P],
+                                rhs=h_codes[0].bitcast(FP8X4), rhs_scale=h_plane[0], start=True, stop=True)
+        turn_hidden(bank2[:, high], h_rows[1:2])
+        leave_bank("y0_first", bank1[:, 0:C], 0, 0)
+        expert_quantise(1, bank2[:, high])
+        leave_bank("y0_mid", bank2[:, low], 0, 1)
+        leave_bank("y0_last", bank1[:, C:2 * C], 0, LAST, "h_rows1")
+        acc = bank(0, "h2_acc")
+        expert_first(2, acc[:], 0)
+        silu(h_rows[2], acc[:], 0)
+        acc = bank(6, "h3_acc")
+        expert_first(3, acc[:], 0)
+        silu(h_rows[3], acc[:], 0)
+        y_rows1 = expert_second_rows(1, 0)
+        turned = bank(6, "h23_turned")
+        turn_hidden(turned[:], h_rows[2:4])
+        expert_quantise(2, turned[:])
         for t in range(PACK):
             scatter(t, 0)
-        leave_bank("y1", turn_results(1, y_rows1, 3), 1, 0, PACK)
+
+        banks = [bank(3, "hs0_low"), bank(5, "hs0_high")]
+        for i in range(2):
+            shared_first(0, banks[i][:, low], i * H // 2)
+        for i in range(2):
+            turn_results(banks[i][:, high], y_rows1, 2 * i)
+        for i, name in enumerate(("y1_low", "y1")):
+            leave_bank(name, banks[i][:, high], 1, 2 * i)
+            silu(hs_rows[0], banks[i][:, low], i * H // 2)
         for t in range(PACK):
             scatter(t, 1)
-
-
         w2s_dealt = deal(nc.gpsimd, "w2s_dealt", w2s[:], I32, "y1")
         w2s_plane_dealt = deal(nc.gpsimd, "w2s_plane_dealt", w2s_plane[:], U8, "w2s")
-        y_rows2 = expert_second_rows(2, 4)
-        hs_rows0 = shared_first(0, 5)
-        turned2 = turn_results(2, y_rows2, 6)
-        leave_bank("y2", turned2, 2, 0, LAST)
-        for t in range(LAST):
+
+        def shared_whole(part, acc_bank):
+            acc = bank(acc_bank, "hs%d_acc" % part)
+            shared_first(part, acc[:], 0)
+            silu(hs_rows[part], acc[:], 0)
+
+        def shared_turn(first, turn_bank):
+            turned = bank(turn_bank, "hs_turned%d" % first)
+            turn_hidden(turned[:], hs_rows[first:first + 2])
+            group_hidden(hs_grouped[:, first * PACK * P:(first + 2) * PACK * P], turned[:])
+
+        shared_whole(1, 2)
+        y_rows2 = expert_second_rows(2, 3)
+        shared_whole(2, 1)
+        turned2 = bank(0, "y2_turned")
+        turn_results(turned2[:], y_rows2, 0)
+        leave_bank("y2", turned2[:, low], 2, 0)
+        for t in range(2):
             scatter(t, 2)
-        hs_rows1 = shared_first(1, 7)
-        shared_turn(0, hs_rows0, 0)
-        hs_rows2 = shared_first(2, 1)
-        shared_turn(1, hs_rows1, 2)
-        hs_rows3 = shared_first(3, 3)
+        shared_whole(3, 5)
         y_rows3 = expert_second_rows(3, 1)
-        shared_turn(2, hs_rows2, 4)
-        shared_turn(3, hs_rows3, 5)
+        shared_turn(0, 3)
+        shared_turn(2, 5)
         hs_codes = tile("hs_codes", T, U32)
         hs_plane = tile("hs_plane", T, U8)
         nc.vector.quantize_mx(out=hs_codes[:].bitcast(FP8X4), scales=hs_plane[:], in_=hs_grouped[:])
-        leave_bank("y2_last", turned2, 2, LAST, PACK, "hs3_rows")
-        scatter(LAST, 2)
-        leave_bank("y3", turn_results(3, y_rows3, 3), 3, 0, PACK)
+        leave_bank("y2_last", turned2[:, high], 2, 2, "hs_rows3")
+        for t in range(2, PACK):
+            scatter(t, 2)
+        turned = bank(2, "y3_turned")
+        turn_results(turned[:], y_rows3, 0)
+        leave_bank("y3_low", turned[:, low], 3, 0, "hs_rows2")
+        leave_bank("y3_high", turned[:, high], 3, 2, "hs_rows1")
         for t in range(PACK):
             scatter(t, 3)
 
         ys = {}
-        for t, acc_bank in ((0, 6), (1, 7), (2, 0), (3, 2)):
+        for t, acc_bank in enumerate((7, 6, 4, 1)):
             ys[t] = bank(acc_bank, "ys%d" % t)
             nc.tensor.matmul_mx(out=ys[t][:], lhsT=w2s_dealt[:, t * P:(t + 1) * P].bitcast(FP8X4),
                                 lhsT_scale=w2s_plane_dealt[:, t * P:(t + 1) * P],
                                 rhs=hs_codes[:].bitcast(FP8X4), rhs_scale=hs_plane[:], start=True, stop=True)
-
 
         total = tile("total", PACK * T, F32)
         out_rows = out_0.rearrange("(p t) c -> p t c", t=PACK)

@@ -23,10 +23,8 @@ PASSES = K // (P * PACK)
 LIST_COLS = C // 16
 PLANE = 512
 FP4_ROW = 2 * PLANE
-GATED_IN_SCATTER = 2
-ADDED_BY_GPSIMD = 2
 LAST = PACK - 1
-PLACED = {"w2_0": 768, "slot_words3_0": 0, "slot_words2_1": 1024, "h_codes0": 1536}
+PLACED = {"slot_words0_0": 0, "slot_words2_0": 0, "routed3": 0}
 
 
 def tile_moe_shf_mlp_silu_kernel(
@@ -46,7 +44,6 @@ def tile_moe_shf_mlp_silu_kernel(
 
         def bank(index, name):
             return ps.tile([P, PLANE], F32, name=name, tag="bank%d" % index)
-
 
         def zero_planes(name, planes):
             zeroed = tile(name, planes * PLANE, U8)
@@ -82,14 +79,12 @@ def tile_moe_shf_mlp_silu_kernel(
         offsets = sb.tile([P, T // 16], U16, name="offsets")
         x_tok = [tile("x_tok%d" % s, T, I32) for s in range(PASSES)]
         w1 = [tile("w1_%d" % e, PASSES * FP4_ROW, U8) for e in range(E)]
-        w2_first = tile("w2_0", FP4_ROW, U8)
-        w2_second = tile("w2_1", FP4_ROW, U8)
-        w2_last = tile("w2_last", 2 * FP4_ROW, U8)
-        w2 = [w2_first[:], w2_second[:], w2_last[:, 0:FP4_ROW], w2_last[:, FP4_ROW:]]
+        w2_early = tile("w2_early", 2 * FP4_ROW, U8)
+        w2_late = tile("w2_late", 2 * FP4_ROW, U8)
         w1s = tile("w1s", PASSES * H, I32)
         w2s = tile("w2s", N, I32)
-        gate_col = tile("gate_col", E - GATED_IN_SCATTER, F32)
-        gate_rows = tile("gate_rows", GATED_IN_SCATTER * C, F32)
+        gate_first, gate_rest = tile("gate_first", 2 * C, F32), tile("gate_rest", 2 * C, F32)
+        gates = [(gate_first, gate_rest)[e // 2][:, e % 2 * C:(e % 2 + 1) * C] for e in range(E)]
 
         nc.sync.dma_start(offsets[:], offs)
         load_fp8(x_tok[0], x_words[0])
@@ -99,23 +94,19 @@ def tile_moe_shf_mlp_silu_kernel(
         load_fp4(w1[0], w1_words[0])
         load_planes(w1_planes[0], w1_scales[0:2].rearrange("e s b c -> (e s) b c"))
         load_fp4(w1[1], w1_words[1])
+        load_fp4(w2_early, w2_words[0:2, 0])
         load_planes(w2_plane, w2_scales.rearrange("e s b c -> (e s) b c"))
-        load_fp4(w2_first, w2_words[0])
-        nc.sync.dma_start(out=gate_rows[:], in_=gate[:, 0:GATED_IN_SCATTER * C])
         load_fp4(w1[2], w1_words[2])
         load_planes(w1_planes[1], w1_scales[2:4].rearrange("e s b c -> (e s) b c"))
+        nc.sync.dma_start(out=gate_first[:], in_=gate[:, 0:2 * C])
         load_fp4(w1[3], w1_words[3])
-        load_fp4(w2_second, w2_words[1])
-        load_fp4(w2_last, w2_words[2:E, 0])
         nc.sync.dma_start(out=w1s[:].rearrange("p (s c) -> p s c", s=PASSES),
                           in_=w1s_words.rearrange("s p c d -> p s (c d)").bitcast(I32))
         load_planes(w1s_plane, w1s_scales)
-        with nc.allow_non_contiguous_dma(reason="one gate value a partition; all rows of gate are equal"):
-            nc.sync.dma_start(out=gate_col[:],
-                              in_=gate[0, GATED_IN_SCATTER * C:].rearrange("(e u) -> u e", e=E - GATED_IN_SCATTER))
+        load_fp4(w2_late, w2_words[2:4, 0])
+        nc.sync.dma_start(out=gate_rest[:], in_=gate[:, 2 * C:])
         load_fp8(w2s, w2s_words[0])
         load_planes(w2s_plane, w2s_scales)
-
 
         slot_words, slot_bytes = {}, {}
 
@@ -128,48 +119,37 @@ def tile_moe_shf_mlp_silu_kernel(
                 for e in range(first, last):
                     into[e, s] = gathered[:, i * width + (e - first) * C:i * width + (e - first + 1) * C]
 
-        def gather_words(e, passes=range(PASSES), tag=None):
-            gather("slot_words", U32, [x_tok[s][:].bitcast(U32) for s in range(PASSES)], slot_words, e, e + 1, passes, tag)
+        def gather_words(first, last, passes=range(PASSES), tag=None):
+            gather("slot_words", U32, [x_tok[s][:].bitcast(U32) for s in range(PASSES)], slot_words, first, last, passes, tag)
 
-        def gather_bytes(first, last):
+        def gather_bytes(first, last, tag=None):
             gather("slot_bytes", U8, [x_plane[:, s * T:(s + 1) * T] for s in range(PASSES)], slot_bytes, first, last,
-                   range(PASSES), None)
+                   range(PASSES), tag)
 
-        def deal(engine, name, source, dtype, tag=None):
+        def deal(engine, name, source, dtype, tag=None, pieces=1):
             dealt = tile(name, source.shape[1], source.dtype, tag)
-            engine.tensor_copy(dealt[:].bitcast(dtype).rearrange("p (t m) -> p t m", t=PACK),
-                               source.bitcast(dtype).rearrange("p (m t) -> p t m", t=PACK))
+            out = dealt[:].bitcast(dtype).rearrange("p (s t m) -> p s t m", t=PACK, m=P)
+            in_ = source.bitcast(dtype).rearrange("p (s m t) -> p s t m", t=PACK, m=P)
+            step = PACK // pieces
+            for first in range(0, PACK, step):
+                engine.tensor_copy(out[:, :, first:first + step, :], in_[:, :, first:first + step, :])
             return dealt
 
-        def silu_sorted(rows, acc, first, width):
+        def silu_sorted(rows, acc, first):
+            width = acc.shape[1]
             nc.scalar.activation(
                 out=rows[:].rearrange("c (u p b) -> c u p b", u=2, b=2)[:, :, first // PACK:(first + width) // PACK, :],
-                in_=acc[:, 0:width].rearrange("c (p u b) -> c u p b", u=2, b=2),
+                in_=acc.rearrange("c (p u b) -> c u p b", u=2, b=2),
                 func=ACT.Silu,
             )
 
-        def first_product(acc, codes, codes_plane, weights, weights_plane, fmt, cols):
-            for s in range(PASSES):
-                nc.tensor.matmul_mx(out=acc, lhsT=codes[s].bitcast(FP8X4), lhsT_scale=codes_plane[s],
-                                    rhs=weights[s][:, cols].bitcast(fmt), rhs_scale=weights_plane[s][:, cols],
-                                    start=(s == 0), stop=(s == PASSES - 1))
-
         def expert_first(e, acc, first):
-            first_product(
-                acc, [slot_words[e, s] for s in range(PASSES)], [slot_bytes[e, s] for s in range(PASSES)],
-                [w1[e][:].bitcast(U16)[:, s * H:(s + 1) * H] for s in range(PASSES)],
-                [w1_planes[e // 2][:, (e % 2 * PASSES + s) * H:(e % 2 * PASSES + s + 1) * H] for s in range(PASSES)],
-                FP4X4, slice(first, first + acc.shape[1]))
-
-        def shared_first(part, acc, first):
-            first_product(
-                acc, [x_tok[s][:, part * P:(part + 1) * P] for s in range(PASSES)],
-                [x_plane[:, s * T + part * P:s * T + (part + 1) * P] for s in range(PASSES)],
-                [w1s[:, s * H:(s + 1) * H] for s in range(PASSES)],
-                [w1s_plane[:, s * H:(s + 1) * H] for s in range(PASSES)], FP8X4, slice(first, first + acc.shape[1]))
-
-        def silu(rows, acc, first):
-            silu_sorted(rows, acc, first, acc.shape[1])
+            cols = slice(first, first + acc.shape[1])
+            for s in range(PASSES):
+                plane = w1_planes[e // 2][:, (e % 2 * PASSES + s) * H:(e % 2 * PASSES + s + 1) * H]
+                nc.tensor.matmul_mx(out=acc, lhsT=slot_words[e, s].bitcast(FP8X4), lhsT_scale=slot_bytes[e, s],
+                                    rhs=w1[e][:].bitcast(U16)[:, s * H:(s + 1) * H][:, cols].bitcast(FP4X4),
+                                    rhs_scale=plane[:, cols], start=(s == 0), stop=(s == PASSES - 1))
 
         def turn_hidden(turned, parts):
             for i, rows in enumerate(parts):
@@ -177,161 +157,152 @@ def tile_moe_shf_mlp_silu_kernel(
                     nc.tensor.transpose(turned[:, (2 * i + u) * P:(2 * i + u + 1) * P],
                                         rows[:].bitcast(F32)[:, u * P:(u + 1) * P], ident[:])
 
-        def group_hidden(grouped, turned):
-            nc.scalar.copy(out=grouped.bitcast(F32).rearrange("p (i c u) -> p i c u", c=P, u=2),
-                           in_=turned.rearrange("p (i u c) -> p i c u", c=P, u=2))
-
         h_codes, h_plane = {}, {}
 
-        def expert_quantise(first, turned):
+        def expert_quantise(first, turned, tag=None):
             cols = turned.shape[1] // 2
             grouped = tile("h_grouped%d" % first, PACK * cols, BF16)
-            group_hidden(grouped[:], turned)
-            codes, plane = tile("h_codes%d" % first, cols, U32), tile("h_plane%d" % first, cols, U8)
+            nc.scalar.copy(out=grouped[:].bitcast(F32).rearrange("p (i c u) -> p i c u", c=P, u=2),
+                           in_=turned.rearrange("p (i u c) -> p i c u", c=P, u=2))
+            codes, plane = tile("h_codes%d" % first, cols, U32), tile("h_plane%d" % first, cols, U8, tag)
             nc.vector.quantize_mx(out=codes[:].bitcast(FP8X4), scales=plane[:], in_=grouped[:])
             for i in range(cols // C):
                 h_codes[first + i], h_plane[first + i] = codes[:, i * C:(i + 1) * C], plane[:, i * C:(i + 1) * C]
 
-        results = {}
+        gated = tile("gated", PACK * T, F32)
 
-        def leave_bank(name, acc, e, first, tag=None):
-            part = tile(name, acc.shape[1], F32, tag)
-            nc.scalar.copy(out=part[:], in_=acc)
+        def second_product(e, acc, first):
             for i in range(acc.shape[1] // C):
-                results[first + i, e] = part[:, i * C:(i + 1) * C]
+                t = first + i
+                nc.tensor.matmul_mx(out=acc[:, i * C:(i + 1) * C], lhsT=words[e][:, 2 * t * P:2 * (t + 1) * P].bitcast(FP4X4),
+                                    lhsT_scale=planes[e][:, t * P:(t + 1) * P],
+                                    rhs=h_codes[e].bitcast(FP8X4), rhs_scale=h_plane[e], start=True, stop=True)
 
-        def expert_second_rows(e, acc_bank):
-            acc = bank(acc_bank, "y_acc%d" % e)
-            nc.tensor.matmul_mx(out=acc[:], lhsT=h_codes[e].bitcast(FP8X4), lhsT_scale=h_plane[e],
-                                rhs=w2[e].bitcast(FP4X4),
-                                rhs_scale=w2_plane[:, e * N:(e + 1) * N], start=True, stop=True)
-            rows = tile("y_rows%d" % e, N, F32)
-            col = e - GATED_IN_SCATTER
-            nc.scalar.activation(
-                out=rows[:].rearrange("c (t p) -> c t p", t=PACK),
-                in_=acc[:].rearrange("c (p t) -> c t p", t=PACK),
-                func=ACT.Copy, scale=gate_col[:, col:col + 1] if col >= 0 else 1.0,
-            )
-            return rows
+        def gate_results(e, acc, first):
+            count = acc.shape[1] // C
+            nc.vector.tensor_tensor(
+                gated[:].rearrange("p (t j) -> p t j", t=PACK)[:, first:first + count, e * C:(e + 1) * C],
+                acc.rearrange("p (t c) -> p t c", t=count),
+                gates[e].unsqueeze(1).to_broadcast([P, count, C]), ALU.mult)
 
-        def turn_results(turned, rows, first):
-            for i in range(turned.shape[1] // C):
-                nc.tensor.transpose(turned[:, i * C:(i + 1) * C], rows[:, (first + i) * P:(first + i + 1) * P], ident[:])
+        def second_dealt(e, acc):
+            second_product(e, acc[:], 0)
+            gate_results(e, acc[:], 0)
 
-        routed = [tile("routed%d" % t, T, F32) for t in range(PACK)]
+        routed = {}
 
-        def scatter(t, e):
-            window = routed[t][:].indirect(offsets[:, e * LIST_COLS:(e + 1) * LIST_COLS])
-            if e < GATED_IN_SCATTER:
-                nc.vector.tensor_tensor(window, results[t, e], gate_rows[:, e * C:(e + 1) * C], ALU.mult)
-            elif e == E - 1:
-                nc.scalar.activation(window, results[t, e], ACT.Copy)
+        def scatter(t, first, last, on_scalar, tag=None):
+            if t not in routed:
+                routed[t] = tile("routed%d" % t, T, F32, tag)
+            window = routed[t][:].indirect(offsets[:, first * LIST_COLS:last * LIST_COLS])
+            values = gated[:, t * T + first * C:t * T + last * C]
+            if on_scalar:
+                nc.scalar.activation(window, values, ACT.Copy)
             else:
-                nc.vector.tensor_copy(window, results[t, e])
+                nc.vector.tensor_copy(window, values)
 
         low, high = slice(0, PLANE // 2), slice(PLANE // 2, PLANE)
         h_rows = [tile("h_rows%d" % e, H, BF16) for e in range(E)]
         hs_rows = [tile("hs_rows%d" % part, H, BF16) for part in range(T // P)]
         hs_grouped = tile("hs_grouped", PACK * T, BF16)
 
-        gather_words(0)
-        gather_words(1)
+        def shared_product(part, acc, first):
+            cols = slice(part * P, (part + 1) * P)
+            for s in range(PASSES):
+                at = slice(s * H + first, s * H + first + acc.shape[1])
+                nc.tensor.matmul_mx(out=acc, lhsT=x_tok[s][:, cols].bitcast(FP8X4),
+                                    lhsT_scale=x_plane[:, s * T:(s + 1) * T][:, cols],
+                                    rhs=w1s[:, at].bitcast(FP8X4), rhs_scale=w1s_plane[:, at],
+                                    start=(s == 0), stop=(s == PASSES - 1))
+
+        def shared_first(part, acc):
+            shared_product(part, acc[:], 0)
+            silu_sorted(hs_rows[part], acc[:], 0)
+
+        def shared_turn(first, turned):
+            turn_hidden(turned[:], hs_rows[first:first + 2])
+            nc.scalar.copy(
+                out=hs_grouped[:, first * PACK * P:(first + 2) * PACK * P].bitcast(F32).rearrange("p (i c u) -> p i c u", c=P, u=2),
+                in_=turned[:].rearrange("p (i u c) -> p i c u", c=P, u=2))
+
+        gather_words(0, 1)
+        gather_words(1, 2)
         gather_bytes(0, 1)
         gather_bytes(1, 2)
         gather_bytes(2, E)
+        planes = {2: deal(nc.gpsimd, "w2_plane2", w2_plane[:, 2 * N:3 * N], U8)}
         for g in range(4):
             acc = bank(g, "h0_acc%d" % g)
             expert_first(0, acc[:, 0:P], g * P)
-            silu(h_rows[0], acc[:, 0:P], g * P)
-        gather_words(2, (0,), "slot_words0_0")
-        w2_plane_dealt = deal(nc.vector, "w2_plane_dealt", w2_plane[:, 0:N], U8)
-        w2_dealt = deal(nc.vector, "w2_dealt", w2_first[:], U16)
-
+            silu_sorted(h_rows[0], acc[:, 0:P], g * P)
+        gather_words(2, E)
+        dealt = deal(nc.vector, "w2_dealt0", w2_early[:], U16)
+        words = {e: dealt[:, e * FP4_ROW:(e + 1) * FP4_ROW] for e in range(2)}
+        planes[0] = deal(nc.vector, "w2_plane0", w2_plane[:, 0:N], U8)
         bank4 = bank(4, "h1_low")
         expert_first(1, bank4[:, low], 0)
         turn_hidden(bank4[:, high], h_rows[0:1])
         expert_quantise(0, bank4[:, high])
-        gather_words(2, (1,))
-        gather_words(3)
-        silu(h_rows[1], bank4[:, low], 0)
-        bank3 = bank(3, "h1_high")
-        expert_first(1, bank3[:, low], H // 2)
-        silu(h_rows[1], bank3[:, low], H // 2)
-
-        bank1 = bank(1, "y0_outer")
-        bank2 = bank(2, "y0_mid")
-        for t, acc in ((0, bank1[:, 0:C]), (3, bank1[:, C:2 * C]), (1, bank2[:, 0:C]), (2, bank2[:, C:2 * C])):
-            nc.tensor.matmul_mx(out=acc, lhsT=w2_dealt[:, 2 * t * P:2 * (t + 1) * P].bitcast(FP4X4),
-                                lhsT_scale=w2_plane_dealt[:, t * P:(t + 1) * P],
-                                rhs=h_codes[0].bitcast(FP8X4), rhs_scale=h_plane[0], start=True, stop=True)
-        turn_hidden(bank2[:, high], h_rows[1:2])
-        leave_bank("y0_first", bank1[:, 0:C], 0, 0)
-        expert_quantise(1, bank2[:, high])
-        leave_bank("y0_mid", bank2[:, low], 0, 1)
-        leave_bank("y0_last", bank1[:, C:2 * C], 0, LAST, "h_rows1")
-        acc = bank(0, "h2_acc")
-        expert_first(2, acc[:], 0)
-        silu(h_rows[2], acc[:], 0)
-        acc = bank(6, "h3_acc")
+        planes[1] = deal(nc.vector, "w2_plane1", w2_plane[:, N:2 * N], U8, "h_rows0")
+        silu_sorted(h_rows[1], bank4[:, low], 0)
+        acc = bank(0, "h1_high")
+        expert_first(1, acc[:, low], H // 2)
+        silu_sorted(h_rows[1], acc[:, low], H // 2)
+        bank1, bank2, bank5 = bank(1, "h2_mid"), bank(2, "h2_first"), bank(5, "h2_last")
+        expert_first(2, bank2[:, 0:P], 0)
+        silu_sorted(h_rows[2], bank2[:, 0:P], 0)
+        expert_first(2, bank1[:, low], P)
+        expert_first(2, bank5[:, 0:P], 3 * P)
+        silu_sorted(h_rows[2], bank5[:, 0:P], 3 * P)
+        turn_hidden(bank1[:, high], h_rows[1:2])
+        second_dealt(0, bank(2, "y0_acc"))
+        expert_quantise(1, bank1[:, high], "h_plane0")
+        silu_sorted(h_rows[2], bank1[:, low], P)
+        acc = bank(3, "h3_acc")
         expert_first(3, acc[:], 0)
-        silu(h_rows[3], acc[:], 0)
-        y_rows1 = expert_second_rows(1, 0)
-        turned = bank(6, "h23_turned")
-        turn_hidden(turned[:], h_rows[2:4])
-        expert_quantise(2, turned[:])
-        for t in range(PACK):
-            scatter(t, 0)
-
-        banks = [bank(3, "hs0_low"), bank(5, "hs0_high")]
-        for i in range(2):
-            shared_first(0, banks[i][:, low], i * H // 2)
-        for i in range(2):
-            turn_results(banks[i][:, high], y_rows1, 2 * i)
-        for i, name in enumerate(("y1_low", "y1")):
-            leave_bank(name, banks[i][:, high], 1, 2 * i)
-            silu(hs_rows[0], banks[i][:, low], i * H // 2)
-        for t in range(PACK):
-            scatter(t, 1)
-        w2s_dealt = deal(nc.gpsimd, "w2s_dealt", w2s[:], I32, "y1")
-        w2s_plane_dealt = deal(nc.gpsimd, "w2s_plane_dealt", w2s_plane[:], U8, "w2s")
-
-        def shared_whole(part, acc_bank):
-            acc = bank(acc_bank, "hs%d_acc" % part)
-            shared_first(part, acc[:], 0)
-            silu(hs_rows[part], acc[:], 0)
-
-        def shared_turn(first, turn_bank):
-            turned = bank(turn_bank, "hs_turned%d" % first)
-            turn_hidden(turned[:], hs_rows[first:first + 2])
-            group_hidden(hs_grouped[:, first * PACK * P:(first + 2) * PACK * P], turned[:])
-
-        shared_whole(1, 2)
-        y_rows2 = expert_second_rows(2, 3)
-        shared_whole(2, 1)
-        turned2 = bank(0, "y2_turned")
-        turn_results(turned2[:], y_rows2, 0)
-        leave_bank("y2", turned2[:, low], 2, 0)
-        for t in range(2):
-            scatter(t, 2)
-        shared_whole(3, 5)
-        y_rows3 = expert_second_rows(3, 1)
-        shared_turn(0, 3)
-        shared_turn(2, 5)
+        silu_sorted(h_rows[3], acc[:], 0)
+        planes[3] = deal(nc.gpsimd, "w2_plane3", w2_plane[:, 3 * N:4 * N], U8, "h_grouped1")
+        turned2 = bank(4, "h2_turned")
+        turn_hidden(turned2[:, low], h_rows[2:3])
+        scatter(0, 0, 1, False)
+        expert_quantise(2, turned2[:, low])
+        second_dealt(1, bank(5, "y1_acc"))
+        scatter(3, 0, 1, True)
+        scatter(1, 0, 1, False)
+        scatter(0, 1, 2, False)
+        scatter(1, 1, 2, False)
+        for e in (2, 3):
+            words[e] = deal(nc.gpsimd, "w2_dealt%d" % e, w2_late[:, e % 2 * FP4_ROW:(e % 2 + 1) * FP4_ROW], U16, None, 2)
+        w2s_dealt = deal(nc.gpsimd, "w2s_dealt", w2s[:], I32, None, 2)
+        w2s_plane_dealt = deal(nc.gpsimd, "w2s_plane_dealt", w2s_plane[:], U8, None, 2)
+        shared_first(0, bank(0, "hs0"))
+        bank1, bank2 = bank(1, "hs1_low"), bank(2, "hs1_high")
+        shared_product(1, bank1[:, low], 0)
+        shared_product(1, bank2[:, low], H // 2)
+        silu_sorted(hs_rows[1], bank1[:, low], 0)
+        turn_hidden(bank2[:, high], h_rows[3:4])
+        expert_quantise(3, bank2[:, high])
+        silu_sorted(hs_rows[1], bank2[:, low], H // 2)
+        shared_first(2, bank(3, "hs2"))
+        second_dealt(2, bank(4, "y2_acc"))
+        shared_first(3, bank(0, "hs3"))
+        shared_turn(0, bank(1, "hs_turned0"))
+        shared_turn(2, bank(2, "hs_turned2"))
+        scatter(0, 2, 3, False)
+        scatter(1, 2, 3, False)
+        second_dealt(3, bank(1, "y3_acc"))
         hs_codes = tile("hs_codes", T, U32)
         hs_plane = tile("hs_plane", T, U8)
         nc.vector.quantize_mx(out=hs_codes[:].bitcast(FP8X4), scales=hs_plane[:], in_=hs_grouped[:])
-        leave_bank("y2_last", turned2[:, high], 2, 2, "hs_rows3")
-        for t in range(2, PACK):
-            scatter(t, 2)
-        turned = bank(2, "y3_turned")
-        turn_results(turned[:], y_rows3, 0)
-        leave_bank("y3_low", turned[:, low], 3, 0, "hs_rows2")
-        leave_bank("y3_high", turned[:, high], 3, 2, "hs_rows1")
-        for t in range(PACK):
-            scatter(t, 3)
+        scatter(2, 0, 3, True, "hs_rows3")
+        scatter(0, 3, 4, False)
+        scatter(3, 2, 4, True)
+        scatter(1, 3, 4, False)
+        scatter(2, 3, 4, True)
+        scatter(3, 1, 2, True)
 
         ys = {}
-        for t, acc_bank in enumerate((7, 6, 4, 1)):
+        for t, acc_bank in enumerate((6, 7, 5, 0)):
             ys[t] = bank(acc_bank, "ys%d" % t)
             nc.tensor.matmul_mx(out=ys[t][:], lhsT=w2s_dealt[:, t * P:(t + 1) * P].bitcast(FP8X4),
                                 lhsT_scale=w2s_plane_dealt[:, t * P:(t + 1) * P],
@@ -348,7 +319,7 @@ def tile_moe_shf_mlp_silu_kernel(
         def store(t):
             nc.sync.dma_start(out=out_rows[:, t, :], in_=total[:, t * T:(t + 1) * T])
 
-        for t in range(LAST):
+        for t in (0, 1, 2):
             add(t, 0, T)
             store(t)
         for first in (3 * quarter, 2 * quarter, 0, quarter):

@@ -24,6 +24,7 @@ LIST_COLS = C // 16
 PLANE = 512
 FP4_ROW = 2 * PLANE
 LAST = PACK - 1
+LINE = 16
 PLACED = {"slot_words0_0": 0, "slot_words2_0": 0, "routed3": 0}
 
 
@@ -128,11 +129,12 @@ def tile_moe_shf_mlp_silu_kernel(
 
         def deal(engine, name, source, dtype, tag=None, pieces=1):
             dealt = tile(name, source.shape[1], source.dtype, tag)
-            out = dealt[:].bitcast(dtype).rearrange("p (s t m) -> p s t m", t=PACK, m=P)
-            in_ = source.bitcast(dtype).rearrange("p (s m t) -> p s t m", t=PACK, m=P)
-            step = PACK // pieces
-            for first in range(0, PACK, step):
-                engine.tensor_copy(out[:, :, first:first + step, :], in_[:, :, first:first + step, :])
+            run = LINE // {I32: 4, U16: 2, U8: 1}[dtype]
+            out = dealt[:].bitcast(dtype).rearrange("p (s t c i) -> p s c t i", t=PACK, c=P // run, i=run)
+            in_ = source.bitcast(dtype).rearrange("p (s c i t) -> p s c t i", t=PACK, c=P // run, i=run)
+            step = P // run // pieces
+            for first in range(0, P // run, step):
+                engine.tensor_copy(out[:, :, first:first + step], in_[:, :, first:first + step])
             return dealt
 
         def silu_sorted(rows, acc, first):
@@ -326,13 +328,13 @@ def tile_moe_shf_mlp_silu_kernel(
             add(LAST, first, quarter)
         store(LAST)
         out_grouped = [tile("out_grouped%d" % i, PACK * half, BF16) for i in range(2)]
-        by_token = total[:].rearrange("p (t c) -> p c t", t=PACK)
-        for first in (quarter, 0):
-            nc.scalar.copy(out=out_grouped[1][:].rearrange("p (c t) -> p c t", t=PACK)[:, first:first + quarter, :],
-                           in_=by_token[:, half + first:half + first + quarter, :])
-        for first in (0, quarter):
-            nc.vector.tensor_copy(out_grouped[0][:].rearrange("p (c t) -> p c t", t=PACK)[:, first:first + quarter, :],
-                                  by_token[:, first:first + quarter, :])
+        by_token = total[:].rearrange("p (t c i) -> p c t i", t=PACK, i=4)
+        grouped = [g[:].rearrange("p (c i t) -> p c t i", t=PACK, i=4) for g in out_grouped]
+        runs = quarter // 4
+        for first in (runs, 0):
+            nc.scalar.copy(out=grouped[1][:, first:first + runs], in_=by_token[:, 2 * runs + first:3 * runs + first])
+        for first in (0, runs):
+            nc.vector.tensor_copy(grouped[0][:, first:first + runs], by_token[:, first:first + runs])
         out_codes = tile("out_codes", T, U32)
         out_plane = tile("out_plane", T, U8)
         words_out = out_1[0].rearrange("p c d -> p (c d)").bitcast(I32)

@@ -95,8 +95,8 @@ def tile_moe_shf_mlp_silu_kernel(
         load_fp4(w1[0], w1_words[0])
         load_planes(w1_planes[0], w1_scales[0:2].rearrange("e s b c -> (e s) b c"))
         load_fp4(w1[1], w1_words[1])
-        load_fp4(w2_early, w2_words[0:2, 0])
         load_planes(w2_plane, w2_scales.rearrange("e s b c -> (e s) b c"))
+        load_fp4(w2_early, w2_words[0:2, 0])
         load_fp4(w1[2], w1_words[2])
         load_planes(w1_planes[1], w1_scales[2:4].rearrange("e s b c -> (e s) b c"))
         nc.sync.dma_start(out=gate_first[:], in_=gate[:, 0:2 * C])
@@ -232,20 +232,18 @@ def tile_moe_shf_mlp_silu_kernel(
         gather_bytes(0, 1)
         gather_bytes(1, 2)
         gather_bytes(2, E)
-        planes = {2: deal(nc.gpsimd, "w2_plane2", w2_plane[:, 2 * N:3 * N], U8)}
+        planes = {0: deal(nc.gpsimd, "w2_plane0", w2_plane[:, 0:N], U8)}
         for g in range(4):
             acc = bank(g, "h0_acc%d" % g)
             expert_first(0, acc[:, 0:P], g * P)
             silu_sorted(h_rows[0], acc[:, 0:P], g * P)
         gather_words(2, E)
-        dealt = deal(nc.vector, "w2_dealt0", w2_early[:], U16)
-        words = {e: dealt[:, e * FP4_ROW:(e + 1) * FP4_ROW] for e in range(2)}
-        planes[0] = deal(nc.vector, "w2_plane0", w2_plane[:, 0:N], U8)
+        words = {e: deal(nc.vector, "w2_dealt%d" % e, w2_early[:, e * FP4_ROW:(e + 1) * FP4_ROW], U16) for e in range(2)}
         bank4 = bank(4, "h1_low")
         expert_first(1, bank4[:, low], 0)
         turn_hidden(bank4[:, high], h_rows[0:1])
-        expert_quantise(0, bank4[:, high])
-        planes[1] = deal(nc.vector, "w2_plane1", w2_plane[:, N:2 * N], U8, "h_rows0")
+        expert_quantise(0, bank4[:, high], "w2_early")
+        planes[1] = deal(nc.vector, "w2_plane1", w2_plane[:, N:2 * N], U8, "h_grouped0")
         silu_sorted(h_rows[1], bank4[:, low], 0)
         acc = bank(0, "h1_high")
         expert_first(1, acc[:, low], H // 2)
@@ -263,7 +261,8 @@ def tile_moe_shf_mlp_silu_kernel(
         acc = bank(3, "h3_acc")
         expert_first(3, acc[:], 0)
         silu_sorted(h_rows[3], acc[:], 0)
-        planes[3] = deal(nc.gpsimd, "w2_plane3", w2_plane[:, 3 * N:4 * N], U8, "h_grouped1")
+        dealt = deal(nc.gpsimd, "w2_plane2", w2_plane[:, 2 * N:], U8, "h_grouped1", 4)
+        planes[2], planes[3] = dealt[:, 0:N], dealt[:, N:]
         turned2 = bank(4, "h2_turned")
         turn_hidden(turned2[:, low], h_rows[2:3])
         scatter(0, 0, 1, False)
@@ -273,8 +272,8 @@ def tile_moe_shf_mlp_silu_kernel(
         scatter(1, 0, 1, False)
         scatter(0, 1, 2, False)
         scatter(1, 1, 2, False)
-        for e in (2, 3):
-            words[e] = deal(nc.gpsimd, "w2_dealt%d" % e, w2_late[:, e % 2 * FP4_ROW:(e % 2 + 1) * FP4_ROW], U16, None, 2)
+        words[2] = deal(nc.gpsimd, "w2_dealt2", w2_late[:, 0:FP4_ROW], U16, None, 2)
+        words[3] = deal(nc.gpsimd, "w2_dealt3", w2_late[:, FP4_ROW:], U16, None, 2)
         w2s_dealt = deal(nc.gpsimd, "w2s_dealt", w2s[:], I32, None, 2)
         w2s_plane_dealt = deal(nc.gpsimd, "w2s_plane_dealt", w2s_plane[:], U8, None, 2)
         shared_first(0, bank(0, "hs0"))
@@ -286,12 +285,11 @@ def tile_moe_shf_mlp_silu_kernel(
         expert_quantise(3, bank2[:, high])
         silu_sorted(hs_rows[1], bank2[:, low], H // 2)
         shared_first(2, bank(3, "hs2"))
-        second_dealt(2, bank(4, "y2_acc"))
         shared_first(3, bank(0, "hs3"))
+        second_dealt(2, bank(3, "y2_acc"))
         shared_turn(0, bank(1, "hs_turned0"))
         shared_turn(2, bank(2, "hs_turned2"))
         scatter(0, 2, 3, False)
-        scatter(1, 2, 3, False)
         second_dealt(3, bank(1, "y3_acc"))
         hs_codes = tile("hs_codes", T, U32)
         hs_plane = tile("hs_plane", T, U8)
@@ -299,7 +297,7 @@ def tile_moe_shf_mlp_silu_kernel(
         scatter(2, 0, 3, True, "hs_rows3")
         scatter(0, 3, 4, False)
         scatter(3, 2, 4, True)
-        scatter(1, 3, 4, False)
+        scatter(1, 2, 4, False)
         scatter(2, 3, 4, True)
         scatter(3, 1, 2, True)
 

@@ -25,7 +25,10 @@ PLANE = 512
 FP4_ROW = 2 * PLANE
 LAST = PACK - 1
 LINE = 16
-PLACED = {"slot_words0_0": 0, "slot_words2_0": 0, "routed3": 0}
+PLACED = {"slot_words0_0": 0, "slot_words2_0": 0, "routed3": 0,
+          "w2_plane2": 2048, "h_grouped1": 2048, "w2_dealt2": 2560,
+          "w2_plane3": 4096, "h_grouped2": 4096, "w2_dealt3": 4608,
+          "w2s_plane_dealt": 6144, "h_grouped3": 6144, "w2s_dealt": 6656}
 
 
 def tile_moe_shf_mlp_silu_kernel(
@@ -95,16 +98,16 @@ def tile_moe_shf_mlp_silu_kernel(
         load_fp4(w1[0], w1_words[0])
         load_planes(w1_planes[0], w1_scales[0:2].rearrange("e s b c -> (e s) b c"))
         load_fp4(w1[1], w1_words[1])
-        load_planes(w2_plane, w2_scales.rearrange("e s b c -> (e s) b c"))
         load_fp4(w2_early, w2_words[0:2, 0])
+        load_planes(w2_plane, w2_scales.rearrange("e s b c -> (e s) b c"))
         load_fp4(w1[2], w1_words[2])
         load_planes(w1_planes[1], w1_scales[2:4].rearrange("e s b c -> (e s) b c"))
         nc.sync.dma_start(out=gate_first[:], in_=gate[:, 0:2 * C])
         load_fp4(w1[3], w1_words[3])
+        load_fp4(w2_late, w2_words[2:4, 0])
         nc.sync.dma_start(out=w1s[:].rearrange("p (s c) -> p s c", s=PASSES),
                           in_=w1s_words.rearrange("s p c d -> p s (c d)").bitcast(I32))
         load_planes(w1s_plane, w1s_scales)
-        load_fp4(w2_late, w2_words[2:4, 0])
         nc.sync.dma_start(out=gate_rest[:], in_=gate[:, 2 * C:])
         load_fp8(w2s, w2s_words[0])
         load_planes(w2s_plane, w2s_scales)
@@ -133,8 +136,9 @@ def tile_moe_shf_mlp_silu_kernel(
             out = dealt[:].bitcast(dtype).rearrange("p (s t c i) -> p s c t i", t=PACK, c=P // run, i=run)
             in_ = source.bitcast(dtype).rearrange("p (s c i t) -> p s c t i", t=PACK, c=P // run, i=run)
             step = P // run // pieces
-            for first in range(0, P // run, step):
-                engine.tensor_copy(out[:, :, first:first + step], in_[:, :, first:first + step])
+            for s in range(out.shape[1]):
+                for first in range(0, P // run, step):
+                    engine(out[:, s, first:first + step], in_[:, s, first:first + step])
             return dealt
 
         def silu_sorted(rows, acc, first):
@@ -227,23 +231,29 @@ def tile_moe_shf_mlp_silu_kernel(
                 out=hs_grouped[:, first * PACK * P:(first + 2) * PACK * P].bitcast(F32).rearrange("p (i c u) -> p i c u", c=P, u=2),
                 in_=turned[:].rearrange("p (i u c) -> p i c u", c=P, u=2))
 
+        def deal_second(e):
+            planes[e] = deal(nc.gpsimd.tensor_copy, "w2_plane%d" % e, w2_plane[:, e * N:(e + 1) * N], U8)
+            words[e] = deal(nc.gpsimd.tensor_copy, "w2_dealt%d" % e, w2_late[:, e % 2 * FP4_ROW:(e % 2 + 1) * FP4_ROW], U16)
+
         gather_words(0, 1)
         gather_words(1, 2)
         gather_bytes(0, 1)
         gather_bytes(1, 2)
         gather_bytes(2, E)
-        planes = {0: deal(nc.gpsimd, "w2_plane0", w2_plane[:, 0:N], U8)}
+        planes = {}
         for g in range(4):
             acc = bank(g, "h0_acc%d" % g)
             expert_first(0, acc[:, 0:P], g * P)
             silu_sorted(h_rows[0], acc[:, 0:P], g * P)
         gather_words(2, E)
-        words = {e: deal(nc.vector, "w2_dealt%d" % e, w2_early[:, e * FP4_ROW:(e + 1) * FP4_ROW], U16) for e in range(2)}
+        dealt = deal(nc.vector.tensor_copy, "w2_dealt0", w2_early[:], U16)
+        words = {e: dealt[:, e * FP4_ROW:(e + 1) * FP4_ROW] for e in range(2)}
+        planes[0] = deal(nc.vector.tensor_copy, "w2_plane0", w2_plane[:, 0:N], U8)
         bank4 = bank(4, "h1_low")
         expert_first(1, bank4[:, low], 0)
         turn_hidden(bank4[:, high], h_rows[0:1])
-        expert_quantise(0, bank4[:, high], "w2_early")
-        planes[1] = deal(nc.vector, "w2_plane1", w2_plane[:, N:2 * N], U8, "h_grouped0")
+        expert_quantise(0, bank4[:, high])
+        planes[1] = deal(nc.vector.tensor_copy, "w2_plane1", w2_plane[:, N:2 * N], U8, "h_rows0")
         silu_sorted(h_rows[1], bank4[:, low], 0)
         acc = bank(0, "h1_high")
         expert_first(1, acc[:, low], H // 2)
@@ -261,8 +271,7 @@ def tile_moe_shf_mlp_silu_kernel(
         acc = bank(3, "h3_acc")
         expert_first(3, acc[:], 0)
         silu_sorted(h_rows[3], acc[:], 0)
-        dealt = deal(nc.gpsimd, "w2_plane2", w2_plane[:, 2 * N:], U8, "h_grouped1", 4)
-        planes[2], planes[3] = dealt[:, 0:N], dealt[:, N:]
+        deal_second(2)
         turned2 = bank(4, "h2_turned")
         turn_hidden(turned2[:, low], h_rows[2:3])
         scatter(0, 0, 1, False)
@@ -272,10 +281,7 @@ def tile_moe_shf_mlp_silu_kernel(
         scatter(1, 0, 1, False)
         scatter(0, 1, 2, False)
         scatter(1, 1, 2, False)
-        words[2] = deal(nc.gpsimd, "w2_dealt2", w2_late[:, 0:FP4_ROW], U16, None, 2)
-        words[3] = deal(nc.gpsimd, "w2_dealt3", w2_late[:, FP4_ROW:], U16, None, 2)
-        w2s_dealt = deal(nc.gpsimd, "w2s_dealt", w2s[:], I32, None, 2)
-        w2s_plane_dealt = deal(nc.gpsimd, "w2s_plane_dealt", w2s_plane[:], U8, None, 2)
+        deal_second(3)
         shared_first(0, bank(0, "hs0"))
         bank1, bank2 = bank(1, "hs1_low"), bank(2, "hs1_high")
         shared_product(1, bank1[:, low], 0)
@@ -283,16 +289,18 @@ def tile_moe_shf_mlp_silu_kernel(
         silu_sorted(hs_rows[1], bank1[:, low], 0)
         turn_hidden(bank2[:, high], h_rows[3:4])
         expert_quantise(3, bank2[:, high])
+        w2s_dealt = deal(nc.gpsimd.tensor_copy, "w2s_dealt", w2s[:], I32)
+        w2s_plane_dealt = deal(nc.gpsimd.tensor_copy, "w2s_plane_dealt", w2s_plane[:], U8)
         silu_sorted(hs_rows[1], bank2[:, low], H // 2)
         shared_first(2, bank(3, "hs2"))
         shared_first(3, bank(0, "hs3"))
-        second_dealt(2, bank(3, "y2_acc"))
+        second_dealt(2, bank(2, "y2_acc"))
         shared_turn(0, bank(1, "hs_turned0"))
-        shared_turn(2, bank(2, "hs_turned2"))
+        shared_turn(2, bank(4, "hs_turned2"))
         scatter(0, 2, 3, False)
         second_dealt(3, bank(1, "y3_acc"))
         hs_codes = tile("hs_codes", T, U32)
-        hs_plane = tile("hs_plane", T, U8)
+        hs_plane = tile("hs_plane", T, U8, "h_plane3")
         nc.vector.quantize_mx(out=hs_codes[:].bitcast(FP8X4), scales=hs_plane[:], in_=hs_grouped[:])
         scatter(2, 0, 3, True, "hs_rows3")
         scatter(0, 3, 4, False)

@@ -25,10 +25,10 @@ PLANE = 512
 FP4_ROW = 2 * PLANE
 LAST = PACK - 1
 LINE = 16
-PLACED = {"slot_words0_0": 0, "slot_words2_0": 0, "routed3": 0,
-          "w2_plane2": 2048, "h_grouped1": 2048, "w2_dealt2": 2560,
-          "w2_plane3": 4096, "h_grouped2": 4096, "w2_dealt3": 4608,
-          "w2s_plane_dealt": 6144, "h_grouped3": 6144, "w2s_dealt": 6656}
+PLACED = {"slot_words3_0": 0, "h_codes0": 1024, "w2_0": 512, "routed3": 0,
+          "routed0": 2048, "h_grouped1": 4096 - 64, "w2_plane2": 4096, "routed1": 4096 + 512,
+          "w2_plane3": 7168, "h_grouped2": 7168, "w2_dealt3": 7680,
+          "w2s_plane_dealt": 9216, "h_grouped3": 9216, "w2s_dealt": 9728}
 
 
 def tile_moe_shf_mlp_silu_kernel(
@@ -73,7 +73,7 @@ def tile_moe_shf_mlp_silu_kernel(
         x_plane = zero_planes("x_plane", PASSES)
         w1_planes = [zero_planes("w1_plane%d" % i, 2 * PASSES) for i in range(2)]
         w2_plane = zero_planes("w2_plane", E)
-        w1s_plane = zero_planes("w1s_plane", PASSES)
+        w1s_plane = zero_planes("w1s_plane", 1)
         w2s_plane = zero_planes("w2s_plane", 1)
 
         ident = tile("ident", P, F32)
@@ -83,7 +83,7 @@ def tile_moe_shf_mlp_silu_kernel(
         offsets = sb.tile([P, T // 16], U16, name="offsets")
         x_tok = [tile("x_tok%d" % s, T, I32) for s in range(PASSES)]
         w1 = [tile("w1_%d" % e, PASSES * FP4_ROW, U8) for e in range(E)]
-        w2_early = tile("w2_early", 2 * FP4_ROW, U8)
+        w2_early = [tile("w2_%d" % e, FP4_ROW, U8) for e in range(2)]
         w2_late = tile("w2_late", 2 * FP4_ROW, U8)
         w1s = tile("w1s", PASSES * H, I32)
         w2s = tile("w2s", N, I32)
@@ -91,23 +91,26 @@ def tile_moe_shf_mlp_silu_kernel(
         gates = [(gate_first, gate_rest)[e // 2][:, e % 2 * C:(e % 2 + 1) * C] for e in range(E)]
 
         nc.sync.dma_start(offsets[:], offs)
+        load_planes(x_plane, x_scales, (0, 1, 2))
         load_fp8(x_tok[0], x_words[0])
-        load_planes(x_plane, x_scales, (0, 1))
         load_fp8(x_tok[1], x_words[1])
-        load_planes(x_plane, x_scales, (2, 3))
+        load_planes(x_plane, x_scales, (3,))
         load_fp4(w1[0], w1_words[0])
         load_planes(w1_planes[0], w1_scales[0:2].rearrange("e s b c -> (e s) b c"))
         load_fp4(w1[1], w1_words[1])
-        load_fp4(w2_early, w2_words[0:2, 0])
         load_planes(w2_plane, w2_scales.rearrange("e s b c -> (e s) b c"))
+        load_fp4(w2_early[0], w2_words[0])
+        nc.sync.dma_start(out=gate_first[:], in_=gate[:, 0:2 * C])
+        load_fp4(w2_early[1], w2_words[1])
         load_fp4(w1[2], w1_words[2])
         load_planes(w1_planes[1], w1_scales[2:4].rearrange("e s b c -> (e s) b c"))
-        nc.sync.dma_start(out=gate_first[:], in_=gate[:, 0:2 * C])
         load_fp4(w1[3], w1_words[3])
         load_fp4(w2_late, w2_words[2:4, 0])
         nc.sync.dma_start(out=w1s[:].rearrange("p (s c) -> p s c", s=PASSES),
                           in_=w1s_words.rearrange("s p c d -> p s (c d)").bitcast(I32))
-        load_planes(w1s_plane, w1s_scales)
+        for q in range(4):
+            nc.sync.dma_start(out=w1s_plane[32 * q:32 * q + 4 * PASSES, :].bitcast(I32),
+                              in_=w1s_scales[:, 4 * q:4 * q + 4, :].bitcast(I32))
         nc.sync.dma_start(out=gate_rest[:], in_=gate[:, 2 * C:])
         load_fp8(w2s, w2s_words[0])
         load_planes(w2s_plane, w2s_scales)
@@ -218,7 +221,7 @@ def tile_moe_shf_mlp_silu_kernel(
                 at = slice(s * H + first, s * H + first + acc.shape[1])
                 nc.tensor.matmul_mx(out=acc, lhsT=x_tok[s][:, cols].bitcast(FP8X4),
                                     lhsT_scale=x_plane[:, s * T:(s + 1) * T][:, cols],
-                                    rhs=w1s[:, at].bitcast(FP8X4), rhs_scale=w1s_plane[:, at],
+                                    rhs=w1s[:, at].bitcast(FP8X4), rhs_scale=w1s_plane[4 * s:P, first:first + acc.shape[1]],
                                     start=(s == 0), stop=(s == PASSES - 1))
 
         def shared_first(part, acc):
@@ -231,70 +234,66 @@ def tile_moe_shf_mlp_silu_kernel(
                 out=hs_grouped[:, first * PACK * P:(first + 2) * PACK * P].bitcast(F32).rearrange("p (i c u) -> p i c u", c=P, u=2),
                 in_=turned[:].rearrange("p (i u c) -> p i c u", c=P, u=2))
 
-        def deal_second(e):
-            planes[e] = deal(nc.gpsimd.tensor_copy, "w2_plane%d" % e, w2_plane[:, e * N:(e + 1) * N], U8)
-            words[e] = deal(nc.gpsimd.tensor_copy, "w2_dealt%d" % e, w2_late[:, e % 2 * FP4_ROW:(e % 2 + 1) * FP4_ROW], U16)
-
         gather_words(0, 1)
         gather_words(1, 2)
         gather_bytes(0, 1)
         gather_bytes(1, 2)
         gather_bytes(2, E)
-        planes = {}
         for g in range(4):
             acc = bank(g, "h0_acc%d" % g)
             expert_first(0, acc[:, 0:P], g * P)
             silu_sorted(h_rows[0], acc[:, 0:P], g * P)
-        gather_words(2, E)
-        dealt = deal(nc.vector.tensor_copy, "w2_dealt0", w2_early[:], U16)
-        words = {e: dealt[:, e * FP4_ROW:(e + 1) * FP4_ROW] for e in range(2)}
-        planes[0] = deal(nc.vector.tensor_copy, "w2_plane0", w2_plane[:, 0:N], U8)
+        gather_words(2, 3, tag="slot_words0_0")
+        planes = {0: deal(nc.vector.tensor_copy, "w2_plane0", w2_plane[:, 0:N], U8)}
+        words = {0: deal(nc.vector.tensor_copy, "w2_dealt0", w2_early[0][:], U16)}
         bank4 = bank(4, "h1_low")
         expert_first(1, bank4[:, low], 0)
         turn_hidden(bank4[:, high], h_rows[0:1])
         expert_quantise(0, bank4[:, high])
-        planes[1] = deal(nc.vector.tensor_copy, "w2_plane1", w2_plane[:, N:2 * N], U8, "h_rows0")
+        gather_words(3, E)
         silu_sorted(h_rows[1], bank4[:, low], 0)
-        acc = bank(0, "h1_high")
+        acc = bank(3, "h1_high")
         expert_first(1, acc[:, low], H // 2)
         silu_sorted(h_rows[1], acc[:, low], H // 2)
-        bank1, bank2, bank5 = bank(1, "h2_mid"), bank(2, "h2_first"), bank(5, "h2_last")
-        expert_first(2, bank2[:, 0:P], 0)
-        silu_sorted(h_rows[2], bank2[:, 0:P], 0)
-        expert_first(2, bank1[:, low], P)
-        expert_first(2, bank5[:, 0:P], 3 * P)
-        silu_sorted(h_rows[2], bank5[:, 0:P], 3 * P)
+        bank0, bank1 = bank(0, "y0_low"), bank(1, "y0_high")
+        second_product(0, bank0[:, low], 0)
+        second_product(0, bank1[:, low], 2)
         turn_hidden(bank1[:, high], h_rows[1:2])
-        second_dealt(0, bank(2, "y0_acc"))
-        expert_quantise(1, bank1[:, high], "h_plane0")
-        silu_sorted(h_rows[2], bank1[:, low], P)
-        acc = bank(3, "h3_acc")
-        expert_first(3, acc[:], 0)
-        silu_sorted(h_rows[3], acc[:], 0)
-        deal_second(2)
-        turned2 = bank(4, "h2_turned")
-        turn_hidden(turned2[:, low], h_rows[2:3])
+        gate_results(0, bank0[:, low], 0)
+        planes[1] = deal(nc.vector.tensor_copy, "w2_plane1", w2_plane[:, N:2 * N], U8, "h_plane0")
+        expert_quantise(1, bank1[:, high])
+        gate_results(0, bank1[:, low], 2)
+        words[1] = deal(nc.scalar.copy, "w2_dealt1", w2_early[1][:], U16)
+        planes[2] = deal(nc.gpsimd.tensor_copy, "w2_plane2", w2_plane[:, 2 * N:3 * N], U8)
+        for e in (2, 3):
+            acc = bank(e, "h%d_acc" % e)
+            expert_first(e, acc[:], 0)
+            silu_sorted(h_rows[e], acc[:], 0)
+        words[2] = deal(nc.gpsimd.tensor_copy, "w2_dealt2", w2_late[:, 0:FP4_ROW], U16)
         scatter(0, 0, 1, False)
-        expert_quantise(2, turned2[:, low])
-        second_dealt(1, bank(5, "y1_acc"))
-        scatter(3, 0, 1, True)
         scatter(1, 0, 1, False)
+        turned = bank(4, "h2_turned")
+        turn_hidden(turned[:, low], h_rows[2:3])
+        expert_quantise(2, turned[:, low])
+        second_dealt(1, bank(2, "y1_acc"))
+        scatter(3, 0, 1, True)
         scatter(0, 1, 2, False)
         scatter(1, 1, 2, False)
-        deal_second(3)
+        planes[3] = deal(nc.gpsimd.tensor_copy, "w2_plane3", w2_plane[:, 3 * N:], U8)
+        words[3] = deal(nc.gpsimd.tensor_copy, "w2_dealt3", w2_late[:, FP4_ROW:], U16)
         shared_first(0, bank(0, "hs0"))
-        bank1, bank2 = bank(1, "hs1_low"), bank(2, "hs1_high")
+        bank1, bank3 = bank(1, "hs1_low"), bank(3, "hs1_high")
         shared_product(1, bank1[:, low], 0)
-        shared_product(1, bank2[:, low], H // 2)
+        shared_product(1, bank3[:, low], H // 2)
         silu_sorted(hs_rows[1], bank1[:, low], 0)
-        turn_hidden(bank2[:, high], h_rows[3:4])
-        expert_quantise(3, bank2[:, high])
+        turn_hidden(bank3[:, high], h_rows[3:4])
+        expert_quantise(3, bank3[:, high])
         w2s_dealt = deal(nc.gpsimd.tensor_copy, "w2s_dealt", w2s[:], I32)
         w2s_plane_dealt = deal(nc.gpsimd.tensor_copy, "w2s_plane_dealt", w2s_plane[:], U8)
-        silu_sorted(hs_rows[1], bank2[:, low], H // 2)
-        shared_first(2, bank(3, "hs2"))
+        silu_sorted(hs_rows[1], bank3[:, low], H // 2)
+        shared_first(2, bank(4, "hs2"))
         shared_first(3, bank(0, "hs3"))
-        second_dealt(2, bank(2, "y2_acc"))
+        second_dealt(2, bank(3, "y2_acc"))
         shared_turn(0, bank(1, "hs_turned0"))
         shared_turn(2, bank(4, "hs_turned2"))
         scatter(0, 2, 3, False)
@@ -310,7 +309,7 @@ def tile_moe_shf_mlp_silu_kernel(
         scatter(3, 1, 2, True)
 
         ys = {}
-        for t, acc_bank in enumerate((6, 7, 5, 0)):
+        for t, acc_bank in enumerate((6, 7, 5, 2)):
             ys[t] = bank(acc_bank, "ys%d" % t)
             nc.tensor.matmul_mx(out=ys[t][:], lhsT=w2s_dealt[:, t * P:(t + 1) * P].bitcast(FP8X4),
                                 lhsT_scale=w2s_plane_dealt[:, t * P:(t + 1) * P],

@@ -91,10 +91,10 @@ def tile_moe_shf_mlp_silu_kernel(
         gates = [(gate_first, gate_rest)[e // 2][:, e % 2 * C:(e % 2 + 1) * C] for e in range(E)]
 
         nc.sync.dma_start(offsets[:], offs)
-        load_planes(x_plane, x_scales, (0, 1, 2))
         load_fp8(x_tok[0], x_words[0])
+        load_planes(x_plane, x_scales, (0, 1))
         load_fp8(x_tok[1], x_words[1])
-        load_planes(x_plane, x_scales, (3,))
+        load_planes(x_plane, x_scales, (2, 3))
         load_fp4(w1[0], w1_words[0])
         load_planes(w1_planes[0], w1_scales[0:2].rearrange("e s b c -> (e s) b c"))
         load_fp4(w1[1], w1_words[1])

@@ -24,11 +24,17 @@ LIST_COLS = C // 16
 PLANE = 512
 FP4_ROW = 2 * PLANE
 LAST = PACK - 1
+SHARE = 96
 LINE = 16
-PLACED = {"slot_words3_0": 0, "h_codes0": 1024, "w2_0": 512, "routed3": 0,
-          "routed0": 2048, "h_grouped1": 4096 - 64, "w2_plane2": 4096, "routed1": 4096 + 512,
-          "w2_plane3": 7168, "h_grouped2": 7168, "w2_dealt3": 7680,
-          "w2s_plane_dealt": 9216, "h_grouped3": 9216, "w2s_dealt": 9728}
+PLACED = {
+    "w2_0": 0, "h_codes0": 512,
+    "h_grouped0": 2048, "w2_plane1": 2048,
+    "w2_1": 6144, "routed3": 4160, "h_grouped1": 7104, "late_planes": 7168,
+    "h_rows3": 8192, "gated1_last": 8192,
+    "h_grouped3": 9216, "w2s_plane_dealt": 9216,
+    "h_grouped2": 14336, "w2s_dealt": 14336,
+    "hs_rows3": 12288, "routed2": 12288,
+}
 
 
 def tile_moe_shf_mlp_silu_kernel(
@@ -99,49 +105,40 @@ def tile_moe_shf_mlp_silu_kernel(
         load_planes(w1_planes[0], w1_scales[0:2].rearrange("e s b c -> (e s) b c"))
         load_fp4(w1[1], w1_words[1])
         load_planes(w2_plane, w2_scales.rearrange("e s b c -> (e s) b c"))
+        load_fp4(w2_early[1], w2_words[1])
         load_fp4(w2_early[0], w2_words[0])
         nc.sync.dma_start(out=gate_first[:], in_=gate[:, 0:2 * C])
-        load_fp4(w2_early[1], w2_words[1])
         load_fp4(w1[2], w1_words[2])
         load_planes(w1_planes[1], w1_scales[2:4].rearrange("e s b c -> (e s) b c"))
         load_fp4(w1[3], w1_words[3])
-        load_fp4(w2_late, w2_words[2:4, 0])
         nc.sync.dma_start(out=w1s[:].rearrange("p (s c) -> p s c", s=PASSES),
                           in_=w1s_words.rearrange("s p c d -> p s (c d)").bitcast(I32))
         for q in range(4):
             nc.sync.dma_start(out=w1s_plane[32 * q:32 * q + 4 * PASSES, :].bitcast(I32),
                               in_=w1s_scales[:, 4 * q:4 * q + 4, :].bitcast(I32))
+        load_fp4(w2_late, w2_words[2:4, 0])
         nc.sync.dma_start(out=gate_rest[:], in_=gate[:, 2 * C:])
         load_fp8(w2s, w2s_words[0])
         load_planes(w2s_plane, w2s_scales)
 
         slot_words, slot_bytes = {}, {}
 
-        def gather(name, dtype, windows, into, first, last, passes, tag):
-            width = (last - first) * C
-            gathered = tile("%s%d_%d" % (name, first, passes[0]), len(passes) * width, dtype, tag)
-            entries = offsets[:, first * LIST_COLS:last * LIST_COLS]
-            for i, s in enumerate(passes):
-                nc.vector.tensor_copy(gathered[:, i * width:(i + 1) * width], windows[s].indirect(entries))
-                for e in range(first, last):
-                    into[e, s] = gathered[:, i * width + (e - first) * C:i * width + (e - first + 1) * C]
+        def gather(gathered, window, into, first, last, s):
+            nc.vector.tensor_copy(gathered, window.indirect(offsets[:, first * LIST_COLS:last * LIST_COLS]))
+            for e in range(first, last):
+                into[e, s] = gathered[:, (e - first) * C:(e - first + 1) * C]
 
-        def gather_words(first, last, passes=range(PASSES), tag=None):
-            gather("slot_words", U32, [x_tok[s][:].bitcast(U32) for s in range(PASSES)], slot_words, first, last, passes, tag)
+        def gather_words(gathered, first, last, s):
+            gather(gathered, x_tok[s][:].bitcast(U32), slot_words, first, last, s)
 
-        def gather_bytes(first, last, tag=None):
-            gather("slot_bytes", U8, [x_plane[:, s * T:(s + 1) * T] for s in range(PASSES)], slot_bytes, first, last,
-                   range(PASSES), tag)
+        def gather_bytes(first, last, s):
+            gathered = tile("slot_bytes%d_%d" % (first, s), (last - first) * C, U8)
+            gather(gathered[:], x_plane[:, s * T:(s + 1) * T], slot_bytes, first, last, s)
 
-        def deal(engine, name, source, dtype, tag=None, pieces=1):
-            dealt = tile(name, source.shape[1], source.dtype, tag)
+        def deal(copy, dealt, source, dtype):
             run = LINE // {I32: 4, U16: 2, U8: 1}[dtype]
-            out = dealt[:].bitcast(dtype).rearrange("p (s t c i) -> p s c t i", t=PACK, c=P // run, i=run)
-            in_ = source.bitcast(dtype).rearrange("p (s c i t) -> p s c t i", t=PACK, c=P // run, i=run)
-            step = P // run // pieces
-            for s in range(out.shape[1]):
-                for first in range(0, P // run, step):
-                    engine(out[:, s, first:first + step], in_[:, s, first:first + step])
+            copy(dealt.bitcast(dtype).rearrange("p (t c i) -> p c t i", t=PACK, i=run),
+                 source.bitcast(dtype).rearrange("p (c i t) -> p c t i", t=PACK, i=run))
             return dealt
 
         def silu_sorted(rows, acc, first):
@@ -152,9 +149,9 @@ def tile_moe_shf_mlp_silu_kernel(
                 func=ACT.Silu,
             )
 
-        def expert_first(e, acc, first):
+        def expert_first(e, acc, first, passes=range(PASSES)):
             cols = slice(first, first + acc.shape[1])
-            for s in range(PASSES):
+            for s in passes:
                 plane = w1_planes[e // 2][:, (e % 2 * PASSES + s) * H:(e % 2 * PASSES + s + 1) * H]
                 nc.tensor.matmul_mx(out=acc, lhsT=slot_words[e, s].bitcast(FP8X4), lhsT_scale=slot_bytes[e, s],
                                     rhs=w1[e][:].bitcast(U16)[:, s * H:(s + 1) * H][:, cols].bitcast(FP4X4),
@@ -168,44 +165,34 @@ def tile_moe_shf_mlp_silu_kernel(
 
         h_codes, h_plane = {}, {}
 
-        def expert_quantise(first, turned, tag=None):
-            cols = turned.shape[1] // 2
-            grouped = tile("h_grouped%d" % first, PACK * cols, BF16)
-            nc.scalar.copy(out=grouped[:].bitcast(F32).rearrange("p (i c u) -> p i c u", c=P, u=2),
+        def group_hidden(grouped, turned):
+            nc.scalar.copy(out=grouped.bitcast(F32).rearrange("p (i c u) -> p i c u", c=P, u=2),
                            in_=turned.rearrange("p (i u c) -> p i c u", c=P, u=2))
-            codes, plane = tile("h_codes%d" % first, cols, U32), tile("h_plane%d" % first, cols, U8, tag)
-            nc.vector.quantize_mx(out=codes[:].bitcast(FP8X4), scales=plane[:], in_=grouped[:])
-            for i in range(cols // C):
-                h_codes[first + i], h_plane[first + i] = codes[:, i * C:(i + 1) * C], plane[:, i * C:(i + 1) * C]
 
-        gated = tile("gated", PACK * T, F32)
+        def expert_quantise(e, turned, plane_tag=None):
+            grouped = tile("h_grouped%d" % e, PACK * C, BF16)
+            group_hidden(grouped[:], turned)
+            h_codes[e], h_plane[e] = tile("h_codes%d" % e, C, U32), tile("h_plane%d" % e, C, U8, plane_tag)
+            nc.vector.quantize_mx(out=h_codes[e][:].bitcast(FP8X4), scales=h_plane[e][:], in_=grouped[:])
 
-        def second_product(e, acc, first):
-            for i in range(acc.shape[1] // C):
-                t = first + i
+        def second_product(e, acc, tiles):
+            for i, t in enumerate(tiles):
                 nc.tensor.matmul_mx(out=acc[:, i * C:(i + 1) * C], lhsT=words[e][:, 2 * t * P:2 * (t + 1) * P].bitcast(FP4X4),
                                     lhsT_scale=planes[e][:, t * P:(t + 1) * P],
-                                    rhs=h_codes[e].bitcast(FP8X4), rhs_scale=h_plane[e], start=True, stop=True)
+                                    rhs=h_codes[e][:].bitcast(FP8X4), rhs_scale=h_plane[e][:], start=True, stop=True)
 
-        def gate_results(e, acc, first):
+        def gate_results(e, acc, into):
             count = acc.shape[1] // C
-            nc.vector.tensor_tensor(
-                gated[:].rearrange("p (t j) -> p t j", t=PACK)[:, first:first + count, e * C:(e + 1) * C],
-                acc.rearrange("p (t c) -> p t c", t=count),
-                gates[e].unsqueeze(1).to_broadcast([P, count, C]), ALU.mult)
-
-        def second_dealt(e, acc):
-            second_product(e, acc[:], 0)
-            gate_results(e, acc[:], 0)
+            nc.vector.tensor_tensor(into, acc.rearrange("p (t c) -> p t c", t=count),
+                                    gates[e].unsqueeze(1).to_broadcast([P, count, C]), ALU.mult)
 
         routed = {}
 
-        def scatter(t, first, last, on_scalar, tag=None):
+        def scatter(engine, t, first, values):
             if t not in routed:
-                routed[t] = tile("routed%d" % t, T, F32, tag)
-            window = routed[t][:].indirect(offsets[:, first * LIST_COLS:last * LIST_COLS])
-            values = gated[:, t * T + first * C:t * T + last * C]
-            if on_scalar:
+                routed[t] = tile("routed%d" % t, T, F32)
+            window = routed[t][:].indirect(offsets[:, first // 16:(first + values.shape[1]) // 16])
+            if engine is nc.scalar:
                 nc.scalar.activation(window, values, ACT.Copy)
             else:
                 nc.vector.tensor_copy(window, values)
@@ -229,87 +216,116 @@ def tile_moe_shf_mlp_silu_kernel(
             silu_sorted(hs_rows[part], acc[:], 0)
 
         def shared_turn(first, turned):
-            turn_hidden(turned[:], hs_rows[first:first + 2])
-            nc.scalar.copy(
-                out=hs_grouped[:, first * PACK * P:(first + 2) * PACK * P].bitcast(F32).rearrange("p (i c u) -> p i c u", c=P, u=2),
-                in_=turned[:].rearrange("p (i u c) -> p i c u", c=P, u=2))
+            parts = turned.shape[1] // (2 * P)
+            turn_hidden(turned, hs_rows[first:first + parts])
+            group_hidden(hs_grouped[:, first * PACK * P:(first + parts) * PACK * P], turned)
 
-        gather_words(0, 1)
-        gather_words(1, 2)
-        gather_bytes(0, 1)
-        gather_bytes(1, 2)
-        gather_bytes(2, E)
+        V, S, G = nc.vector, nc.scalar, nc.gpsimd
+        for e, s in ((0, 0), (1, 0), (2, 0), (0, 1), (1, 1)):
+            gather_words(tile("slot_words%d_%d" % (e, s), C, U32)[:], e, e + 1, s)
+        for first, last in ((0, 1), (1, 2), (2, E)):
+            for s in range(PASSES):
+                gather_bytes(first, last, s)
+        accs = [bank(g, "h0_acc%d" % g) for g in range(4)]
+        for s in range(PASSES):
+            for g in range(4):
+                expert_first(0, accs[g][:, 0:P], g * P, [s])
         for g in range(4):
-            acc = bank(g, "h0_acc%d" % g)
-            expert_first(0, acc[:, 0:P], g * P)
-            silu_sorted(h_rows[0], acc[:, 0:P], g * P)
-        gather_words(2, 3, tag="slot_words0_0")
-        planes = {0: deal(nc.vector.tensor_copy, "w2_plane0", w2_plane[:, 0:N], U8)}
-        words = {0: deal(nc.vector.tensor_copy, "w2_dealt0", w2_early[0][:], U16)}
-        bank4 = bank(4, "h1_low")
-        expert_first(1, bank4[:, low], 0)
-        turn_hidden(bank4[:, high], h_rows[0:1])
-        expert_quantise(0, bank4[:, high])
-        gather_words(3, E)
-        silu_sorted(h_rows[1], bank4[:, low], 0)
-        acc = bank(3, "h1_high")
-        expert_first(1, acc[:, low], H // 2)
-        silu_sorted(h_rows[1], acc[:, low], H // 2)
-        bank0, bank1 = bank(0, "y0_low"), bank(1, "y0_high")
-        second_product(0, bank0[:, low], 0)
-        second_product(0, bank1[:, low], 2)
-        turn_hidden(bank1[:, high], h_rows[1:2])
-        gate_results(0, bank0[:, low], 0)
-        planes[1] = deal(nc.vector.tensor_copy, "w2_plane1", w2_plane[:, N:2 * N], U8, "h_plane0")
-        expert_quantise(1, bank1[:, high])
-        gate_results(0, bank1[:, low], 2)
-        words[1] = deal(nc.scalar.copy, "w2_dealt1", w2_early[1][:], U16)
-        planes[2] = deal(nc.gpsimd.tensor_copy, "w2_plane2", w2_plane[:, 2 * N:3 * N], U8)
+            silu_sorted(h_rows[0], accs[g][:, 0:P], g * P)
+        late_words = tile("late_words", 3 * C, U32, "slot_words0_0")
+        gather_words(late_words[:, 0:2 * C], 2, E, 1)
+        gather_words(late_words[:, 2 * C:], 3, E, 0)
+        planes = {0: deal(V.tensor_copy, tile("w2_plane0", N, U8)[:], w2_plane[:, 0:N], U8)}
+        words = {0: deal(V.tensor_copy, tile("w2_dealt0", FP4_ROW, U8)[:], w2_early[0][:], U16)}
+
+        for acc, first in ((bank(4, "h1_low"), 0), (bank(7, "h1_high"), H // 2)):
+            expert_first(1, acc[:, low], first)
+            silu_sorted(h_rows[1], acc[:, low], first)
+        turned = bank(5, "h0_turned")
+        turn_hidden(turned[:, low], h_rows[0:1])
+        expert_quantise(0, turned[:, low])
+        planes[1] = deal(G.tensor_copy, tile("w2_plane1", N, U8)[:], w2_plane[:, N:2 * N], U8)
+        words[1] = deal(S.copy, tile("w2_dealt1", FP4_ROW, U8, "w1_1")[:], w2_early[1][:], U16)
+        turned = bank(6, "h1_turned")
+        turn_hidden(turned[:, low], h_rows[1:2])
+        gated = tile("gated", PACK * T, F32)[:].rearrange("p (t j) -> p t j", t=PACK)
+        bank0, bank1 = bank(0, "y0_outer"), bank(1, "y0_inner")
+        second_product(0, bank0[:, low], (0, 3))
+        second_product(0, bank1[:, low], (1, 2))
+        gate_results(0, bank0[:, low], gated[:, 0:4:3, 0:C])
+        expert_quantise(1, turned[:, low], "h_plane0")
+        gate_results(0, bank1[:, low], gated[:, 1:3, 0:C])
+        scatter(V, 0, 0, gated[:, 0, 0:C])
+        scatter(S, 3, 0, gated[:, 3, 0:C])
+        scatter(V, 1, 0, gated[:, 1, 0:C])
+        late_planes, late_dealt = tile("late_planes", 2 * N, U8), tile("late_dealt", 2 * FP4_ROW, U8)
         for e in (2, 3):
-            acc = bank(e, "h%d_acc" % e)
-            expert_first(e, acc[:], 0)
-            silu_sorted(h_rows[e], acc[:], 0)
-        words[2] = deal(nc.gpsimd.tensor_copy, "w2_dealt2", w2_late[:, 0:FP4_ROW], U16)
-        scatter(0, 0, 1, False)
-        scatter(1, 0, 1, False)
-        turned = bank(4, "h2_turned")
+            planes[e] = deal(G.tensor_copy, late_planes[:, (e - 2) * N:(e - 1) * N], w2_plane[:, e * N:(e + 1) * N], U8)
+        for e in (2, 3):
+            cols = slice((e - 2) * FP4_ROW, (e - 1) * FP4_ROW)
+            words[e] = deal(G.tensor_copy, late_dealt[:, cols], w2_late[:, cols], U16)
+
+        bank2, bank4 = bank(2, "h2_low"), bank(4, "h2_high")
+        bank3, bank7 = bank(3, "h3_low"), bank(7, "h3_high")
+        expert_first(2, bank2[:, low], 0)
+        expert_first(2, bank4[:, low], H // 2)
+        second_product(1, bank4[:, high], (0, 1))
+        expert_first(3, bank3[:, low], 0)
+        second_product(1, bank3[:, high], (2, 3))
+        expert_first(3, bank7[:, low], H // 2)
+        silu_sorted(h_rows[2], bank2[:, low], 0)
+        silu_sorted(h_rows[2], bank4[:, low], H // 2)
+        silu_sorted(h_rows[3], bank3[:, low], 0)
+        silu_sorted(h_rows[3], bank7[:, low], H // 2)
+        for t in range(2):
+            gate_results(1, bank4[:, (2 + t) * C:(3 + t) * C], gated[:, t:t + 1, C:2 * C])
+        gate_results(1, bank3[:, 2 * C:3 * C], gated[:, 2:3, C:2 * C])
+        scatter(V, 0, C, gated[:, 0, C:2 * C])
+        scatter(V, 1, C, gated[:, 1, C:2 * C])
+        turned = bank(5, "h2_turned")
         turn_hidden(turned[:, low], h_rows[2:3])
         expert_quantise(2, turned[:, low])
-        second_dealt(1, bank(2, "y1_acc"))
-        scatter(3, 0, 1, True)
-        scatter(0, 1, 2, False)
-        scatter(1, 1, 2, False)
-        planes[3] = deal(nc.gpsimd.tensor_copy, "w2_plane3", w2_plane[:, 3 * N:], U8)
-        words[3] = deal(nc.gpsimd.tensor_copy, "w2_dealt3", w2_late[:, FP4_ROW:], U16)
-        shared_first(0, bank(0, "hs0"))
-        bank1, bank3 = bank(1, "hs1_low"), bank(3, "hs1_high")
-        shared_product(1, bank1[:, low], 0)
-        shared_product(1, bank3[:, low], H // 2)
-        silu_sorted(hs_rows[1], bank1[:, low], 0)
-        turn_hidden(bank3[:, high], h_rows[3:4])
-        expert_quantise(3, bank3[:, high])
-        w2s_dealt = deal(nc.gpsimd.tensor_copy, "w2s_dealt", w2s[:], I32)
-        w2s_plane_dealt = deal(nc.gpsimd.tensor_copy, "w2s_plane_dealt", w2s_plane[:], U8)
-        silu_sorted(hs_rows[1], bank3[:, low], H // 2)
-        shared_first(2, bank(4, "hs2"))
-        shared_first(3, bank(0, "hs3"))
-        second_dealt(2, bank(3, "y2_acc"))
-        shared_turn(0, bank(1, "hs_turned0"))
-        shared_turn(2, bank(4, "hs_turned2"))
-        scatter(0, 2, 3, False)
-        second_dealt(3, bank(1, "y3_acc"))
+
+        bank0, bank1 = bank(0, "hs0_low"), bank(1, "hs0_high")
+        shared_product(0, bank0[:, low], 0)
+        shared_product(0, bank1[:, low], H // 2)
+        silu_sorted(hs_rows[0], bank0[:, low], 0)
+        turn_hidden(bank1[:, high], h_rows[3:4])
+        held = tile("gated1_last", 2 * C, F32)
+        gate_results(1, bank3[:, 3 * C:], held[:, 0:C].unsqueeze(1))
+        expert_quantise(3, bank1[:, high])
+        scatter(V, 3, C, held[:, 0:SHARE])
+        w2s_dealt = deal(G.tensor_copy, tile("w2s_dealt", N, I32)[:], w2s[:], I32)
+        w2s_plane_dealt = deal(G.tensor_copy, tile("w2s_plane_dealt", N, U8)[:], w2s_plane[:], U8)
+        silu_sorted(hs_rows[0], bank1[:, low], H // 2)
+        shared_first(1, bank(2, "hs1"))
+        shared_first(2, bank(6, "hs2"))
+        shared_first(3, bank(7, "hs3"))
+        acc = bank(2, "y2_acc")
+        second_product(2, acc[:], range(PACK))
+        gate_results(2, acc[:, low], gated[:, 0:2, 2 * C:3 * C])
+        gate_results(2, acc[:, 2 * C:3 * C], gated[:, 2:3, 2 * C:3 * C])
+        gate_results(2, acc[:, 3 * C:], held[:, C:].unsqueeze(1))
+        scatter(V, 0, 2 * C, gated[:, 0, 2 * C:3 * C])
+        shared_turn(0, bank(5, "hs_turned0")[:])
+        shared_turn(2, bank(0, "hs_turned2")[:, low])
+        shared_turn(3, bank(6, "hs_turned3")[:, low])
+        acc = bank(7, "y3_acc")
+        second_product(3, acc[:], range(PACK))
         hs_codes = tile("hs_codes", T, U32)
-        hs_plane = tile("hs_plane", T, U8, "h_plane3")
+        hs_plane = tile("hs_plane", T, U8)
         nc.vector.quantize_mx(out=hs_codes[:].bitcast(FP8X4), scales=hs_plane[:], in_=hs_grouped[:])
-        scatter(2, 0, 3, True, "hs_rows3")
-        scatter(0, 3, 4, False)
-        scatter(3, 2, 4, True)
-        scatter(1, 2, 4, False)
-        scatter(2, 3, 4, True)
-        scatter(3, 1, 2, True)
+        gate_results(3, acc[:, low], gated[:, 0:2, 3 * C:])
+        gate_results(3, acc[:, high], gated[:, 2:4, 3 * C:])
+        scatter(S, 2, 0, gated[:, 2, 0:3 * C])
+        scatter(V, 0, 3 * C, gated[:, 0, 3 * C:])
+        scatter(V, 1, 2 * C, gated[:, 1, 2 * C:])
+        scatter(S, 3, 3 * C, gated[:, 3, 3 * C:])
+        scatter(S, 2, 3 * C, gated[:, 2, 3 * C:])
+        scatter(S, 3, C + SHARE, held[:, SHARE:])
 
         ys = {}
-        for t, acc_bank in enumerate((6, 7, 5, 2)):
+        for t, acc_bank in enumerate((3, 4, 1, 5)):
             ys[t] = bank(acc_bank, "ys%d" % t)
             nc.tensor.matmul_mx(out=ys[t][:], lhsT=w2s_dealt[:, t * P:(t + 1) * P].bitcast(FP8X4),
                                 lhsT_scale=w2s_plane_dealt[:, t * P:(t + 1) * P],
@@ -326,16 +342,17 @@ def tile_moe_shf_mlp_silu_kernel(
         def store(t):
             nc.sync.dma_start(out=out_rows[:, t, :], in_=total[:, t * T:(t + 1) * T])
 
-        for t in (0, 1, 2):
+        for t in range(LAST):
             add(t, 0, T)
             store(t)
         for first in (3 * quarter, 2 * quarter, 0, quarter):
             add(LAST, first, quarter)
         store(LAST)
         out_grouped = [tile("out_grouped%d" % i, PACK * half, BF16) for i in range(2)]
-        by_token = total[:].rearrange("p (t c i) -> p c t i", t=PACK, i=4)
-        grouped = [g[:].rearrange("p (c i t) -> p c t i", t=PACK, i=4) for g in out_grouped]
-        runs = quarter // 4
+        run = LINE // 4
+        by_token = total[:].rearrange("p (t c i) -> p c t i", t=PACK, i=run)
+        grouped = [g[:].rearrange("p (c i t) -> p c t i", t=PACK, i=run) for g in out_grouped]
+        runs = quarter // run
         for first in (runs, 0):
             nc.scalar.copy(out=grouped[1][:, first:first + runs], in_=by_token[:, 2 * runs + first:3 * runs + first])
         for first in (0, runs):

@@ -24,15 +24,15 @@ LIST_COLS = C // 16
 PLANE = 512
 FP4_ROW = 2 * PLANE
 LAST = PACK - 1
-SHARE = 96
+SHARE = 64
 LINE = 16
 PLACED = {
-    "w2_0": 0, "h_codes0": 512,
-    "h_grouped0": 2048, "w2_plane1": 2048,
-    "w2_1": 6144, "routed3": 4160, "h_grouped1": 7104, "late_planes": 7168,
+    "w2_0": 512, "slot_words3": 0, "h_codes0": 1024, "w2_plane1": 1024,
+    "h_rows1": 4096, "routed3": 4096,
+    "h_grouped1": 7168, "late_planes": 7168,
     "h_rows3": 8192, "gated1_last": 8192,
-    "h_grouped3": 9216, "w2s_plane_dealt": 9216,
-    "h_grouped2": 14336, "w2s_dealt": 14336,
+    "h_grouped3": 9216, "w2s_plane_dealt": 9216, "w2s_dealt1": 9728,
+    "h_grouped2": 14336, "w2s_dealt0": 14336,
     "hs_rows3": 12288, "routed2": 12288,
 }
 
@@ -105,8 +105,8 @@ def tile_moe_shf_mlp_silu_kernel(
         load_planes(w1_planes[0], w1_scales[0:2].rearrange("e s b c -> (e s) b c"))
         load_fp4(w1[1], w1_words[1])
         load_planes(w2_plane, w2_scales.rearrange("e s b c -> (e s) b c"))
-        load_fp4(w2_early[1], w2_words[1])
         load_fp4(w2_early[0], w2_words[0])
+        load_fp4(w2_early[1], w2_words[1])
         nc.sync.dma_start(out=gate_first[:], in_=gate[:, 0:2 * C])
         load_fp4(w1[2], w1_words[2])
         load_planes(w1_planes[1], w1_scales[2:4].rearrange("e s b c -> (e s) b c"))
@@ -135,10 +135,10 @@ def tile_moe_shf_mlp_silu_kernel(
             gathered = tile("slot_bytes%d_%d" % (first, s), (last - first) * C, U8)
             gather(gathered[:], x_plane[:, s * T:(s + 1) * T], slot_bytes, first, last, s)
 
-        def deal(copy, dealt, source, dtype):
+        def deal(copy, dealt, source, dtype, tiles=slice(0, PACK)):
             run = LINE // {I32: 4, U16: 2, U8: 1}[dtype]
-            copy(dealt.bitcast(dtype).rearrange("p (t c i) -> p c t i", t=PACK, i=run),
-                 source.bitcast(dtype).rearrange("p (c i t) -> p c t i", t=PACK, i=run))
+            copy(dealt.bitcast(dtype).rearrange("p (g t c i) -> p g c t i", t=tiles.stop - tiles.start, c=P // run, i=run),
+                 source.bitcast(dtype).rearrange("p (g c i t) -> p g c t i", t=PACK, c=P // run, i=run)[:, :, :, tiles])
             return dealt
 
         def silu_sorted(rows, acc, first):
@@ -226,79 +226,84 @@ def tile_moe_shf_mlp_silu_kernel(
         for first, last in ((0, 1), (1, 2), (2, E)):
             for s in range(PASSES):
                 gather_bytes(first, last, s)
-        accs = [bank(g, "h0_acc%d" % g) for g in range(4)]
-        for s in range(PASSES):
-            for g in range(4):
-                expert_first(0, accs[g][:, 0:P], g * P, [s])
         for g in range(4):
-            silu_sorted(h_rows[0], accs[g][:, 0:P], g * P)
-        late_words = tile("late_words", 3 * C, U32, "slot_words0_0")
-        gather_words(late_words[:, 0:2 * C], 2, E, 1)
-        gather_words(late_words[:, 2 * C:], 3, E, 0)
+            acc = bank(g, "h0_acc%d" % g)
+            expert_first(0, acc[:, 0:P], g * P)
+            silu_sorted(h_rows[0], acc[:, 0:P], g * P)
+        gather_words(tile("slot_words2_1", C, U32, "slot_words0_0")[:], 2, 3, 1)
         planes = {0: deal(V.tensor_copy, tile("w2_plane0", N, U8)[:], w2_plane[:, 0:N], U8)}
         words = {0: deal(V.tensor_copy, tile("w2_dealt0", FP4_ROW, U8)[:], w2_early[0][:], U16)}
 
-        for acc, first in ((bank(4, "h1_low"), 0), (bank(7, "h1_high"), H // 2)):
-            expert_first(1, acc[:, low], first)
-            silu_sorted(h_rows[1], acc[:, low], first)
+        acc = bank(4, "h1_low")
+        expert_first(1, acc[:, low], 0)
+        silu_sorted(h_rows[1], acc[:, low], 0)
         turned = bank(5, "h0_turned")
         turn_hidden(turned[:, low], h_rows[0:1])
         expert_quantise(0, turned[:, low])
-        planes[1] = deal(G.tensor_copy, tile("w2_plane1", N, U8)[:], w2_plane[:, N:2 * N], U8)
+        last_words = tile("slot_words3", PASSES * C, U32)
+        for s in range(PASSES):
+            gather_words(last_words[:, s * C:(s + 1) * C], 3, E, s)
+        acc = bank(3, "h1_high")
+        expert_first(1, acc[:, low], H // 2)
+        silu_sorted(h_rows[1], acc[:, low], H // 2)
         words[1] = deal(S.copy, tile("w2_dealt1", FP4_ROW, U8, "w1_1")[:], w2_early[1][:], U16)
-        turned = bank(6, "h1_turned")
-        turn_hidden(turned[:, low], h_rows[1:2])
         gated = tile("gated", PACK * T, F32)[:].rearrange("p (t j) -> p t j", t=PACK)
+
+        def gate_tile(e, acc, t):
+            gate_results(e, acc, gated[:, t:t + 1, e * C:(e + 1) * C])
+
         bank0, bank1 = bank(0, "y0_outer"), bank(1, "y0_inner")
         second_product(0, bank0[:, low], (0, 3))
         second_product(0, bank1[:, low], (1, 2))
-        gate_results(0, bank0[:, low], gated[:, 0:4:3, 0:C])
-        expert_quantise(1, turned[:, low], "h_plane0")
-        gate_results(0, bank1[:, low], gated[:, 1:3, 0:C])
+        turn_hidden(bank1[:, high], h_rows[1:2])
+        planes[1] = deal(G.tensor_copy, tile("w2_plane1", N, U8)[:], w2_plane[:, N:2 * N], U8)
+        gate_tile(0, bank0[:, 0:C], 0)
+        gate_tile(0, bank0[:, C:2 * C], 3)
         scatter(V, 0, 0, gated[:, 0, 0:C])
+        expert_quantise(1, bank1[:, high])
         scatter(S, 3, 0, gated[:, 3, 0:C])
+        gate_tile(0, bank1[:, 0:C], 1)
+        gate_tile(0, bank1[:, C:2 * C], 2)
         scatter(V, 1, 0, gated[:, 1, 0:C])
         late_planes, late_dealt = tile("late_planes", 2 * N, U8), tile("late_dealt", 2 * FP4_ROW, U8)
+        deal(G.tensor_copy, late_planes[:], w2_plane[:, 2 * N:], U8)
+        deal(G.tensor_copy, late_dealt[:], w2_late[:], U16)
         for e in (2, 3):
-            planes[e] = deal(G.tensor_copy, late_planes[:, (e - 2) * N:(e - 1) * N], w2_plane[:, e * N:(e + 1) * N], U8)
-        for e in (2, 3):
-            cols = slice((e - 2) * FP4_ROW, (e - 1) * FP4_ROW)
-            words[e] = deal(G.tensor_copy, late_dealt[:, cols], w2_late[:, cols], U16)
+            planes[e] = late_planes[:, (e - 2) * N:(e - 1) * N]
+            words[e] = late_dealt[:, (e - 2) * FP4_ROW:(e - 1) * FP4_ROW]
 
-        bank2, bank4 = bank(2, "h2_low"), bank(4, "h2_high")
-        bank3, bank7 = bank(3, "h3_low"), bank(7, "h3_high")
-        expert_first(2, bank2[:, low], 0)
-        expert_first(2, bank4[:, low], H // 2)
+        acc = bank(2, "h2_acc")
+        expert_first(2, acc[:], 0)
+        silu_sorted(h_rows[2], acc[:], 0)
+        bank4, bank3 = bank(4, "h3_low"), bank(3, "h3_high")
+        expert_first(3, bank4[:, low], 0)
+        expert_first(3, bank3[:, low], H // 2)
         second_product(1, bank4[:, high], (0, 1))
-        expert_first(3, bank3[:, low], 0)
         second_product(1, bank3[:, high], (2, 3))
-        expert_first(3, bank7[:, low], H // 2)
-        silu_sorted(h_rows[2], bank2[:, low], 0)
-        silu_sorted(h_rows[2], bank4[:, low], H // 2)
-        silu_sorted(h_rows[3], bank3[:, low], 0)
-        silu_sorted(h_rows[3], bank7[:, low], H // 2)
+        silu_sorted(h_rows[3], bank4[:, low], 0)
+        silu_sorted(h_rows[3], bank3[:, low], H // 2)
         for t in range(2):
-            gate_results(1, bank4[:, (2 + t) * C:(3 + t) * C], gated[:, t:t + 1, C:2 * C])
-        gate_results(1, bank3[:, 2 * C:3 * C], gated[:, 2:3, C:2 * C])
+            gate_tile(1, bank4[:, (2 + t) * C:(3 + t) * C], t)
+        gate_tile(1, bank3[:, 2 * C:3 * C], 2)
         scatter(V, 0, C, gated[:, 0, C:2 * C])
         scatter(V, 1, C, gated[:, 1, C:2 * C])
-        turned = bank(5, "h2_turned")
-        turn_hidden(turned[:, low], h_rows[2:3])
-        expert_quantise(2, turned[:, low])
 
         bank0, bank1 = bank(0, "hs0_low"), bank(1, "hs0_high")
         shared_product(0, bank0[:, low], 0)
         shared_product(0, bank1[:, low], H // 2)
+        turn_hidden(bank1[:, high], h_rows[2:3])
         silu_sorted(hs_rows[0], bank0[:, low], 0)
-        turn_hidden(bank1[:, high], h_rows[3:4])
+        silu_sorted(hs_rows[0], bank1[:, low], H // 2)
+        expert_quantise(2, bank1[:, high])
+        shared_first(1, bank(2, "hs1"))
+        turn_hidden(bank0[:, high], h_rows[3:4])
         held = tile("gated1_last", 2 * C, F32)
         gate_results(1, bank3[:, 3 * C:], held[:, 0:C].unsqueeze(1))
-        expert_quantise(3, bank1[:, high])
+        expert_quantise(3, bank0[:, high])
         scatter(V, 3, C, held[:, 0:SHARE])
-        w2s_dealt = deal(G.tensor_copy, tile("w2s_dealt", N, I32)[:], w2s[:], I32)
+        shared_turn(0, bank(5, "hs_turned0")[:, low])
+        w2s_dealt = [deal(G.tensor_copy, tile("w2s_dealt%d" % i, N // 2, I32)[:], w2s[:], I32, slice(2 * i, 2 * i + 2)) for i in range(2)]
         w2s_plane_dealt = deal(G.tensor_copy, tile("w2s_plane_dealt", N, U8)[:], w2s_plane[:], U8)
-        silu_sorted(hs_rows[0], bank1[:, low], H // 2)
-        shared_first(1, bank(2, "hs1"))
         shared_first(2, bank(6, "hs2"))
         shared_first(3, bank(7, "hs3"))
         acc = bank(2, "y2_acc")
@@ -307,8 +312,7 @@ def tile_moe_shf_mlp_silu_kernel(
         gate_results(2, acc[:, 2 * C:3 * C], gated[:, 2:3, 2 * C:3 * C])
         gate_results(2, acc[:, 3 * C:], held[:, C:].unsqueeze(1))
         scatter(V, 0, 2 * C, gated[:, 0, 2 * C:3 * C])
-        shared_turn(0, bank(5, "hs_turned0")[:])
-        shared_turn(2, bank(0, "hs_turned2")[:, low])
+        shared_turn(1, bank(0, "hs_turned1")[:])
         shared_turn(3, bank(6, "hs_turned3")[:, low])
         acc = bank(7, "y3_acc")
         second_product(3, acc[:], range(PACK))
@@ -327,7 +331,7 @@ def tile_moe_shf_mlp_silu_kernel(
         ys = {}
         for t, acc_bank in enumerate((3, 4, 1, 5)):
             ys[t] = bank(acc_bank, "ys%d" % t)
-            nc.tensor.matmul_mx(out=ys[t][:], lhsT=w2s_dealt[:, t * P:(t + 1) * P].bitcast(FP8X4),
+            nc.tensor.matmul_mx(out=ys[t][:], lhsT=w2s_dealt[t // 2][:, t % 2 * P:(t % 2 + 1) * P].bitcast(FP8X4),
                                 lhsT_scale=w2s_plane_dealt[:, t * P:(t + 1) * P],
                                 rhs=hs_codes[:].bitcast(FP8X4), rhs_scale=hs_plane[:], start=True, stop=True)
 

@@ -221,7 +221,7 @@ def tile_moe_shf_mlp_silu_kernel(
             group_hidden(hs_grouped[:, first * PACK * P:(first + parts) * PACK * P], turned)
 
         V, S, G = nc.vector, nc.scalar, nc.gpsimd
-        for e, s in ((0, 0), (1, 0), (2, 0), (0, 1), (1, 1)):
+        for e, s in ((0, 0), (1, 0), (0, 1), (1, 1)):
             gather_words(tile("slot_words%d_%d" % (e, s), C, U32)[:], e, e + 1, s)
         for first, last in ((0, 1), (1, 2), (2, E)):
             for s in range(PASSES):
@@ -230,7 +230,9 @@ def tile_moe_shf_mlp_silu_kernel(
             acc = bank(g, "h0_acc%d" % g)
             expert_first(0, acc[:, 0:P], g * P)
             silu_sorted(h_rows[0], acc[:, 0:P], g * P)
-        gather_words(tile("slot_words2_1", C, U32, "slot_words0_0")[:], 2, 3, 1)
+        next_words = tile("slot_words2", PASSES * C, U32, "slot_words0_0")
+        for s in range(PASSES):
+            gather_words(next_words[:, s * C:(s + 1) * C], 2, 3, s)
         planes = {0: deal(V.tensor_copy, tile("w2_plane0", N, U8)[:], w2_plane[:, 0:N], U8)}
         words = {0: deal(V.tensor_copy, tile("w2_dealt0", FP4_ROW, U8)[:], w2_early[0][:], U16)}
 

@@ -31,8 +31,9 @@ PLACED = {
     "h_rows1": 4096, "routed3": 4096,
     "h_grouped1": 7168, "late_planes": 7168,
     "h_rows3": 8192, "gated1_last": 8192,
-    "h_grouped3": 9216, "w2s_plane_dealt": 9216, "w2s_dealt1": 9728,
-    "h_grouped2": 14336, "w2s_dealt0": 14336,
+    "h_grouped3": 9216, "w2_dealt3_1": 9216, "w2s_dealt0": 9728,
+    "h_grouped2": 14336, "w2_dealt3_0": 14336,
+    "hs_grouped": 16384, "w2s_plane_dealt": 16384, "w2s_dealt1": 16896,
     "hs_rows3": 12288, "routed2": 12288,
 }
 
@@ -177,7 +178,7 @@ def tile_moe_shf_mlp_silu_kernel(
 
         def second_product(e, acc, tiles):
             for i, t in enumerate(tiles):
-                nc.tensor.matmul_mx(out=acc[:, i * C:(i + 1) * C], lhsT=words[e][:, 2 * t * P:2 * (t + 1) * P].bitcast(FP4X4),
+                nc.tensor.matmul_mx(out=acc[:, i * C:(i + 1) * C], lhsT=words[e][t // 2][:, t % 2 * 2 * P:(t % 2 + 1) * 2 * P].bitcast(FP4X4),
                                     lhsT_scale=planes[e][:, t * P:(t + 1) * P],
                                     rhs=h_codes[e][:].bitcast(FP8X4), rhs_scale=h_plane[e][:], start=True, stop=True)
 
@@ -221,6 +222,10 @@ def tile_moe_shf_mlp_silu_kernel(
             group_hidden(hs_grouped[:, first * PACK * P:(first + parts) * PACK * P], turned)
 
         V, S, G = nc.vector, nc.scalar, nc.gpsimd
+
+        def halves(dealt):
+            return [dealt[:, 0:FP4_ROW // 2], dealt[:, FP4_ROW // 2:]]
+
         for e, s in ((0, 0), (1, 0), (0, 1), (1, 1)):
             gather_words(tile("slot_words%d_%d" % (e, s), C, U32)[:], e, e + 1, s)
         for first, last in ((0, 1), (1, 2), (2, E)):
@@ -234,7 +239,7 @@ def tile_moe_shf_mlp_silu_kernel(
         for s in range(PASSES):
             gather_words(next_words[:, s * C:(s + 1) * C], 2, 3, s)
         planes = {0: deal(V.tensor_copy, tile("w2_plane0", N, U8)[:], w2_plane[:, 0:N], U8)}
-        words = {0: deal(V.tensor_copy, tile("w2_dealt0", FP4_ROW, U8)[:], w2_early[0][:], U16)}
+        words = {0: halves(deal(V.tensor_copy, tile("w2_dealt0", FP4_ROW, U8)[:], w2_early[0][:], U16))}
 
         acc = bank(4, "h1_low")
         expert_first(1, acc[:, low], 0)
@@ -248,7 +253,7 @@ def tile_moe_shf_mlp_silu_kernel(
         acc = bank(3, "h1_high")
         expert_first(1, acc[:, low], H // 2)
         silu_sorted(h_rows[1], acc[:, low], H // 2)
-        words[1] = deal(S.copy, tile("w2_dealt1", FP4_ROW, U8, "w1_1")[:], w2_early[1][:], U16)
+        words[1] = halves(deal(S.copy, tile("w2_dealt1", FP4_ROW, U8, "w1_1")[:], w2_early[1][:], U16))
         gated = tile("gated", PACK * T, F32)[:].rearrange("p (t j) -> p t j", t=PACK)
 
         def gate_tile(e, acc, t):
@@ -267,12 +272,10 @@ def tile_moe_shf_mlp_silu_kernel(
         gate_tile(0, bank1[:, 0:C], 1)
         gate_tile(0, bank1[:, C:2 * C], 2)
         scatter(V, 1, 0, gated[:, 1, 0:C])
-        late_planes, late_dealt = tile("late_planes", 2 * N, U8), tile("late_dealt", 2 * FP4_ROW, U8)
-        deal(G.tensor_copy, late_planes[:], w2_plane[:, 2 * N:], U8)
-        deal(G.tensor_copy, late_dealt[:], w2_late[:], U16)
+        late_planes = deal(G.tensor_copy, tile("late_planes", 2 * N, U8)[:], w2_plane[:, 2 * N:], U8)
         for e in (2, 3):
             planes[e] = late_planes[:, (e - 2) * N:(e - 1) * N]
-            words[e] = late_dealt[:, (e - 2) * FP4_ROW:(e - 1) * FP4_ROW]
+        words[2] = halves(deal(G.tensor_copy, tile("w2_dealt2", FP4_ROW, U8)[:], w2_late[:, 0:FP4_ROW], U16))
 
         acc = bank(2, "h2_acc")
         expert_first(2, acc[:], 0)
@@ -304,8 +307,9 @@ def tile_moe_shf_mlp_silu_kernel(
         expert_quantise(3, bank0[:, high])
         scatter(V, 3, C, held[:, 0:SHARE])
         shared_turn(0, bank(5, "hs_turned0")[:, low])
-        w2s_dealt = [deal(G.tensor_copy, tile("w2s_dealt%d" % i, N // 2, I32)[:], w2s[:], I32, slice(2 * i, 2 * i + 2)) for i in range(2)]
-        w2s_plane_dealt = deal(G.tensor_copy, tile("w2s_plane_dealt", N, U8)[:], w2s_plane[:], U8)
+        words[3] = [deal(G.tensor_copy, tile("w2_dealt3_%d" % i, FP4_ROW // 2, U8)[:], w2_late[:, FP4_ROW:], U16, slice(2 * i, 2 * i + 2))
+                    for i in range(2)]
+        w2s_dealt = [deal(G.tensor_copy, tile("w2s_dealt0", N // 2, I32)[:], w2s[:], I32, slice(0, 2))]
         shared_first(2, bank(6, "hs2"))
         shared_first(3, bank(7, "hs3"))
         acc = bank(2, "y2_acc")
@@ -321,6 +325,8 @@ def tile_moe_shf_mlp_silu_kernel(
         hs_codes = tile("hs_codes", T, U32)
         hs_plane = tile("hs_plane", T, U8)
         nc.vector.quantize_mx(out=hs_codes[:].bitcast(FP8X4), scales=hs_plane[:], in_=hs_grouped[:])
+        w2s_plane_dealt = deal(G.tensor_copy, tile("w2s_plane_dealt", N, U8)[:], w2s_plane[:], U8)
+        w2s_dealt.append(deal(G.tensor_copy, tile("w2s_dealt1", N // 2, I32)[:], w2s[:], I32, slice(2, 4)))
         gate_results(3, acc[:, low], gated[:, 0:2, 3 * C:])
         gate_results(3, acc[:, high], gated[:, 2:4, 3 * C:])
         scatter(S, 2, 0, gated[:, 2, 0:3 * C])

@@ -379,5 +379,4 @@ def tile_moe_shf_mlp_silu_kernel(
         for first in (0, half):
             nc.sync.dma_start(out=words_out[:, first:first + half], in_=out_codes[:, first:first + half].bitcast(I32))
         for r in range(4):
-            queue = nc.sync if r % 2 else nc.scalar
-            queue.dma_start(out=out_2[0, r:16:4, :].bitcast(I32), in_=out_plane[r:P:32, :].bitcast(I32))
+            nc.scalar.dma_start(out=out_2[0, r:16:4, :].bitcast(I32), in_=out_plane[r:P:32, :].bitcast(I32))

from contextlib import ExitStack

import concourse.mybir as mybir
from concourse.masks import make_identity

K, T, E, C, H, N = 1024, 512, 4, 128, 512, 512
FLOPS = 2 * T * (K * H + H * N) * 2

F32 = mybir.dt.float32
BF16 = mybir.dt.bfloat16
I32 = mybir.dt.int32
U32 = mybir.dt.uint32
U16 = mybir.dt.uint16
U8 = mybir.dt.uint8
FP8X4 = mybir.dt.float8_e4m3fn_x4
FP4X4 = mybir.dt.float4_e2m1fn_x4
ACT = mybir.ActivationFunctionType
ALU = mybir.AluOpType

P = 128
PACK = 4
PASSES = K // (P * PACK)
LIST_COLS = C // 16
PLANE = 512
FP4_ROW = 2 * PLANE
LAST = PACK - 1
SHARE = 64
LINE = 16
PLACED = {
    "w2_0": 512, "slot_words3": 0, "h_codes0": 1024, "w2_plane1": 1024,
    "h_rows1": 4096, "routed3": 4096,
    "h_grouped1": 7168, "late_planes": 7168,
    "h_rows3": 8192, "gated1_last": 8192,
    "h_grouped3": 9216, "w2_dealt3_1": 9216, "w2s_dealt0": 9728,
    "h_grouped2": 14336, "w2_dealt3_0": 14336,
    "hs_grouped": 16384, "w2s_plane_dealt": 16384, "w2s_dealt1": 16896,
    "hs_rows3": 12288, "routed2": 12288,
}


def tile_moe_shf_mlp_silu_kernel(
    tc, x_words, x_scales, w1_words, w1_scales, w2_words, w2_scales,
    w1s_words, w1s_scales, w2s_words, w2s_scales, gate, offs, out_0, out_1, out_2,
):
    nc = tc.nc
    with ExitStack() as ctx:
        sb = ctx.enter_context(tc.tile_pool(name="sb", bufs=1))
        placed = ctx.enter_context(tc.tile_pool(name="placed", bufs=1))
        ps = ctx.enter_context(tc.psum_pool(name="ps", bufs=1))

        def tile(name, cols, dtype, tag=None):
            if name in PLACED:
                return placed.tile([P, cols], dtype, name=name, tag=name, align_bytes=64, offset=PLACED[name])
            return sb.tile([P, cols], dtype, name=name, tag=tag or name, align_bytes=64)

        def bank(index, name):
            return ps.tile([P, PLANE], F32, name=name, tag="bank%d" % index)

        def zero_planes(name, planes):
            zeroed = tile(name, planes * PLANE, U8)
            nc.vector.memset(zeroed[:].bitcast(I32), 0)
            return zeroed

        def load_planes(dst, rows, loads=range(4)):
            for r in loads:
                nc.sync.dma_start(
                    out=dst[r:P:32, :].bitcast(I32).rearrange("q (g w) -> q g w", g=rows.shape[0]),
                    in_=rows[:, r:16:4, :].rearrange("g q c -> q g c").bitcast(I32),
                )

        def load_fp8(dst, words):
            nc.sync.dma_start(out=dst[:], in_=words.rearrange("p c d -> p (c d)").bitcast(I32))

        def load_fp4(dst, words):
            nc.sync.dma_start(
                out=dst[:].bitcast(I32).rearrange("p (g w) -> p g w", g=words.shape[0]),
                in_=words.rearrange("g p b -> p g b").bitcast(I32),
            )

        x_plane = zero_planes("x_plane", PASSES)
        w1_planes = [zero_planes("w1_plane%d" % i, 2 * PASSES) for i in range(2)]
        w2_plane = zero_planes("w2_plane", E)
        w1s_plane = zero_planes("w1s_plane", 1)
        w2s_plane = zero_planes("w2s_plane", 1)

        ident = tile("ident", P, F32)
        nc.vector.memset(ident[:], 0.0)
        make_identity(nc, ident[:], nomemset=True)

        offsets = sb.tile([P, T // 16], U16, name="offsets")
        x_tok = [tile("x_tok%d" % s, T, I32) for s in range(PASSES)]
        w1 = [tile("w1_%d" % e, PASSES * FP4_ROW, U8) for e in range(E)]
        w2_early = [tile("w2_%d" % e, FP4_ROW, U8) for e in range(2)]
        w2_late = tile("w2_late", 2 * FP4_ROW, U8)
        w1s = tile("w1s", PASSES * H, I32)
        w2s = tile("w2s", N, I32)
        gate_first, gate_rest = tile("gate_first", 2 * C, F32), tile("gate_rest", 2 * C, F32)
        gates = [(gate_first, gate_rest)[e // 2][:, e % 2 * C:(e % 2 + 1) * C] for e in range(E)]

        nc.sync.dma_start(offsets[:], offs)
        load_fp8(x_tok[0], x_words[0])
        load_planes(x_plane, x_scales, (0, 1))
        load_fp8(x_tok[1], x_words[1])
        load_planes(x_plane, x_scales, (2, 3))
        load_fp4(w1[0], w1_words[0])
        load_planes(w1_planes[0], w1_scales[0:2].rearrange("e s b c -> (e s) b c"))
        load_fp4(w1[1], w1_words[1])
        load_planes(w2_plane, w2_scales.rearrange("e s b c -> (e s) b c"))
        load_fp4(w2_early[0], w2_words[0])
        load_fp4(w2_early[1], w2_words[1])
        nc.sync.dma_start(out=gate_first[:], in_=gate[:, 0:2 * C])
        load_fp4(w1[2], w1_words[2])
        load_planes(w1_planes[1], w1_scales[2:4].rearrange("e s b c -> (e s) b c"))
        load_fp4(w1[3], w1_words[3])
        nc.sync.dma_start(out=w1s[:].rearrange("p (s c) -> p s c", s=PASSES),
                          in_=w1s_words.rearrange("s p c d -> p s (c d)").bitcast(I32))
        for q in range(4):
            nc.sync.dma_start(out=w1s_plane[32 * q:32 * q + 4 * PASSES, :].bitcast(I32),
                              in_=w1s_scales[:, 4 * q:4 * q + 4, :].bitcast(I32))
        load_fp4(w2_late, w2_words[2:4, 0])
        nc.sync.dma_start(out=gate_rest[:], in_=gate[:, 2 * C:])
        load_fp8(w2s, w2s_words[0])
        load_planes(w2s_plane, w2s_scales)

        slot_words, slot_bytes = {}, {}

        def gather(gathered, window, into, first, last, s):
            nc.vector.tensor_copy(gathered, window.indirect(offsets[:, first * LIST_COLS:last * LIST_COLS]))
            for e in range(first, last):
                into[e, s] = gathered[:, (e - first) * C:(e - first + 1) * C]

        def gather_words(gathered, first, last, s):
            gather(gathered, x_tok[s][:].bitcast(U32), slot_words, first, last, s)

        def gather_bytes(first, last, s):
            gathered = tile("slot_bytes%d_%d" % (first, s), (last - first) * C, U8)
            gather(gathered[:], x_plane[:, s * T:(s + 1) * T], slot_bytes, first, last, s)

        def deal(copy, dealt, source, dtype, tiles=slice(0, PACK)):
            run = LINE // {I32: 4, U16: 2, U8: 1}[dtype]
            copy(dealt.bitcast(dtype).rearrange("p (g t c i) -> p g c t i", t=tiles.stop - tiles.start, c=P // run, i=run),
                 source.bitcast(dtype).rearrange("p (g c i t) -> p g c t i", t=PACK, c=P // run, i=run)[:, :, :, tiles])
            return dealt

        def silu_sorted(rows, acc, first):
            width = acc.shape[1]
            nc.scalar.activation(
                out=rows[:].rearrange("c (u p b) -> c u p b", u=2, b=2)[:, :, first // PACK:(first + width) // PACK, :],
                in_=acc.rearrange("c (p u b) -> c u p b", u=2, b=2),
                func=ACT.Silu,
            )

        def expert_first(e, acc, first, passes=range(PASSES)):
            cols = slice(first, first + acc.shape[1])
            for s in passes:
                plane = w1_planes[e // 2][:, (e % 2 * PASSES + s) * H:(e % 2 * PASSES + s + 1) * H]
                nc.tensor.matmul_mx(out=acc, lhsT=slot_words[e, s].bitcast(FP8X4), lhsT_scale=slot_bytes[e, s],
                                    rhs=w1[e][:].bitcast(U16)[:, s * H:(s + 1) * H][:, cols].bitcast(FP4X4),
                                    rhs_scale=plane[:, cols], start=(s == 0), stop=(s == PASSES - 1))

        def turn_hidden(turned, parts):
            for i, rows in enumerate(parts):
                for u in range(2):
                    nc.tensor.transpose(turned[:, (2 * i + u) * P:(2 * i + u + 1) * P],
                                        rows[:].bitcast(F32)[:, u * P:(u + 1) * P], ident[:])

        h_codes, h_plane = {}, {}

        def group_hidden(grouped, turned):
            nc.scalar.copy(out=grouped.bitcast(F32).rearrange("p (i c u) -> p i c u", c=P, u=2),
                           in_=turned.rearrange("p (i u c) -> p i c u", c=P, u=2))

        def expert_quantise(e, turned, plane_tag=None):
            grouped = tile("h_grouped%d" % e, PACK * C, BF16)
            group_hidden(grouped[:], turned)
            h_codes[e], h_plane[e] = tile("h_codes%d" % e, C, U32), tile("h_plane%d" % e, C, U8, plane_tag)
            nc.vector.quantize_mx(out=h_codes[e][:].bitcast(FP8X4), scales=h_plane[e][:], in_=grouped[:])

        def second_product(e, acc, tiles):
            for i, t in enumerate(tiles):
                nc.tensor.matmul_mx(out=acc[:, i * C:(i + 1) * C], lhsT=words[e][t // 2][:, t % 2 * 2 * P:(t % 2 + 1) * 2 * P].bitcast(FP4X4),
                                    lhsT_scale=planes[e][:, t * P:(t + 1) * P],
                                    rhs=h_codes[e][:].bitcast(FP8X4), rhs_scale=h_plane[e][:], start=True, stop=True)

        def gate_results(e, acc, into):
            count = acc.shape[1] // C
            nc.vector.tensor_tensor(into, acc.rearrange("p (t c) -> p t c", t=count),
                                    gates[e].unsqueeze(1).to_broadcast([P, count, C]), ALU.mult)

        routed = {}

        def scatter(engine, t, first, values):
            if t not in routed:
                routed[t] = tile("routed%d" % t, T, F32)
            window = routed[t][:].indirect(offsets[:, first // 16:(first + values.shape[1]) // 16])
            if engine is nc.scalar:
                nc.scalar.activation(window, values, ACT.Copy)
            else:
                nc.vector.tensor_copy(window, values)

        low, high = slice(0, PLANE // 2), slice(PLANE // 2, PLANE)
        h_rows = [tile("h_rows%d" % e, H, BF16) for e in range(E)]
        hs_rows = [tile("hs_rows%d" % part, H, BF16) for part in range(T // P)]
        hs_grouped = tile("hs_grouped", PACK * T, BF16)

        def shared_product(part, acc, first):
            cols = slice(part * P, (part + 1) * P)
            for s in range(PASSES):
                at = slice(s * H + first, s * H + first + acc.shape[1])
                nc.tensor.matmul_mx(out=acc, lhsT=x_tok[s][:, cols].bitcast(FP8X4),
                                    lhsT_scale=x_plane[:, s * T:(s + 1) * T][:, cols],
                                    rhs=w1s[:, at].bitcast(FP8X4), rhs_scale=w1s_plane[4 * s:P, first:first + acc.shape[1]],
                                    start=(s == 0), stop=(s == PASSES - 1))

        def shared_first(part, acc):
            shared_product(part, acc[:], 0)
            silu_sorted(hs_rows[part], acc[:], 0)

        def shared_turn(first, turned):
            parts = turned.shape[1] // (2 * P)
            turn_hidden(turned, hs_rows[first:first + parts])
            group_hidden(hs_grouped[:, first * PACK * P:(first + parts) * PACK * P], turned)

        V, S, G = nc.vector, nc.scalar, nc.gpsimd

        def halves(dealt):
            return [dealt[:, 0:FP4_ROW // 2], dealt[:, FP4_ROW // 2:]]

        for e, s in ((0, 0), (1, 0), (0, 1), (1, 1)):
            gather_words(tile("slot_words%d_%d" % (e, s), C, U32)[:], e, e + 1, s)
        for first, last in ((0, 1), (1, 2), (2, E)):
            for s in range(PASSES):
                gather_bytes(first, last, s)
        for g in range(4):
            acc = bank(g, "h0_acc%d" % g)
            expert_first(0, acc[:, 0:P], g * P)
            silu_sorted(h_rows[0], acc[:, 0:P], g * P)
        next_words = tile("slot_words2", PASSES * C, U32, "slot_words0_0")
        for s in range(PASSES):
            gather_words(next_words[:, s * C:(s + 1) * C], 2, 3, s)
        planes = {0: deal(V.tensor_copy, tile("w2_plane0", N, U8)[:], w2_plane[:, 0:N], U8)}
        words = {0: halves(deal(V.tensor_copy, tile("w2_dealt0", FP4_ROW, U8)[:], w2_early[0][:], U16))}

        acc = bank(4, "h1_low")
        expert_first(1, acc[:, low], 0)
        silu_sorted(h_rows[1], acc[:, low], 0)
        turned = bank(5, "h0_turned")
        turn_hidden(turned[:, low], h_rows[0:1])
        expert_quantise(0, turned[:, low])
        last_words = tile("slot_words3", PASSES * C, U32)
        for s in range(PASSES):
            gather_words(last_words[:, s * C:(s + 1) * C], 3, E, s)
        acc = bank(3, "h1_high")
        expert_first(1, acc[:, low], H // 2)
        silu_sorted(h_rows[1], acc[:, low], H // 2)
        words[1] = halves(deal(S.copy, tile("w2_dealt1", FP4_ROW, U8, "w1_1")[:], w2_early[1][:], U16))
        gated = tile("gated", PACK * T, F32)[:].rearrange("p (t j) -> p t j", t=PACK)

        def gate_tile(e, acc, t):
            gate_results(e, acc, gated[:, t:t + 1, e * C:(e + 1) * C])

        bank0, bank1 = bank(0, "y0_outer"), bank(1, "y0_inner")
        second_product(0, bank0[:, low], (0, 3))
        second_product(0, bank1[:, low], (1, 2))
        turn_hidden(bank1[:, high], h_rows[1:2])
        planes[1] = deal(G.tensor_copy, tile("w2_plane1", N, U8)[:], w2_plane[:, N:2 * N], U8)
        gate_tile(0, bank0[:, 0:C], 0)
        gate_tile(0, bank0[:, C:2 * C], 3)
        scatter(V, 0, 0, gated[:, 0, 0:C])
        expert_quantise(1, bank1[:, high])
        scatter(S, 3, 0, gated[:, 3, 0:C])
        gate_tile(0, bank1[:, 0:C], 1)
        gate_tile(0, bank1[:, C:2 * C], 2)
        scatter(V, 1, 0, gated[:, 1, 0:C])
        late_planes = deal(G.tensor_copy, tile("late_planes", 2 * N, U8)[:], w2_plane[:, 2 * N:], U8)
        for e in (2, 3):
            planes[e] = late_planes[:, (e - 2) * N:(e - 1) * N]
        words[2] = halves(deal(G.tensor_copy, tile("w2_dealt2", FP4_ROW, U8)[:], w2_late[:, 0:FP4_ROW], U16))

        acc = bank(2, "h2_acc")
        expert_first(2, acc[:], 0)
        silu_sorted(h_rows[2], acc[:], 0)
        bank4, bank3 = bank(4, "h3_low"), bank(3, "h3_high")
        expert_first(3, bank4[:, low], 0)
        expert_first(3, bank3[:, low], H // 2)
        second_product(1, bank4[:, high], (0, 1))
        second_product(1, bank3[:, high], (2, 3))
        silu_sorted(h_rows[3], bank4[:, low], 0)
        silu_sorted(h_rows[3], bank3[:, low], H // 2)
        for t in range(2):
            gate_tile(1, bank4[:, (2 + t) * C:(3 + t) * C], t)
        gate_tile(1, bank3[:, 2 * C:3 * C], 2)
        scatter(V, 0, C, gated[:, 0, C:2 * C])
        scatter(V, 1, C, gated[:, 1, C:2 * C])

        bank0, bank1 = bank(0, "hs0_low"), bank(1, "hs0_high")
        shared_product(0, bank0[:, low], 0)
        shared_product(0, bank1[:, low], H // 2)
        turn_hidden(bank1[:, high], h_rows[2:3])
        silu_sorted(hs_rows[0], bank0[:, low], 0)
        silu_sorted(hs_rows[0], bank1[:, low], H // 2)
        expert_quantise(2, bank1[:, high])
        shared_first(1, bank(2, "hs1"))
        turn_hidden(bank0[:, high], h_rows[3:4])
        held = tile("gated1_last", 2 * C, F32)
        gate_results(1, bank3[:, 3 * C:], held[:, 0:C].unsqueeze(1))
        expert_quantise(3, bank0[:, high])
        scatter(V, 3, C, held[:, 0:SHARE])
        shared_turn(0, bank(5, "hs_turned0")[:, low])
        words[3] = [deal(G.tensor_copy, tile("w2_dealt3_%d" % i, FP4_ROW // 2, U8)[:], w2_late[:, FP4_ROW:], U16, slice(2 * i, 2 * i + 2))
                    for i in range(2)]
        w2s_dealt = [deal(G.tensor_copy, tile("w2s_dealt0", N // 2, I32)[:], w2s[:], I32, slice(0, 2))]
        shared_first(2, bank(6, "hs2"))
        shared_first(3, bank(7, "hs3"))
        acc = bank(2, "y2_acc")
        second_product(2, acc[:], range(PACK))
        gate_results(2, acc[:, low], gated[:, 0:2, 2 * C:3 * C])
        gate_results(2, acc[:, 2 * C:3 * C], gated[:, 2:3, 2 * C:3 * C])
        gate_results(2, acc[:, 3 * C:], held[:, C:].unsqueeze(1))
        scatter(V, 0, 2 * C, gated[:, 0, 2 * C:3 * C])
        shared_turn(1, bank(0, "hs_turned1")[:])
        shared_turn(3, bank(6, "hs_turned3")[:, low])
        acc = bank(7, "y3_acc")
        second_product(3, acc[:], range(PACK))
        hs_codes = tile("hs_codes", T, U32)
        hs_plane = tile("hs_plane", T, U8)
        nc.vector.quantize_mx(out=hs_codes[:].bitcast(FP8X4), scales=hs_plane[:], in_=hs_grouped[:])
        w2s_plane_dealt = deal(G.tensor_copy, tile("w2s_plane_dealt", N, U8)[:], w2s_plane[:], U8)
        w2s_dealt.append(deal(G.tensor_copy, tile("w2s_dealt1", N // 2, I32)[:], w2s[:], I32, slice(2, 4)))
        gate_results(3, acc[:, low], gated[:, 0:2, 3 * C:])
        gate_results(3, acc[:, high], gated[:, 2:4, 3 * C:])
        scatter(S, 2, 0, gated[:, 2, 0:3 * C])
        scatter(V, 0, 3 * C, gated[:, 0, 3 * C:])
        scatter(V, 1, 2 * C, gated[:, 1, 2 * C:])
        scatter(S, 3, 3 * C, gated[:, 3, 3 * C:])
        scatter(S, 2, 3 * C, gated[:, 2, 3 * C:])
        scatter(S, 3, C + SHARE, held[:, SHARE:])

        ys = {}
        for t, acc_bank in enumerate((3, 4, 1, 5)):
            ys[t] = bank(acc_bank, "ys%d" % t)
            nc.tensor.matmul_mx(out=ys[t][:], lhsT=w2s_dealt[t // 2][:, t % 2 * P:(t % 2 + 1) * P].bitcast(FP8X4),
                                lhsT_scale=w2s_plane_dealt[:, t * P:(t + 1) * P],
                                rhs=hs_codes[:].bitcast(FP8X4), rhs_scale=hs_plane[:], start=True, stop=True)

        total = tile("total", PACK * T, F32)
        out_rows = out_0.rearrange("(p t) c -> p t c", t=PACK)
        half, quarter = T // 2, T // 4

        def add(t, first, width):
            nc.vector.tensor_tensor(total[:, t * T + first:t * T + first + width], ys[t][:, first:first + width],
                                    routed[t][:, first:first + width], ALU.add)

        def store(t):
            nc.sync.dma_start(out=out_rows[:, t, :], in_=total[:, t * T:(t + 1) * T])

        for t in range(LAST):
            add(t, 0, T)
            store(t)
        for first in (3 * quarter, 2 * quarter, 0, quarter):
            add(LAST, first, quarter)
        store(LAST)
        out_grouped = [tile("out_grouped%d" % i, PACK * half, BF16) for i in range(2)]
        run = LINE // 4
        by_token = total[:].rearrange("p (t c i) -> p c t i", t=PACK, i=run)
        grouped = [g[:].rearrange("p (c i t) -> p c t i", t=PACK, i=run) for g in out_grouped]
        runs = quarter // run
        for first in (runs, 0):
            nc.scalar.copy(out=grouped[1][:, first:first + runs], in_=by_token[:, 2 * runs + first:3 * runs + first])
        for first in (0, runs):
            nc.vector.tensor_copy(grouped[0][:, first:first + runs], by_token[:, first:first + runs])
        out_codes = tile("out_codes", T, U32)
        out_plane = tile("out_plane", T, U8)
        words_out = out_1[0].rearrange("p c d -> p (c d)").bitcast(I32)
        for first in (0, 3 * quarter, quarter, 2 * quarter):
            cols = slice(first, first + quarter)
            nc.vector.quantize_mx(out=out_codes[:, cols].bitcast(FP8X4), scales=out_plane[:, cols],
                                  in_=out_grouped[first // half][:, first % half * PACK:(first % half + quarter) * PACK])
        for first in (0, half):
            nc.sync.dma_start(out=words_out[:, first:first + half], in_=out_codes[:, first:first + half].bitcast(I32))
        for r in range(4):
            nc.scalar.dma_start(out=out_2[0, r:16:4, :].bitcast(I32), in_=out_plane[r:P:32, :].bitcast(I32))
